import numpy as np, ml_dtypes
CORES = [35,38,43,46]
N = 4
import mx_ref
BF = ml_dtypes.bfloat16
def cols(t, e):
    v = np.concatenate([t.reshape(128, -1, 4), np.zeros((128, 1, 4), BF)], axis=1)
    return np.ascontiguousarray(v[:, e]).reshape(128, -1)
def cut(t, i, w=512):
    return t[:, w * i:w * i + w]
def tile(rs):
    return np.stack(rs, axis=2).reshape(128, -1).astype(BF)
def pick(q, e):
    c = np.concatenate([q[0].reshape(128, -1, 4), np.zeros((128, 1, 4), np.uint8)], axis=1); s = np.concatenate([q[1], np.ones((16, 1), np.uint8)], axis=1)
    return (np.ascontiguousarray(c[:, e].reshape(128, -1)), np.ascontiguousarray(s[:, e]))
def join(*qs):
    return (np.concatenate([q[0] for q in qs], axis=1), np.concatenate([q[1] for q in qs], axis=1))
def put(q, e, v):
    c, s = q[0].reshape(128, -1, 4).copy(), q[1].copy(); c[:, e] = v[0].reshape(128, -1, 4); s[:, e] = v[1]
    return (c.reshape(128, -1), s)
def pk(c, s):
    return (np.ascontiguousarray(c), mx_ref.live(s))
def emit(q):
    return q[0], q[1]
def decode(q):
    o = []
    for b in range(4):
        e = np.zeros((128, 128, 4), np.float32); e[np.arange(128), np.arange(128), b] = 1
        o.append(mx_ref.matmul(mx_ref.quantize(e.reshape(128, 512).astype(BF)), q))
    return np.stack(o, axis=2).reshape(128, -1)
def f(rng, *shape):
    return mx_ref.flush((rng.standard_normal(shape, dtype=np.float32) * np.exp2(rng.integers(-2, 3, shape[:-1] + (1,)))).astype(BF))
def wide(rng, *shape, cols=0):
    v = rng.standard_normal(shape, dtype=np.float32) * np.exp2(rng.integers(-12, 13, shape)).astype(np.float32)
    if cols: v *= np.repeat(np.exp2(rng.integers(-cols, cols + 1, shape[:-2] + (1, shape[-1] // 4))) * (rng.random(shape[:-2] + (1, shape[-1] // 4)) > 0.0625), 4, axis=-1).astype(np.float32)
    return mx_ref.flush(v.astype(BF))
T, CAPP, CAPR = 192, 112, 48
def big(v, k):
    v = v.astype(np.float32) * np.float32(k)
    v[np.abs(v) < np.float32(2.0 ** -6)] = 0
    return v.astype(BF)
def same(t):
    return np.repeat(t[None], N, axis=0)
def only(t, k):
    t = np.array(t)
    t[:, 4 * k:] = 0
    return t
def plain(rng):
    return {"x": f(rng, N, 128, 4 * T), "gr": big(f(rng, N, 128, 4 * T), 8), "rt": same(only(f(rng, 128, 512), N)), "w": f(rng, N, 128, 2048), "ub": big(f(rng, N, 128, 2048), 4), "pr": same(only(f(rng, 128, 512), 1)), "v": f(rng, N, 128, 512)}
def deal(rng, n, among):
    m, j, p = len(among), np.arange(n), rng.permutation(among)
    return np.stack([p[j % m], p[(j + 1 + j // m % (m - 1)) % m]], axis=1)
def routed(rng, to, far=False):
    g = np.arange(128) // (128 // N)
    rt = np.zeros((128, 128, 4), np.float32)
    rt[np.arange(128), g, 0] = 1 + rng.random(128)
    x = rng.standard_normal((N, 128, T, 4)) * (2 if far else 8)
    low = 0.125 * rng.choice([-1.0, 1.0], (N, 128, T))
    first, second = to[:, None, :, 0] == g[None, :, None], to[:, None, :, 1] == g[None, :, None]
    size = np.where(first, low, np.where(second, -4.0, -16.0)) if far else np.where(first, 16.0, np.where(second, 2.0, low))
    x[..., 0] = size * (1 + rng.random((N, 128, T)))
    if far: x, rt = x * 2.0 ** 25, rt * np.float32(2.0 ** 29)
    return {"x": mx_ref.flush(x.reshape(N, 128, 4 * T).astype(np.float32).astype(BF)), "rt": same(rt.reshape(128, 512).astype(BF))}
def setup_inputs(rng):
    return plain(rng)
def setup_inputs_crowd(rng):
    h = int(rng.integers(0, N))
    rest, n, to = np.delete(np.arange(N), h), [CAPP, T, CAPP + 1, CAPR, 0, CAPR + 1, CAPR - 1, 1], np.zeros((N, T, 2), int)
    for i in range(N):
        t = deal(rng, T, rest)
        t[np.arange(n[i]), rng.integers(0, 2, n[i])] = h
        to[(h + 1 + i) % N] = t[rng.permutation(T)]
    d = {**plain(rng), **routed(rng, to)}
    sign, pr = rng.choice([-1.0, 1.0], (128, 1, 4)), np.zeros((128, 128, 4), np.float32)
    pr[:, :1] = 2.0 ** 29 * sign * (1 + rng.random((128, 1, 4)))
    gr = 2.0 ** 28 * sign[None] * (1 + rng.random((N, 128, T, 4))) * rng.choice([-1.0, 1.0], (N, 1, T, 1))
    d["pr"] = same(pr.reshape(128, 512).astype(BF))
    d["gr"] = gr.reshape(N, 128, 4 * T).astype(np.float32).astype(BF)
    d["ub"] = (d["ub"].astype(np.float32) * np.float32(2.0 ** -22)).astype(BF)
    return d
def setup_inputs_dead(rng):
    rest = np.delete(np.arange(N), int(rng.integers(0, N)))
    to, dead = np.zeros((N, T, 2), int), np.zeros((N, T), bool)
    for q in range(N):
        s = rng.permutation(T)
        to[q] = deal(rng, T, rest)[s]
        dead[q] = s // (N - 1) % 4 != 0
    d = {**plain(rng), **routed(rng, to)}
    x = d["x"].astype(np.float32).reshape(N, 128, T, 4)
    x[..., 1:] = 16 * (1 + rng.random((N, 128, T, 3))) * np.where(dead, 1.0, -1.0)[:, None, :, None]
    d["x"] = x.reshape(N, 128, 4 * T).astype(BF)
    w = np.array(d["w"])
    w[rng.permutation(rest)[:N // 2]] = (-1 - rng.random((N // 2, 128, 2048))).astype(np.float32).astype(BF)
    d["w"] = w
    return d
def setup_inputs_one(rng):
    h = int(rng.integers(0, N))
    to = np.full((N, T, 2), h)
    for q in range(N): to[q, :, 1] = rng.permutation(deal(rng, T, np.delete(np.arange(N), h))[:, 0])
    return {**plain(rng), **routed(rng, to, far=True)}
def setup_inputs_spread(rng):
    d = plain(rng)
    x = (wide(rng, N, 128, 4 * T, cols=6).astype(np.float32) * np.float32(2.0 ** 8)).reshape(N, 128, T, 4)
    for q in range(N):
        i = rng.permutation(T)[:T // 8]
        x[q][:, i] = 2.0 ** -29 * (1 + rng.random((128, i.size, 4))) * rng.choice([-1.0, 1.0], (128, i.size, 4))
    d["x"] = x.reshape(N, 128, 4 * T).astype(BF)
    d["rt"] = (d["rt"].astype(np.float32) * np.float32(2.0 ** 20)).astype(BF)
    d["gr"] = big(wide(rng, N, 128, 4 * T, cols=3), 16)
    return d
def setup_inputs_ties(rng):
    u, o = sorted(rng.permutation(N)[:2].tolist())
    rest = np.delete(np.arange(N), [u, o])
    to, at = np.zeros((N, T, 2), int), []
    for q in range(N):
        t, s = deal(rng, T, rest), rng.permutation(T)
        t[:T // 2] = np.array([u, rest[0]])
        t[T // 2:T // 2 + 4, 1] = u
        to[q] = t[s]
        at.append(np.flatnonzero(s < T // 2))
    d = {**plain(rng), **routed(rng, to)}
    r = np.array(d["rt"]).reshape(N, 128, 128, 4)
    r[:, :, o] = r[:, :, u]
    x, g = d["x"].astype(np.float32).reshape(N, 128, T, 4), d["gr"].astype(np.float32).reshape(N, 128, T, 4)
    for q in range(N):
        i = at[q]
        x[q][:, i] = x[q][:, i[:1]].copy()
        g[q][:, i] = g[q][:, i[:1]].copy() * rng.choice([-1.0, 1.0], i.size)[None, :, None]
    return {**d, "x": x.reshape(N, 128, 4 * T).astype(BF), "gr": g.reshape(N, 128, 4 * T).astype(BF), "rt": r.reshape(N, 128, 512)}
def check_inputs(d):
    b = []
    for k in ("x", "gr", "rt", "w", "ub", "pr", "v"):
        a = np.abs(d[k].astype(np.float32))
        if not (np.isfinite(a).all() and ((a == 0) | (a >= 2.0 ** -30) & (a <= 2.0 ** 30)).all()): b.append("a value of " + k)
    for k, n in (("rt", N), ("pr", 1)):
        a = d[k].astype(np.float32)
        if (a != a[:1]).any(): b.append(k + " differs between ranks")
        if (a[:, :, 4 * n:] != 0).any(): b.append(k + " has numbers behind its first columns")
    return b
def reference(x, gr, rt, w, ub, pr, v):
    qz = lambda t: mx_ref.quantize(np.ascontiguousarray(t))
    to = []
    for q in range(N):
        s = mx_ref.matmul(qz(rt[q]), qz(x[q]))[:N] + np.float32(0)
        to.append(np.argsort(-s, axis=0, kind="stable")[:2])
    everyx, everyg = np.concatenate([x[q] for q in range(N)], axis=1), np.concatenate([gr[q] for q in range(N)], axis=1)
    came = np.zeros((N, 128, 2 * T, 4), np.float32)
    ct = np.zeros((N, 1, T), np.float32)
    for e in range(N):
        taken = [np.flatnonzero((to[q] == e).any(axis=0))[:CAPP] for q in range(N)]
        at = np.full((N, CAPP), -1)
        for q in range(N): at[q, :taken[q].size] = T * q + taken[q]
        at = at.reshape(-1)
        xs, gs = qz(cols(everyx, at)), qz(cols(everyg, at))
        forward = np.stack([mx_ref.matmul(qz(cut(w[e], i)), xs) for i in range(4)], axis=2).reshape(128, -1)
        m = qz(np.where(forward > 0, decode(gs), np.float32(0)).astype(BF))
        strength = np.abs(mx_ref.matmul(qz(pr[e]), m)[0])
        dx = decode(qz(tile([mx_ref.matmul(qz(cut(ub[e], i)), m) * np.float32(0.0625) for i in range(4)]))).reshape(128, -1, 4)
        for q in range(N):
            k = np.argsort(-strength[CAPP * q:CAPP * q + taken[q].size], kind="stable")[:CAPR]
            j = taken[q][k]
            second = (to[q][1, j] == e).astype(int)
            came[q][:, T * second + j] = dx[:, CAPP * q + k]
            ct[q, 0, j] += 1 + second
    oc, osc, y = np.zeros((N, 128, 4 * T), np.uint8), np.zeros((N, 16, T), np.uint8), np.zeros((N, 128, T), np.float32)
    for q in range(N):
        z = qz((came[q][:, :T] + came[q][:, T:]).reshape(128, 4 * T).astype(BF))
        oc[q], osc[q] = emit(z)
        y[q] = mx_ref.matmul(qz(v[q]), z)
    return {"oc": oc, "osc": osc, "ct": ct, "y": y}

@@ -1,0 +1,565 @@
+from concourse.bass import DstId, RemoteDMATransfer
+from concourse.mybir import dt, AluOpType as A, AxisListType, ActivationFunctionType as F
+
+NT, CP, CR = 192, 112, 48
+NS = 7
+TINY = 2.0 ** -100
+EPS = 2.0 ** -120
+BELOW = 1.0 - 2.0 ** -24
+WHOLE = 1.5 * 2.0 ** 23
+HOP, CY, PE, OUT, BACK = 0.11, 0.001, 0.0012, {1: 2.2, 2: 2.7, 3: 4.5}, 3.6
+AHEAD = {"first": 0.2, "early": 21.0, "route": 0.8, "prep": -8.9, "out": 0.1, "look": -4.3, "ct": -2.1, "": -11.3,
+         "k0": -4.2, "k0b": 4.3, "k0c": 0.1, "k1": 2.7, "k1b": -3.1, "k1c": 0.0, "k2": -3.0, "k2b": 0.3, "k2c": 0.5,
+         "k3": -0.4, "k3b": 1.4, "k3c": 3.1, "h0": -13.7, "h1": -2.0, "h2": -1.8, "h3": -2.5}
+HOLD, GAP = 0.5, 1.0
+TAB = {0: 0, 2: 1, 3: 2, 1: 3}
+POS = {0: 0, 3: 1, 1: 2, 2: 3}
+
+SCRATCH = {
+    "xt": ("sbuf", [128, 776], "bfloat16"), "gt": ("sbuf", [128, 776], "bfloat16"),
+    "rtt": ("sbuf", [128, 512], "bfloat16"), "prt": ("sbuf", [128, 16], "bfloat16"), "nt": ("sbuf", [128, 512], "bfloat16"),
+    "wt": ("sbuf", [128, 2048], "bfloat16"), "ut": ("sbuf", [128, 2048], "bfloat16"), "ppt": ("sbuf", [128, 512], "bfloat16"),
+    "vt": ("sbuf", [128, 512], "bfloat16"), "et": ("sbuf", [128, 2048], "bfloat16"), "wnt": ("sbuf", [128, 512], "bfloat16"),
+    "pt": ("sbuf", [128, 1024], "bfloat16"), "zt": ("sbuf", [128, 768], "bfloat16"),
+    "fi": ("sbuf", [128, 224], "float32"), "own": ("sbuf", [128, 224], "float32"),
+    "pf": ("sbuf", [128, 24], "float32"), "ii": ("sbuf", [128, 48], "float32"),
+    "rl": ("sbuf", [128, 16], "uint16"), "tie": ("sbuf", [128, 8], "float32"), "sb": ("sbuf", [128, 16], "float32"),
+    "tri0": ("sbuf", [128, 112], "float32"), "tri": ("sbuf", [128, 112], "float32"),
+    "idn": ("sbuf", [128, 128], "bfloat16"), "idr": ("sbuf", [128, 128], "bfloat16"), "gid": ("sbuf", [128, 192], "bfloat16"),
+    "vals": ("sbuf", [128, 50], "bfloat16"), "k4": ("sbuf", [128, 512], "bfloat16"),
+    "s0": ("sbuf", [128, 192], "float32"), "dd": ("sbuf", [128, 576], "float32"), "sg": ("sbuf", [128, 576], "bfloat16"),
+    "seg": ("sbuf", [128, 576], "bfloat16"), "ss": ("sbuf", [128, 576], "bfloat16"),
+    "win": ("sbuf", [128, 192], "bfloat16"), "m": ("sbuf", [128, 192], "bfloat16"), "pref": ("sbuf", [128, 192], "bfloat16"),
+    "le": ("sbuf", [128, 192 * (32 - NS)], "bfloat16"),
+    "cn": ("sbuf", [128, 32], "float32"), "cnt": ("sbuf", [128, 32], "float32"), "off": ("sbuf", [128, 32], "uint16"),
+    "tv": ("sbuf", [128, 384], "bfloat16"), "hh": ("sbuf", [128, 240], "float32"),
+    "offt": ("sbuf", [128, 48], "uint16"), "wgt": ("sbuf", [128, 48], "float32"),
+    "tab": ("sbuf", [128, 512], "bfloat16"), "gg": ("sbuf", [128, 1536], "bfloat16"), "hof": ("sbuf", [128, 48], "uint16"),
+    "ff": ("sbuf", [128, 144], "float32"), "cs": ("sbuf", [128, 32], "float32"), "cst": ("sbuf", [128, 32], "float32"),
+    "ysb": ("sbuf", [128, 192], "float32"), "ll": ("sbuf", [128, 32], "uint16"), "lo": ("sbuf", [128, 32], "uint16"),
+    "mt": ("sbuf", [128, 2048], "bfloat16"), "dxt": ("sbuf", [128, 2048], "bfloat16"), "ot": ("sbuf", [128, 2048], "bfloat16"),
+    "sm": ("sbuf", [128, 1792], "bfloat16"), "mk": ("sbuf", [128, 1792], "bfloat16"), "ra": ("sbuf", [128, 1344], "float32"),
+    "ca": ("sbuf", [128, 16], "float32"), "rk": ("sbuf", [128, 16], "float32"),
+    "pz": ("psum", [128, 2048], "float32"), "px": ("psum", [128, 2048], "float32"),
+}
+_CODES = [("xq", 194), ("gq", 194), ("rq", 128), ("rp", 160), ("pp", 128), ("wq", 512), ("uq", 512), ("wn", 128),
+          ("vq", 128), ("eq", 512), ("cq", 256), ("zq", 192), ("qm", 512), ("qd", 512), ("qo", 512), ("nq", 224)]
+for _k in range(4):
+    _CODES += [("lc%d" % _k, 224), ("zc%d" % _k, 192)]
+    if _k:
+        _CODES += [("sc%d" % _k, 224), ("ld%d" % _k, 128)]
+for _n, _w in _CODES:
+    SCRATCH[_n] = ("sbuf", [128, _w], "float8_e4m3fn_x4")
+    SCRATCH[_n + "s"] = ("sbuf", [128, _w], "uint8")
+
+SEMAPHORES = ["cV", "cS", "cP", "cG", "dx", "dgr", "drt", "dpr", "dw", "dub", "dv", "doy", "dos", "left", "az"]
+for _k in (1, 2, 3):
+    SEMAPHORES += ["ax%d" % _k, "al%d" % _k, "ar%d" % _k]
+
+
+def rank_program(g, core, T, topo):
+    rank = T.rank_of(core)
+    if rank is None:
+        return
+    queue = {"V": g.vector, "S": g.scalar, "P": g.tensor, "G": g, "Y": g.sync}
+    tasks, wrote, read, total = [], {}, {}, {}
+    turn_of = [""]
+
+    def task(q, call, reads, writes, cost, sem=None, inc=1, late=0.0, after=()):
+        before = {i: True for i in after}
+        for k in reads:
+            if k in wrote:
+                before[wrote[k]] = True
+            if k[0] == "*":
+                for i in read.get(k, []):
+                    if tasks[i]["q"] != q:
+                        before[i] = True
+        for k in writes:
+            if k in wrote:
+                i = wrote[k]
+                before[i] = before.get(i, False) or not (q == "P" and tasks[i]["q"] == "P")
+            for i in read.get(k, []):
+                before[i] = before.get(i, False) or tasks[i]["q"] != q
+        n = len(tasks)
+        tasks.append({"q": q, "call": call, "before": before, "cost": cost, "late": late, "sem": sem, "inc": inc,
+                      "ahead": AHEAD.get(turn_of[0], 0.0)})
+        for k in reads:
+            read.setdefault(k, []).append(n)
+        for k in writes:
+            wrote[k], read[k] = n, []
+        return n
+
+    def run(q, call, reads, writes, cost):
+        return task(q, call, reads, writes, cost, "c" + q)
+
+    def dma(q, sem, out, in_, reads, writes, late):
+        return task(q, lambda e: e.dma_start(out, in_), reads, writes, 0.06, sem, 16, late)
+
+    def n_of(a):
+        n = 1
+        for w in a.shape[1:]:
+            n *= w
+        return n
+
+    def el(n):
+        return max(64, n) * CY
+
+    def ts(out, in0, s1, s2, o0, o1, reads, writes, fast=False):
+        c = el(n_of(in0) // (2 if fast else 1))
+        if o1 is None:
+            run("V", lambda e: e.tensor_scalar(out, in0, s1, None, o0), reads, writes, c)
+        else:
+            run("V", lambda e: e.tensor_scalar(out, in0, s1, s2, o0, o1), reads, writes, c)
+
+    def tt(out, a, b, op, reads, writes, psum=False):
+        run("V", lambda e: e.tensor_tensor(out, a, b, op), reads, writes, el(n_of(out) * (1 if psum else 2)))
+
+    def scan(out, a, b, op, reads, writes, start=0.0):
+        run("V", lambda e: e.tensor_tensor_scan(out, a, b, start, op, A.add), reads, writes, el(n_of(out) // 2))
+
+    def cp(out, a, reads, writes, cost=None):
+        run("V", lambda e: e.tensor_copy(out, a), reads, writes, cost or el(n_of(out)))
+
+    def turn(out, a, reads, writes, wide=False):
+        run("V", lambda e: e.transpose(out, a), reads, writes, el(n_of(out) // (1 if wide else 2)))
+
+    def fill(ap, v, writes):
+        run("V", lambda e: e.memset(ap, v), [], writes, el(n_of(ap) // 2))
+
+    def act(out, a, f, reads, writes, cost=None, **kw):
+        run("S", lambda e: e.activation(out, a, f, **kw), reads, writes, cost or el(n_of(out)))
+
+    def clear(ap, key):
+        act(ap, T.nt[:, 0:n_of(ap)], F.Copy, ["nt"], [key])
+
+    def quant(q, a, b, tile, c, d, reads, writes):
+        o, s, i = T[q][:, a:b], T[q + "s"][:, a:b], T[tile][:, c:d]
+        run("V", lambda e: e.quantize_mx(o, s, i), reads, writes, 0.014 + 0.00026 * (d - c))
+
+    def mm(out, l, la, r, ra, n, start, stop, reads, writes):
+        w, ws, x, xs = T[l][:, la:la + 128], T[l + "s"][:, la:la + 128], T[r][:, ra:ra + n], T[r + "s"][:, ra:ra + n]
+        run("P", lambda e: e.matmul_mx(out, w, ws, x, xs, start, stop), reads, writes, (n + 16) * PE)
+
+    def pick(dst, c, n, src, a, b, offs, reads, key):
+        o, i = T[dst][:, c:c + n].bitcast(dt.uint32), T[src][:, a:b].bitcast(dt.uint32).indirect(offs)
+        cp(o, i, reads, [key], 0.05 + 1.5 * n * CY)
+        act(T[dst + "s"][:, c:c + n], T[src + "s"][:, a:b].indirect(offs), F.Copy, reads, [key + "s"], 0.065 + 1.5 * n * CY)
+
+    peer = [T.cores[rank ^ k] for k in range(4)]
+    away = [k for k in (1, 2, 3) if topo.chip(peer[k]) != topo.chip(core)]
+    out_eng = topo.engines(core, peer[away[0]])
+    near_eng = [e for e in topo.engines(core, peer[1]) if e not in out_eng] or out_eng
+    eng = {k: (out_eng if k in away else near_eng) for k in (1, 2, 3)}
+    half = {k: (out_eng[4 * away.index(k):4 * away.index(k) + 4] if k in away else near_eng) for k in (1, 2, 3)}
+
+    def bits(es):
+        return sum(1 << e for e in es)
+
+    def send(parts, sem, reads):
+        total["left"] = total.get("left", 0) + sum(len(p[3]) for p in parts)
+
+        def call(e):
+            if len(parts) == 1:
+                k, dst, src, es = parts[0]
+                rid, pid, _s = topo.addr(peer[k])
+                g.remote_dma(out_ap=dst, in_ap=src, remote_sem=T.sem[sem % k], local_sem=T.sem["left"], pid=pid,
+                             routing_id=rid, dma_engine_mask=bits(es))
+                return
+            tr = []
+            for k, dst, src, es in parts:
+                rid, pid, _s = topo.addr(peer[k])
+                tr.append(RemoteDMATransfer(dst_ids=[DstId(rid=rid, pnc=pid)], dma_engine_mask=bits(es),
+                                            remote_sem=T.sem[sem % k if "%" in sem else sem], srcs=[src], dsts=[dst]))
+            g.remote_dma_fused(tr, local_sem=T.sem["left"])
+        return task("G", call, reads, [], 0.9)
+
+    def arrive(sem, n, keys, after, late):
+        total[sem] = total.get(sem, 0) + n
+        return task(None, None, [], keys, 0.0, sem, total[sem], late, after)
+
+    def codes(name, a, b):
+        return T[name][:, a:b].bitcast(dt.uint8)
+
+    dma("S", "drt", T.rtt[:, 0:16], T.rt[:, 0:16], [], ["rtt"], 2.0)
+    dma("Y", "dx", T.xt[:, 0:768], T.x[:, :], [], ["xt"], 3.0)
+    dma("Y", "dgr", T.gt[:, 0:768], T.gr[:, :], [], ["gt"], 4.3)
+    dma("Y", "dw", T.wt[:, :], T.w[:, :], [], ["wt"], 6.7)
+    dma("Y", "dpr", T.prt[:, 0:8], T.pr[:, 0:8], [], ["prt"], 6.9)
+    dma("Y", "dub", T.ut[:, :], T.ub[:, :], [], ["ut"], 9.4)
+    dma("Y", "dv", T.vt[:, :], T.v[:, :], [], ["vt"], 10.0)
+
+    turn_of[0] = "early"
+    fill(T.nt[:, :], 0.0, ["nt"])
+    turn_of[0] = "first"
+    quant("nq", 48, 176, "nt", 0, 512, ["nt"], ["nq"])
+    a = send([(k, codes("ld%d" % k, z, z + 2), codes("nq", c, c + 2), eng[k]) for k, z, c in ((2, 64, 174), (1, 48, 48))],
+             "az", ["nq"])
+    arrive("az", len(eng[1]) + len(eng[2]), ["ldz"], [a], 6.0)
+
+    def iota(out, pattern, base, ch, key, **kw):
+        run("G", lambda e: e.iota(out, pattern, base, ch, **kw), [], key if isinstance(key, list) else [key],
+            0.15 + 2 * n_of(out) * CY)
+
+    def pf(i):
+        return T.pf[:, i:i + 1]
+
+    fl_ok = {"allow_small_or_imprecise_dtypes": True}
+    E3, TIE2, P7, P15, ODD, HIGH, ENT = (T.own[:, 32 * i:32 * i + 1] for i in range(7))
+    turn_of[0] = "early"
+    for i, (pattern, ch) in enumerate([([[0, 2], [1, 2], [0, 8]], 0), ([[2, 4], [0, 8]], 0), ([[0, 4], [1, 8]], 0)]):
+        iota(T.fi[:, 32 * i:32 * i + 32], pattern, 0, ch, "fi%d" % i, **fl_ok)
+    iota(T.ii[:, 16:26], [[0, 5], [2, 2]], 0, 0, "i10", **fl_ok)
+    turn(T.own[:, 0:96], T.fi[:, 0:96], ["fi0", "fi1", "fi2"], ["owa"], True)
+    turn_of[0] = "prep"
+    for i, (pattern, ch) in enumerate([([[0, 2], [1, 16]], 0), ([[1, 2], [0, 16]], 0), ([[16, 2], [0, 16]], 1),
+                                       ([[16, 2], [112, 16]], 1)], 3):
+        iota(T.fi[:, 32 * i:32 * i + 32], pattern, 0, ch, "fi%d" % i, **fl_ok)
+    turn(T.own[:, 96:224], T.fi[:, 96:224], ["fi%d" % i for i in range(3, 7)], ["owb"], True)
+    iota(T.ii[:, 32:35], [[-2, 3]], 5, 0, "i3", **fl_ok)
+    iota(T.ii[:, 0:16], [[7, 16]], 0, 0, "i16", **fl_ok)
+    iota(T.seg[:, :], [[0, NT], [1, 3]], 0, 0, "seg", **fl_ok)
+    iota(T.ot[:, 0:512], [[0, 512]], 1, 0, ["one", "oneb"], **fl_ok)
+    iota(T.tri0[:, :], [[16, 7], [112, 16]], 0, 0, "tri0", **fl_ok)
+    turn_of[0] = "early"
+    clear(T.rtt[:, 16:512], "rtz")
+    clear(T.xt[:, 768:776], "xz")
+    turn_of[0] = "prep"
+    clear(T.gt[:, 768:776], "gz")
+    turn_of[0] = "early"
+    ts(T.rl[:, 0:10], T.ii[:, 16:26], E3, None, A.add, None, ["i10", "owa"], ["rl"])
+    turn_of[0] = "prep"
+    ts(T.tie[:, 0:3], T.ii[:, 32:35], TIE2, TINY, A.subtract, A.mult, ["i3", "owa"], ["tie"])
+    ts(T.sb[:, :], T.ii[:, 0:16], P7, 0.5, A.add, A.add, ["i16", "owa"], ["sb"])
+    ts(pf(9), P15, 3.5, 0.5 * NT, A.mult, A.add, ["owb"], ["pf9"])
+    ts(pf(17), HIGH, float(CP), 2048.0, A.is_ge, A.mult, ["owb"], ["pf17"])
+    ts(pf(18), pf(17), ENT, None, A.add, None, ["pf17", "owb"], ["pf18"])
+    ts(T.tri[:, :], T.tri0[:, :], pf(18), BELOW - 1.0, A.is_lt, A.mult, ["tri0", "pf18"], ["tri1"])
+    ts(T.tri[:, :], T.tri[:, :], 1.0, None, A.add, None, ["tri1"], ["tri"])
+    for b in range(4):
+        clear(T.et[:, 512 * b:512 * b + 512], "ez%d" % b)
+    run("G", lambda e: e.affine_select(T.idn[:, :], T.ot[:, 0:128], [[-1, 128]], A.is_equal, 0.0, 0, 1), ["one"], ["idn"], 0.4)
+    iota(T.idr[:, :], [[1, 128]], -CP, 0, "idr", **fl_ok)
+    iota(T.k4[:, :], [[0, 8], [1, 16], [16, 4]], 0, 0, "k4", **fl_ok)
+    iota(T.vals[:, :], [[1, CR + 2]], 0, 0, "vals", **fl_ok)
+
+    turn_of[0] = "route"
+    quant("rq", 0, 128, "rtt", 0, 512, ["rtt", "rtz"], ["rq"])
+    pick("rp", 0, 160, "rq", 0, 128, T.rl[:, 0:10], ["rq", "rl"], "rp")
+    quant("xq", 0, 194, "xt", 0, 776, ["xt", "xz"], ["xq"])
+    for r in range(4):
+        mm(T.pz[:, 512 * r:512 * r + NT], "rp", 8 * r, "xq", 0, NT, True, True, ["rp", "rps", "xq"], ["*z%d" % r])
+    act(T.s0[:, :], T.pz[:, 0:NT], F.Copy, ["*z0"], ["s0"])
+    for r in (1, 2, 3):
+        a = NT * (r - 1)
+        tt(T.dd[:, a:a + NT], T.s0[:, :], T.pz[:, 512 * r:512 * r + NT], A.subtract, ["s0", "*z%d" % r], ["dd%d" % r], True)
+        act(T.sg[:, r - 1:3 * NT:3], T.dd[:, a:a + NT], F.Sign, ["dd%d" % r, "tie"], ["sg%d" % r], bias=T.tie[:, r - 1:r])
+    scan(T.ss[:, :], T.seg[:, :], T.sg[:, :], A.mult, ["seg", "sg1", "sg2", "sg3"], ["ss"])
+    ts(T.m[:, :], T.ss[:, 2:3 * NT:3], 0.0, None, A.is_gt, None, ["ss"], ["m"], True)
+    scan(T.pref[:, :], T.m[:, :], T.nt[:, 0:NT], A.add, ["m", "nt"], ["pref"])
+
+    def piece(i, t):
+        return T.le[:, NT * i + 7 * t:NT * i + NT]
+
+    for t in range(NS):
+        act(piece(t, t), T.pref[:, 7 * t:NT], F.Sign, ["pref", "sb"], ["cn%d" % t], bias=T.sb[:, t:t + 1], scale=-1.0,
+            accum_out=T.cn[:, t:t + 1])
+    for t in range(NS, 16):
+        ts(piece(t, t), T.pref[:, 7 * t:NT], T.sb[:, t:t + 1], 2.0, A.is_le, A.mult, ["pref", "sb"], ["le%d" % t], True)
+    for t in range(NS, 16):
+        scan(piece(t + 16 - NS, t), piece(t, t), T.nt[:, 0:NT - 7 * t], A.add, ["le%d" % t, "nt"], ["ls%d" % t],
+             float(7 * t - NT))
+    mine, last = ["cn%d" % t for t in range(NS)], T.le[:, NT * 17 - 1:NT * (32 - NS):NT]
+    act(T.cn[:, 16:16 + NS], T.cn[:, 0:NS], F.Copy, mine, ["cnd"])
+    for c in (0, 16):
+        cp(T.cn[:, c + NS:c + 16], last, ["ls%d" % t for t in range(NS, 16)], ["cnl%d" % c])
+    turn(T.cnt[:, :], T.cn[:, :], mine + ["cnd", "cnl0", "cnl16"], ["cnt"])
+    ts(T.off[:, :], T.cnt[:, :], 0.5, pf(9), A.mult, A.add, ["cnt", "pf9"], ["off"])
+    turn_of[0] = "prep"
+    quant("gq", 0, 194, "gt", 0, 776, ["gt", "gz"], ["gq"])
+
+    def take(k):
+        o = T.off[:, 8 * (rank ^ k):8 * (rank ^ k) + 7]
+        d = ("sc%d" if k else "lc%d") % k
+
+        def part(c, src, key):
+            cost, r = 1.5 * CP * CY, [src, "off"]
+            cp(T[d][:, c:c + CP].bitcast(dt.uint32), T[src][:, 0:194].bitcast(dt.uint32).indirect(o), r, [d + key], 0.05 + cost)
+            act(T[d + "s"][:, c:c + CP], T[src + "s"][:, 0:194].indirect(o), F.Copy, r, [d + key + "s"], 0.065 + cost)
+        part(CP, "xq", "x")
+        part(0, "gq", "g")
+
+    turn_of[0] = "out"
+    out = {}
+    for k in (1, 2, 3):
+        take(k)
+        out[k] = send([(k, codes("lc%d" % k, 0, 2 * CP), codes("sc%d" % k, 0, 2 * CP), eng[k])], "ax%d",
+                      ["sc%dx" % k, "sc%dg" % k])
+    b = send([(k, T["lc%ds" % k][:, 0:2 * CP], T["sc%ds" % k][:, 0:2 * CP], half[k]) for k in (2, 3, 1)], "ax%d",
+             [n % k for k in (2, 3, 1) for n in ("sc%dxs", "sc%dgs")])
+    for k in (1, 2, 3):
+        arrive("ax%d" % k, len(eng[k]) + len(half[k]), ["lc%d" % k], [out[k], b], OUT[k])
+    turn_of[0] = "k0"
+    take(0)
+    came = {k: ["lc%d" % k] for k in (1, 2, 3)}
+    came[0] = ["lc0x", "lc0g", "lc0xs", "lc0gs"]
+
+    turn_of[0] = "prep"
+    for b in range(4):
+        act(T.et[:, 512 * b + b:512 * b + 512:4], T.idn[:, :], F.Copy, ["idn", "ez%d" % b], ["et%d" % b])
+    quant("eq", 0, 512, "et", 0, 2048, ["et0", "et1", "et2", "et3"], ["eq"])
+    quant("wq", 0, 512, "wt", 0, 2048, ["wt"], ["wq"])
+    quant("uq", 0, 512, "ut", 0, 2048, ["ut"], ["uq"])
+    quant("vq", 0, 128, "vt", 0, 512, ["vt"], ["vq"])
+    for t in range(4):
+        act(T.ppt[:, t:512:4], T.nt[:, 0:128], F.Identity, ["nt", "prt"], ["ppt%d" % t], bias=T.prt[:, t:t + 1])
+    quant("pp", 0, 128, "ppt", 0, 512, ["ppt%d" % t for t in range(4)], ["pp"])
+    for t, v in ((0, -256.0), (1, 160.0), (2, -1.0), (3, 0.0)):
+        act(T.wnt[:, t:512:4], T.ot[:, 0:128], F.Copy, ["one"], ["wnt%d" % t], scale=v)
+    quant("wn", 0, 128, "wnt", 0, 512, ["wnt%d" % t for t in range(4)], ["wn"])
+    clear(T.pt[:, 0:512], "pt0")
+    clear(T.pt[:, 512:1024], "pt1")
+    ts(T.pt[:, 0:11:5], T.nt[:, 0:3], HIGH, None, A.add, None, ["nt", "owb", "pt0"], ["pth"])
+    ts(T.pt[:, 512:523:5], T.nt[:, 0:3], P15, None, A.add, None, ["nt", "owb", "pt1"], ["ptl"])
+    quant("cq", 0, 256, "pt", 0, 1024, ["pt0", "pt1", "pth", "ptl"], ["cq"])
+    for k in range(4):
+        clear(T.mt[:, 512 * k + 448:512 * k + 512], "mz%d" % k)
+        clear(T.dxt[:, 512 * k + 448:512 * k + 512], "dz%d" % k)
+    fill(pf(12), EPS, ["eps"])
+
+    def bank(k, x):
+        return (T.px if k % 2 else T.pz), 512 * x, "*%s%d" % ("zx"[k % 2], x)
+
+    def stage1(k):
+        lc, c = "lc%d" % k, came[k]
+        for b in range(4):
+            ps, x, key = bank(k, b % 2)
+            mm(ps[:, x:x + 128], "wq", 128 * b, lc, 96, 128, True, True, ["wq"] + c, [key])
+            o = 448 * k + CP * b
+            if b == 3:
+                ts(T.mk[:, o:o + CP], ps[:, x + 16:x + 128], 0.0, None, A.is_gt, None, [key], ["mk%d_%d" % (k, b)])
+            else:
+                act(T.sm[:, o:o + CP], ps[:, x + 16:x + 128], F.Sign, [key], ["sm%d_%d" % (k, b)])
+                act(T.mk[:, o:o + CP], T.sm[:, o:o + CP], F.Relu, ["sm%d_%d" % (k, b)], ["mk%d_%d" % (k, b)])
+            ps, x, key = bank(k, 2 + b % 2)
+            mm(ps[:, x:x + 128], "eq", 128 * b, lc, 0, 128, True, True, ["eq"] + c, [key])
+            tt(T.mt[:, 512 * k + b:512 * k + 448:4], T.mk[:, o:o + CP], ps[:, x:x + CP], A.mult,
+               ["mk%d_%d" % (k, b), key], ["mt%d_%d" % (k, b)], True)
+        quant("qm", 128 * k, 128 * k + 128, "mt", 512 * k, 512 * k + 512,
+              ["mz%d" % k] + ["mt%d_%d" % (k, b) for b in range(4)], ["qm%d" % k])
+
+    def stage2(k):
+        m, rk, one_hot = "qm%d" % k, T.rk[:, 4 * k:4 * k + 1], T.ot[:, 512 * k:512 * k + 512]
+        pc, xc, kc = bank(k, 1)
+        pr, xr, kr = bank(k, 0)
+        mm(pc[:, xc:xc + 128], "qm", 128 * k, "pp", 0, 128, True, True, [m, "pp"], [kc])
+        mm(pr[:, xr:xr + 128], "pp", 0, "qm", 128 * k, 128, True, True, [m, "pp"], [kr])
+        act(T.ca[:, 4 * k:4 * k + 1], pc[:, xc:xc + 1], F.Abs, [kc, "eps"], ["ca%d" % k], bias=pf(12))
+        s, sd, sx = (slice(c + CP * k, c + CP * k + CP) for c in (0, 448, 896))
+        act(T.ra[:, s], pr[:, xr:xr + CP], F.Abs, [kr, "eps"], ["ra%d" % k], bias=pf(12))
+        act(T.ra[:, sd], T.tri[:, :], F.Copy, ["tri", "ca%d" % k], ["rd%d" % k], scale=T.ca[:, 4 * k:4 * k + 1])
+        if k:
+            tt(T.ra[:, sx], T.ra[:, s], T.ra[:, sd], A.is_gt, ["rd%d" % k, "ra%d" % k], ["rx%d" % k])
+            run("V", lambda e: e.tensor_reduce(rk, T.ra[:, sx], AxisListType.X, A.add), ["rx%d" % k], ["rk%d" % k], 0.11)
+            ts(one_hot, T.k4[:, :], rk, None, A.is_equal, None, ["k4", "rk%d" % k], ["ot%d" % k], True)
+        else:
+            tt(T.ot[:, 0:448:4], T.ra[:, s], T.ra[:, sd], A.is_gt, ["rd0", "ra0"], ["ot0", "one"])
+        quant("qo", 128 * k, 128 * k + 128, "ot", 512 * k, 512 * k + 512, ["ot%d" % k], ["qo%d" % k])
+        for b, y in ((0, 2), (1, 3), (2, 1), (3, 0)):
+            ps, x, key = bank(k, y)
+            mm(ps[:, x:x + 128], "uq", 128 * b, "qm", 128 * k, 128, True, True, ["uq", m], [key])
+            act(T.dxt[:, 512 * k + b:512 * k + 448:4], ps[:, x:x + CP], F.Copy, [key], ["dt%d_%d" % (k, b)], scale=0.0625)
+
+    def stage3(k):
+        ps, x, key = bank(k, 2)
+        quant("qd", 128 * k, 128 * k + 128, "dxt", 512 * k, 512 * k + 512,
+              ["dz%d" % k] + ["dt%d_%d" % (k, b) for b in range(4)], ["qd%d" % k])
+        if not k:
+            mm(ps[:, x:x + 128], "wn", 0, "qo", 0, 128, True, True, ["qo0", "wn"], [key])
+            tt(T.tab[:, 0:CP], T.idr[:, 0:CP], ps[:, x:x + CP], A.max, ["idr", key], ["tab0"], True)
+            return
+        if k == 3:
+            a = send([(3, codes("ld3", 0, CP + 2), codes("qd", 384, 386 + CP), eng[3])], "ar%d", ["qd3"])
+            b = send([(3, T.ld3s[:, 0:CP + 2], T.qds[:, 384:386 + CP], eng[3])], "ar%d", ["qd3"])
+            arrive("ar3", 2 * len(eng[3]), ["ld3", "ld3s"], [a, b], BACK)
+        for c in (0, 1):
+            mm(ps[:, x:x + 128], "qo", 128 * k, "cq", 128 * c, 128, c == 0, c == 1, ["qo%d" % k, "cq"], [key])
+        cp(T.lo[:, 8 * k:8 * k + 3], ps[:, x:x + 3], [key], ["lo%d" % k])
+        if k < 3:
+            d, (c, z, h) = "sd%d" % k, {1: (0, 0, 0), 2: (176, 128, 66)}[k]
+            pick("nq", c, CR, "qd", 128 * k, 128 * k + 128, T.lo[:, 8 * k:8 * k + 3], ["qd%d" % k, "lo%d" % k], d)
+        if k != 2:
+            to = (1,) if k == 1 else (2, 3)
+            a = send([(j, T.ll[:, 8 * j:8 * j + 3], T.lo[:, 8 * j:8 * j + 3], half[j]) for j in to], "al%d",
+                     ["lo%d" % j for j in to])
+            for j in to:
+                arrive("al%d" % j, len(half[j]), ["ll%d" % j], [a], BACK - 0.5)
+        if k < 3:
+            b = send([(k, codes("ld%d" % k, h, h + 24), codes("nq", c, c + 24), eng[k][0:2]),
+                      (k, codes("ld%d" % k, h + 24, h + 48), codes("nq", c + 24, c + 48), eng[k][2:4]),
+                      (k, T["ld%ds" % k][:, h + z - c:h + z - c + 96], T.nqs[:, z:z + 96], eng[k][4:8])], "ar%d",
+                     [d, d + "s", "nq"])
+            arrive("ar%d" % k, len(eng[k]), ["ld%d" % k, "ld%ds" % k], [b], BACK)
+
+    turn_of[0] = "look"
+    fill(T.tab[:, 0:384], 0.0, ["tab0", "tab2", "tab3"])
+    fill(T.tab[:, 384:512], float(CR), ["tab1"])
+    for k in range(4):
+        turn_of[0] = "k%d" % k
+        stage1(k)
+        turn_of[0] = "k%db" % k
+        stage2(k)
+        turn_of[0] = "k%dc" % k
+        stage3(k)
+
+    turn_of[0] = "look"
+    h1, h2, h3, h4, h5, h6, h7, h8, h9, h10 = (T.hh[:, 24 * i:24 * i + 24] for i in range(10))
+    cp(T.win[:, :], T.ss[:, 2:3 * NT:3], ["ss"], ["win"], el(NT // 2))
+    turn(T.tv[:, 0:NT], T.win[:, :], ["win"], ["tw"])
+    turn(T.tv[:, NT:2 * NT], T.pref[:, :], ["pref"], ["tp"])
+    tw, tp = T.tv[:, 0:NT:8], T.tv[:, NT:2 * NT:8]
+    ts(h1, tw, 0.0, None, A.is_gt, None, ["tw"], ["h1"])
+    ts(h2, tp, float(CP), None, A.is_le, None, ["tp"], ["h2"])
+    ts(h6, tw, 4.0, 1.0, A.is_lt, A.add, ["tw"], ["h6"])
+    tt(h4, h1, h2, A.mult, ["h1", "h2"], ["h4"])
+    ts(h7, tp, 1.0 / 7, -4.0 / 7, A.mult, A.add, ["tp"], ["h7"])
+    ts(h8, h7, WHOLE, WHOLE, A.add, A.subtract, ["h7"], ["h8"])
+    ts(h9, h8, -111.0, -16.0 - CP, A.mult, A.add, ["h8"], ["h9"])
+    act(h10, tp, F.Copy, ["tp"], ["h10"], scale=16.0)
+    tt(h3, h9, h10, A.add, ["h9", "h10"], ["h3"])
+    tt(h5, h4, h3, A.mult, ["h4", "h3"], ["h5"])
+    ts(pf(10), ODD, -1.0, 1.0, A.mult, A.add, ["owb"], ["pf10"])
+    for k in (0, 1, 2, 3):
+        e = rank ^ k
+        for h in (0, 1):
+            o, p = slice(12 * POS[k] + h, 12 * POS[k] + 12, 2), (pf(10), ODD)[h]
+            ts(T.offt[:, o], T.hh[:, 96 + e:120:4], float(CP), None, A.add, None, ["h5"], ["offt%d%d" % (k, h)])
+            act(T.wgt[:, o], T.hh[:, 120 + e:144:4], F.Copy, ["h6", "owb", "pf10"], ["wgt%d%d" % (k, h)], scale=p)
+    fill(T.cs[:, :], 0.0, ["csz"])
+
+    def home(k, first, last):
+        tab, zc, q = T.tab[:, 128 * TAB[k]:128 * TAB[k] + 128], "zc%d" % k, 12 * POS[k]
+        offt, of, ko = T.offt[:, q:q + 12], T.hof[:, q:q + 12], ["offt%d0" % k, "offt%d1" % k]
+        s, s1 = slice(192 * k, 192 * k + 192), slice(768 + 192 * k, 960 + 192 * k)
+        lst, g1 = T.ll[:, 8 * k:8 * k + 3], T.gg[:, 768 + 192 * k:960 + 192 * k:16]
+        if k in (1, 2):
+            cp(tab.indirect(lst), T.vals[:, 2 * k - 2:2 * k - 2 + CR], ["vals", "ll%d" % k], ["tab%d" % k], 0.23)
+        elif k:
+            cp(tab.indirect(lst), T.ot[:, 448:448 + CR], ["oneb", "ll3"], ["tab3"], 0.23)
+            act(T.gid[:, :], T.idr[:, :].indirect(offt), F.Copy, ["idr"] + ko, ["gid"], 0.35)
+        if k == 3:
+            run("V", lambda e: e.tensor_tensor(T.gg[:, s], tab.indirect(offt), T.gid[:, :], A.mult),
+                ["tab3", "gid"] + ko, ["gr03"], 0.35)
+        else:
+            act(T.gg[:, s], tab.indirect(offt), F.Copy, ["tab%d" % k] + ko, ["gr0%d" % k], 0.35)
+        turn(T.gg[:, s1], T.gg[:, s], ["gr0%d" % k], ["gr1%d" % k])
+        if k in (1, 2):
+            cp(of, g1, ["gr1%d" % k], ["hof%d" % k])
+            pick(zc, 0, NT, "ld%d" % k, 64 * k - 64, 64 * k - 14, of, ["hof%d" % k, "ld%d" % k, "ld%ds" % k, "ldz"], zc)
+        else:
+            ts(of, g1, 0.0, float(CP), A.min, A.add, ["gr1%d" % k], ["hof%d" % k])
+            if k:
+                pick(zc, 0, NT, "ld3", 0, CP + 2, of, ["hof3", "ld3", "ld3s"], zc)
+            else:
+                pick(zc, 0, NT, "qd", 0, 128, of, ["hof0", "qd0"], zc)
+        for b in range(4):
+            mm(T.pz[:, 512 * b:512 * b + NT], "eq", 128 * b, zc, 0, NT, first, last, ["eq", zc, zc + "s"], ["*z%d" % b])
+
+    for k in range(4):
+        turn_of[0] = "h%d" % k
+        home(k, k == 0, k == 3)
+    turn_of[0] = "ct"
+    ts(T.ff[:, 0:24], T.hof[:, 0:24], CP - 0.5, None, A.is_lt, None, ["hof0", "hof3"], ["fl0"])
+    ts(T.ff[:, 24:36], T.hof[:, 24:36], CR - 0.5, None, A.is_lt, None, ["hof1"], ["fl1"])
+    ts(T.ff[:, 36:48], T.hof[:, 36:48], 1.0, None, A.is_gt, None, ["hof2"], ["fl2"])
+    tt(T.ff[:, 48:96], T.ff[:, 0:48], T.wgt[:, :], A.mult,
+       ["fl0", "fl1", "fl2"] + ["wgt%d%d" % (k, h) for k in range(4) for h in (0, 1)], ["fw"])
+    tt(T.ff[:, 96:120], T.ff[:, 48:72], T.ff[:, 72:96], A.add, ["fw"], ["fs"])
+    tt(T.ff[:, 120:132], T.ff[:, 96:108], T.ff[:, 108:120], A.add, ["fs"], ["ft"])
+    tt(T.cs[:, 0:6], T.ff[:, 120:132:2], T.ff[:, 121:132:2], A.add, ["ft", "csz"], ["cs"])
+    turn(T.cst[0:32, :], T.cs[0:32, :], ["cs", "csz"], ["cst"], True)
+
+    turn_of[0] = ""
+    for b in range(4):
+        move = (T.zt[:, b:768:4], T.pz[:, 512 * b:512 * b + NT])
+        if b % 2:
+            cp(move[0], move[1], ["*z%d" % b], ["zt%d" % b])
+        else:
+            act(move[0], move[1], F.Copy, ["*z%d" % b], ["zt%d" % b])
+    quant("zq", 0, 192, "zt", 0, 768, ["zt0", "zt1", "zt2", "zt3"], ["zq"])
+    mm(T.px[:, 0:NT], "vq", 0, "zq", 0, NT, True, True, ["vq", "zq"], ["*x0"])
+    cp(T.ysb[:, :], T.px[:, 0:NT], ["*x0"], ["ysb"])
+    dma("Y", "doy", T.ct[0:1, 0:NT], T.cst[0:6, 0:32], ["cst"], [], 2.0)
+    dma("Y", "doy", T.oc[:, 0:768], T.zq[:, 0:NT].bitcast(dt.uint8), ["zq"], [], 2.0)
+    for i in range(4):
+        q, s = ("S", "dos") if i < 3 else ("Y", "doy")
+        dma(q, s, T.osc[4 * i:4 * i + 4, 0:NT], T.zqs[32 * i:32 * i + 4, 0:NT], ["zq"], [], 2.0)
+    dma("Y", "doy", T.y[:, :], T.ysb[:, :], ["ysb"], [], 2.0)
+
+    n = len(tasks)
+    follow = [[] for _i in range(n)]
+    for i, t in enumerate(tasks):
+        for j in t["before"]:
+            follow[j].append(i)
+    rest = [0.0] * n
+    for i in range(n - 1, -1, -1):
+        far = max([rest[j] + (HOP if tasks[j]["before"][i] else 0.0) for j in follow[i]] or [0.0])
+        rest[i] = max(far, 0.0) + tasks[i]["cost"] + tasks[i]["late"] + tasks[i]["ahead"]
+    left = [len(t["before"]) for t in tasks]
+    ready = [0.0] * n
+    free = {q: 0.0 for q in ("V", "S", "P", "G", "Y", None)}
+    able = [i for i in range(n) if not left[i]]
+    order = []
+    while able:
+        best = None
+        for q in free:
+            mine = sorted(i for i in able if tasks[i]["q"] == q)
+            if not mine:
+                continue
+            at = max(free[q], min(ready[i] for i in mine)) if q else min(ready[i] for i in mine)
+            pool = [i for i in mine if ready[i] <= at + 1e-9]
+            i = min(pool) if q == "Y" else max(pool, key=lambda j: rest[j])
+            for j in mine:
+                if q not in ("Y", None) and ready[j] < at + HOLD * tasks[i]["cost"] and rest[j] > rest[i] + GAP:
+                    i = j
+            at = max(at, ready[i])
+            if best is None or at < best[0]:
+                best = (at, i)
+        at, i = best
+        t = tasks[i]
+        able.remove(i)
+        order.append(i)
+        if t["q"]:
+            free[t["q"]] = at + t["cost"]
+        done = at + t["cost"] + t["late"]
+        for j in follow[i]:
+            ready[j] = max(ready[j], done + HOP if tasks[j]["before"][i] else at + t["cost"])
+            left[j] -= 1
+            if not left[j]:
+                able.append(j)
+
+    waited, token = {}, {}
+
+    def need(q, tok):
+        if waited.get((q, tok[0]), 0) < tok[1]:
+            queue[q].wait_ge(T.sem[tok[0]], tok[1])
+            waited[(q, tok[0])] = tok[1]
+
+    for i in order:
+        t = tasks[i]
+        if t["q"] is None:
+            token[i] = (t["sem"], t["inc"])
+            continue
+        best = {}
+        for j, full in t["before"].items():
+            if full:
+                s, v = token[j]
+                best[s] = max(best.get(s, 0), v)
+        for s, v in best.items():
+            need(t["q"], (s, v))
+        made = t["call"](queue[t["q"]])
+        if t["sem"]:
+            made.then_inc(T.sem[t["sem"]], t["inc"])
+            total[t["sem"]] = total.get(t["sem"], 0) + t["inc"]
+            token[i] = (t["sem"], total[t["sem"]])
+    for s, v in total.items():
+        need("G", (s, v))

@@ -1,49 +1,42 @@
 from concourse.bass import DstId, RemoteDMATransfer
-from concourse.mybir import dt, AluOpType as A, AxisListType, ActivationFunctionType as F
+from concourse.mybir import dt, AluOpType as A, ActivationFunctionType as F
 
 NT, CP, CR = 192, 112, 48
-NS = 7
-TINY = 2.0 ** -100
 EPS = 2.0 ** -120
 BELOW = 1.0 - 2.0 ** -24
 WHOLE = 1.5 * 2.0 ** 23
-HOP, CY, PE, OUT, BACK = 0.11, 0.001, 0.0012, {1: 2.2, 2: 2.7, 3: 4.5}, 3.6
-AHEAD = {"first": 0.2, "early": 21.0, "route": 0.8, "prep": -8.9, "out": 0.1, "look": -4.3, "ct": -2.1, "": -11.3,
-         "k0": -4.2, "k0b": 4.3, "k0c": 0.1, "k1": 2.7, "k1b": -3.1, "k1c": 0.0, "k2": -3.0, "k2b": 0.3, "k2c": 0.5,
-         "k3": -0.4, "k3b": 1.4, "k3c": 3.1, "h0": -13.7, "h1": -2.0, "h2": -1.8, "h3": -2.5}
-HOLD, GAP = 0.5, 1.0
+OPT = {"ns": 9, "out": "c13 s13 c2 s2", "back": "l13 l2 t1 c2 s2", "mv": "3333", "seq": "0312", "bank": "zxzz", "sum": "x"}
+ORDER = "27 0 28 10 26 12 32 29 6 33 149 364 148 7 13 16 31 151 14 150 11 25 40 34 24 127 15 20 23 145 35 17 18 36 133 147 1 2 3 4 5 19 49 47 45 142 139 132 135 46 44 48 138 22 21 128 130 50 51 37 52 53 115 134 347 38 54 55 56 30 116 113 57 88 58 136 69 71 73 72 74 68 70 76 81 78 79 75 77 80 337 84 83 65 61 67 64 63 62 60 59 66 129 82 85 86 89 91 99 97 123 87 122 102 98 92 344 90 104 100 101 117 103 342 118 39 143 125 96 114 336 93 152 157 153 124 126 155 158 160 162 167 154 159 163 137 164 156 161 339 165 131 168 166 169 170 171 172 173 119 120 343 349 144 94 174 179 181 175 176 340 182 180 95 8 9 41 105 106 42 108 111 109 185 183 141 184 186 177 338 341 345 178 346 187 348 356 350 362 107 43 110 240 235 238 241 353 236 195 190 112 196 191 242 237 197 192 250 188 189 251 239 205 198 199 193 200 245 207 365 201 146 202 206 194 360 366 208 367 203 243 204 244 248 252 246 247 369 363 209 210 211 212 221 223 225 249 253 368 254 213 214 222 224 226 227 228 256 255 266 285 280 288 357 257 259 258 286 281 287 215 358 216 229 282 375 219 218 217 220 232 233 295 290 260 261 234 283 231 230 291 292 267 289 262 263 264 297 284 272 293 296 265 298 270 271 273 140 294 299 275 276 268 269 300 277 274 302 301 303 304 278 305 306 307 309 308 310 352 335 325 279 372 313 317 311 315 370 355 312 316 318 320 321 314 319 322 324 323 334 330 385 374 354 327 331 326 332 328 121 376 377 351 386 387 329 333 378 379 361 380 359 405 388 395 396 397 373 384 383 381 390 389 371 382 393 391 394 392 398 406 407 399 408 409 410 400 402 403 415 414 404 411 416 412 420 401 413 417 424 421 425 423 422 418 419 426"
 TAB = {0: 0, 2: 1, 3: 2, 1: 3}
 POS = {0: 0, 3: 1, 1: 2, 2: 3}
 
 SCRATCH = {
     "xt": ("sbuf", [128, 776], "bfloat16"), "gt": ("sbuf", [128, 776], "bfloat16"),
-    "rtt": ("sbuf", [128, 512], "bfloat16"), "prt": ("sbuf", [128, 16], "bfloat16"), "nt": ("sbuf", [128, 512], "bfloat16"),
+    "rtt": ("sbuf", [128, 16], "bfloat16"), "prt": ("sbuf", [128, 16], "bfloat16"), "nt": ("sbuf", [128, 512], "bfloat16"),
     "wt": ("sbuf", [128, 2048], "bfloat16"), "ut": ("sbuf", [128, 2048], "bfloat16"), "ppt": ("sbuf", [128, 512], "bfloat16"),
-    "vt": ("sbuf", [128, 512], "bfloat16"), "et": ("sbuf", [128, 2048], "bfloat16"), "wnt": ("sbuf", [128, 512], "bfloat16"),
-    "pt": ("sbuf", [128, 1024], "bfloat16"), "zt": ("sbuf", [128, 768], "bfloat16"),
-    "fi": ("sbuf", [128, 224], "float32"), "own": ("sbuf", [128, 224], "float32"),
-    "pf": ("sbuf", [128, 24], "float32"), "ii": ("sbuf", [128, 48], "float32"),
-    "rl": ("sbuf", [128, 16], "uint16"), "tie": ("sbuf", [128, 8], "float32"), "sb": ("sbuf", [128, 16], "float32"),
+    "vt": ("sbuf", [128, 512], "bfloat16"), "et": ("sbuf", [128, 516], "bfloat16"), "wnt": ("sbuf", [128, 512], "bfloat16"),
+    "pt": ("sbuf", [128, 528], "bfloat16"), "zt": ("sbuf", [128, 768], "bfloat16"),
+    "fi": ("sbuf", [128, 256], "float32"), "own": ("sbuf", [128, 256], "float32"), "pf": ("sbuf", [128, 24], "float32"),
+    "sb": ("sbuf", [128, 16], "float32"), "rct": ("sbuf", [128, 1088], "bfloat16"), "ex": ("sbuf", [128, 384], "bfloat16"),
+    "bt": ("sbuf", [128, 768], "bfloat16"), "rx": ("sbuf", [128, 896], "bfloat16"),
     "tri0": ("sbuf", [128, 112], "float32"), "tri": ("sbuf", [128, 112], "float32"),
-    "idn": ("sbuf", [128, 128], "bfloat16"), "idr": ("sbuf", [128, 128], "bfloat16"), "gid": ("sbuf", [128, 192], "bfloat16"),
-    "vals": ("sbuf", [128, 50], "bfloat16"), "k4": ("sbuf", [128, 512], "bfloat16"),
-    "s0": ("sbuf", [128, 192], "float32"), "dd": ("sbuf", [128, 576], "float32"), "sg": ("sbuf", [128, 576], "bfloat16"),
-    "seg": ("sbuf", [128, 576], "bfloat16"), "ss": ("sbuf", [128, 576], "bfloat16"),
-    "win": ("sbuf", [128, 192], "bfloat16"), "m": ("sbuf", [128, 192], "bfloat16"), "pref": ("sbuf", [128, 192], "bfloat16"),
-    "le": ("sbuf", [128, 192 * (32 - NS)], "bfloat16"),
+    "idr": ("sbuf", [128, 128], "bfloat16"), "gid": ("sbuf", [128, 192], "bfloat16"),
+    "vals": ("sbuf", [128, 50], "bfloat16"), "k4": ("sbuf", [128, 384], "bfloat16"),
+    "win": ("sbuf", [128, 192], "bfloat16"), "m": ("sbuf", [128, 200], "bfloat16"), "pref": ("sbuf", [128, 192], "bfloat16"),
+    "le": ("sbuf", [128, 192 * 26], "bfloat16"),
     "cn": ("sbuf", [128, 32], "float32"), "cnt": ("sbuf", [128, 32], "float32"), "off": ("sbuf", [128, 32], "uint16"),
     "tv": ("sbuf", [128, 384], "bfloat16"), "hh": ("sbuf", [128, 240], "float32"),
     "offt": ("sbuf", [128, 48], "uint16"), "wgt": ("sbuf", [128, 48], "float32"),
     "tab": ("sbuf", [128, 512], "bfloat16"), "gg": ("sbuf", [128, 1536], "bfloat16"), "hof": ("sbuf", [128, 48], "uint16"),
     "ff": ("sbuf", [128, 144], "float32"), "cs": ("sbuf", [128, 32], "float32"), "cst": ("sbuf", [128, 32], "float32"),
     "ysb": ("sbuf", [128, 192], "float32"), "ll": ("sbuf", [128, 32], "uint16"), "lo": ("sbuf", [128, 32], "uint16"),
-    "mt": ("sbuf", [128, 2048], "bfloat16"), "dxt": ("sbuf", [128, 2048], "bfloat16"), "ot": ("sbuf", [128, 2048], "bfloat16"),
-    "sm": ("sbuf", [128, 1792], "bfloat16"), "mk": ("sbuf", [128, 1792], "bfloat16"), "ra": ("sbuf", [128, 1344], "float32"),
-    "ca": ("sbuf", [128, 16], "float32"), "rk": ("sbuf", [128, 16], "float32"),
+    "mt": ("sbuf", [128, 2048], "bfloat16"), "dxt": ("sbuf", [128, 2048], "bfloat16"), "ot": ("sbuf", [128, 2052], "bfloat16"),
+    "sm": ("sbuf", [128, 1792], "bfloat16"), "mk": ("sbuf", [128, 1792], "bfloat16"), "ra": ("sbuf", [128, 896], "float32"),
+    "ca": ("sbuf", [128, 16], "float32"),
     "pz": ("psum", [128, 2048], "float32"), "px": ("psum", [128, 2048], "float32"),
 }
-_CODES = [("xq", 194), ("gq", 194), ("rq", 128), ("rp", 160), ("pp", 128), ("wq", 512), ("uq", 512), ("wn", 128),
-          ("vq", 128), ("eq", 512), ("cq", 256), ("zq", 192), ("qm", 512), ("qd", 512), ("qo", 512), ("nq", 224)]
+_CODES = [("xq", 194), ("gq", 194), ("rq", 272), ("bq", 192), ("pp", 128), ("wq", 512), ("uq", 512), ("wn", 128),
+          ("vq", 128), ("eq", 512), ("cq", 132), ("zq", 192), ("qm", 512), ("qd", 512), ("qo", 512), ("nq", 224)]
 for _k in range(4):
     _CODES += [("lc%d" % _k, 224), ("zc%d" % _k, 192)]
     if _k:
@@ -63,9 +56,9 @@ def rank_program(g, core, T, topo):
         return
     queue = {"V": g.vector, "S": g.scalar, "P": g.tensor, "G": g, "Y": g.sync}
     tasks, wrote, read, total = [], {}, {}, {}
-    turn_of = [""]
+    NS = OPT["ns"]
 
-    def task(q, call, reads, writes, cost, sem=None, inc=1, late=0.0, after=()):
+    def task(q, call, reads, writes, sem=None, inc=1, after=()):
         before = {i: True for i in after}
         for k in reads:
             if k in wrote:
@@ -81,69 +74,60 @@ def rank_program(g, core, T, topo):
             for i in read.get(k, []):
                 before[i] = before.get(i, False) or tasks[i]["q"] != q
         n = len(tasks)
-        tasks.append({"q": q, "call": call, "before": before, "cost": cost, "late": late, "sem": sem, "inc": inc,
-                      "ahead": AHEAD.get(turn_of[0], 0.0)})
+        tasks.append({"q": q, "call": call, "before": before, "sem": sem, "inc": inc})
         for k in reads:
             read.setdefault(k, []).append(n)
         for k in writes:
             wrote[k], read[k] = n, []
         return n
 
-    def run(q, call, reads, writes, cost):
-        return task(q, call, reads, writes, cost, "c" + q)
+    def run(q, call, reads, writes):
+        return task(q, call, reads, writes, "c" + q)
 
-    def dma(q, sem, out, in_, reads, writes, late):
-        return task(q, lambda e: e.dma_start(out, in_), reads, writes, 0.06, sem, 16, late)
+    def dma(q, sem, out, in_, reads, writes):
+        return task(q, lambda e: e.dma_start(out, in_), reads, writes, sem, 16)
 
-    def n_of(a):
-        n = 1
-        for w in a.shape[1:]:
-            n *= w
-        return n
-
-    def el(n):
-        return max(64, n) * CY
-
-    def ts(out, in0, s1, s2, o0, o1, reads, writes, fast=False):
-        c = el(n_of(in0) // (2 if fast else 1))
+    def ts(out, in0, s1, s2, o0, o1, reads, writes):
         if o1 is None:
-            run("V", lambda e: e.tensor_scalar(out, in0, s1, None, o0), reads, writes, c)
+            run("V", lambda e: e.tensor_scalar(out, in0, s1, None, o0), reads, writes)
         else:
-            run("V", lambda e: e.tensor_scalar(out, in0, s1, s2, o0, o1), reads, writes, c)
+            run("V", lambda e: e.tensor_scalar(out, in0, s1, s2, o0, o1), reads, writes)
 
-    def tt(out, a, b, op, reads, writes, psum=False):
-        run("V", lambda e: e.tensor_tensor(out, a, b, op), reads, writes, el(n_of(out) * (1 if psum else 2)))
+    def tt(out, a, b, op, reads, writes):
+        run("V", lambda e: e.tensor_tensor(out, a, b, op), reads, writes)
 
-    def scan(out, a, b, op, reads, writes, start=0.0):
-        run("V", lambda e: e.tensor_tensor_scan(out, a, b, start, op, A.add), reads, writes, el(n_of(out) // 2))
+    def scan(out, a, b, reads, writes, start=0.0):
+        run("V", lambda e: e.tensor_tensor_scan(out, a, b, start, A.add, A.add), reads, writes)
 
-    def cp(out, a, reads, writes, cost=None):
-        run("V", lambda e: e.tensor_copy(out, a), reads, writes, cost or el(n_of(out)))
+    def cp(out, a, reads, writes):
+        run("V", lambda e: e.tensor_copy(out, a), reads, writes)
 
-    def turn(out, a, reads, writes, wide=False):
-        run("V", lambda e: e.transpose(out, a), reads, writes, el(n_of(out) // (1 if wide else 2)))
+    def turn(out, a, reads, writes):
+        run("V", lambda e: e.transpose(out, a), reads, writes)
 
     def fill(ap, v, writes):
-        run("V", lambda e: e.memset(ap, v), [], writes, el(n_of(ap) // 2))
+        run("V", lambda e: e.memset(ap, v), [], writes)
 
-    def act(out, a, f, reads, writes, cost=None, **kw):
-        run("S", lambda e: e.activation(out, a, f, **kw), reads, writes, cost or el(n_of(out)))
+    def act(out, a, f, reads, writes, **kw):
+        run("S", lambda e: e.activation(out, a, f, **kw), reads, writes)
 
     def clear(ap, key):
-        act(ap, T.nt[:, 0:n_of(ap)], F.Copy, ["nt"], [key])
+        act(ap, T.nt[:, 0:ap.shape[1]], F.Copy, ["nt"], [key])
 
     def quant(q, a, b, tile, c, d, reads, writes):
         o, s, i = T[q][:, a:b], T[q + "s"][:, a:b], T[tile][:, c:d]
-        run("V", lambda e: e.quantize_mx(o, s, i), reads, writes, 0.014 + 0.00026 * (d - c))
+        run("V", lambda e: e.quantize_mx(o, s, i), reads, writes)
 
     def mm(out, l, la, r, ra, n, start, stop, reads, writes):
         w, ws, x, xs = T[l][:, la:la + 128], T[l + "s"][:, la:la + 128], T[r][:, ra:ra + n], T[r + "s"][:, ra:ra + n]
-        run("P", lambda e: e.matmul_mx(out, w, ws, x, xs, start, stop), reads, writes, (n + 16) * PE)
+        run("P", lambda e: e.matmul_mx(out, w, ws, x, xs, start, stop), reads, writes)
 
     def pick(dst, c, n, src, a, b, offs, reads, key):
-        o, i = T[dst][:, c:c + n].bitcast(dt.uint32), T[src][:, a:b].bitcast(dt.uint32).indirect(offs)
-        cp(o, i, reads, [key], 0.05 + 1.5 * n * CY)
-        act(T[dst + "s"][:, c:c + n], T[src + "s"][:, a:b].indirect(offs), F.Copy, reads, [key + "s"], 0.065 + 1.5 * n * CY)
+        cp(T[dst][:, c:c + n].bitcast(dt.uint32), T[src][:, a:b].bitcast(dt.uint32).indirect(offs), reads, [key])
+        act(T[dst + "s"][:, c:c + n], T[src + "s"][:, a:b].indirect(offs), F.Copy, reads, [key + "s"])
+
+    def iota(out, pattern, base, ch, key):
+        run("G", lambda e: e.iota(out, pattern, base, ch, allow_small_or_imprecise_dtypes=True), [], [key])
 
     peer = [T.cores[rank ^ k] for k in range(4)]
     away = [k for k in (1, 2, 3) if topo.chip(peer[k]) != topo.chip(core)]
@@ -151,281 +135,273 @@ def rank_program(g, core, T, topo):
     near_eng = [e for e in topo.engines(core, peer[1]) if e not in out_eng] or out_eng
     eng = {k: (out_eng if k in away else near_eng) for k in (1, 2, 3)}
     half = {k: (out_eng[4 * away.index(k):4 * away.index(k) + 4] if k in away else near_eng) for k in (1, 2, 3)}
-
-    def bits(es):
-        return sum(1 << e for e in es)
+    due = {}
 
     def send(parts, sem, reads):
-        total["left"] = total.get("left", 0) + sum(len(p[3]) for p in parts)
-
         def call(e):
-            if len(parts) == 1:
-                k, dst, src, es = parts[0]
-                rid, pid, _s = topo.addr(peer[k])
-                g.remote_dma(out_ap=dst, in_ap=src, remote_sem=T.sem[sem % k], local_sem=T.sem["left"], pid=pid,
-                             routing_id=rid, dma_engine_mask=bits(es))
-                return
             tr = []
             for k, dst, src, es in parts:
                 rid, pid, _s = topo.addr(peer[k])
-                tr.append(RemoteDMATransfer(dst_ids=[DstId(rid=rid, pnc=pid)], dma_engine_mask=bits(es),
-                                            remote_sem=T.sem[sem % k if "%" in sem else sem], srcs=[src], dsts=[dst]))
-            g.remote_dma_fused(tr, local_sem=T.sem["left"])
-        return task("G", call, reads, [], 0.9)
+                tr.append((dst, src, T.sem[sem % k if "%" in sem else sem], rid, pid, sum(1 << x for x in es)))
+            if len(tr) == 1:
+                dst, src, s, rid, pid, mask = tr[0]
+                g.remote_dma(out_ap=dst, in_ap=src, remote_sem=s, local_sem=T.sem["left"], pid=pid, routing_id=rid,
+                             dma_engine_mask=mask)
+            else:
+                g.remote_dma_fused([RemoteDMATransfer(dst_ids=[DstId(rid=rid, pnc=pid)], dma_engine_mask=mask, remote_sem=s,
+                                                      srcs=[src], dsts=[dst]) for dst, src, s, rid, pid, mask in tr],
+                                   local_sem=T.sem["left"])
+        n = task("G", call, reads, [])
+        for k, _d, _s, es in parts:
+            name = sem % k if "%" in sem else sem
+            due.setdefault(name, []).append(n)
+            for s in (name, "left"):
+                total[s] = total.get(s, 0) + len(es)
 
-    def arrive(sem, n, keys, after, late):
-        total[sem] = total.get(sem, 0) + n
-        return task(None, None, [], keys, 0.0, sem, total[sem], late, after)
+    def share(to):
+        return half if len([k for k in to if k in away]) > 1 else eng
+
+    def arrive(sem, keys):
+        task(None, None, [], keys, sem, total[sem], due[sem])
 
     def codes(name, a, b):
         return T[name][:, a:b].bitcast(dt.uint8)
 
-    dma("S", "drt", T.rtt[:, 0:16], T.rt[:, 0:16], [], ["rtt"], 2.0)
-    dma("Y", "dx", T.xt[:, 0:768], T.x[:, :], [], ["xt"], 3.0)
-    dma("Y", "dgr", T.gt[:, 0:768], T.gr[:, :], [], ["gt"], 4.3)
-    dma("Y", "dw", T.wt[:, :], T.w[:, :], [], ["wt"], 6.7)
-    dma("Y", "dpr", T.prt[:, 0:8], T.pr[:, 0:8], [], ["prt"], 6.9)
-    dma("Y", "dub", T.ut[:, :], T.ub[:, :], [], ["ut"], 9.4)
-    dma("Y", "dv", T.vt[:, :], T.v[:, :], [], ["vt"], 10.0)
+    dma("S", "drt", T.rtt[:, 0:16], T.rt[:, 0:16], [], ["rtt"])
+    dma("Y", "dx", T.xt[:, 0:768], T.x[:, :], [], ["xt"])
+    dma("Y", "dgr", T.gt[:, 0:768], T.gr[:, :], [], ["gt"])
+    dma("Y", "dw", T.wt[:, :], T.w[:, :], [], ["wt"])
+    dma("Y", "dpr", T.prt[:, 0:8], T.pr[:, 0:8], [], ["prt"])
+    dma("Y", "dub", T.ut[:, :], T.ub[:, :], [], ["ut"])
 
-    turn_of[0] = "early"
     fill(T.nt[:, :], 0.0, ["nt"])
-    turn_of[0] = "first"
     quant("nq", 48, 176, "nt", 0, 512, ["nt"], ["nq"])
-    a = send([(k, codes("ld%d" % k, z, z + 2), codes("nq", c, c + 2), eng[k]) for k, z, c in ((2, 64, 174), (1, 48, 48))],
-             "az", ["nq"])
-    arrive("az", len(eng[1]) + len(eng[2]), ["ldz"], [a], 6.0)
-
-    def iota(out, pattern, base, ch, key, **kw):
-        run("G", lambda e: e.iota(out, pattern, base, ch, **kw), [], key if isinstance(key, list) else [key],
-            0.15 + 2 * n_of(out) * CY)
+    send([(k, codes("ld%d" % k, z, z + 2), codes("nq", c, c + 2), eng[k]) for k, z, c in ((2, 64, 174), (1, 48, 48))],
+         "az", ["nq"])
+    arrive("az", ["ldz"])
 
     def pf(i):
         return T.pf[:, i:i + 1]
 
-    fl_ok = {"allow_small_or_imprecise_dtypes": True}
-    E3, TIE2, P7, P15, ODD, HIGH, ENT = (T.own[:, 32 * i:32 * i + 1] for i in range(7))
-    turn_of[0] = "early"
-    for i, (pattern, ch) in enumerate([([[0, 2], [1, 2], [0, 8]], 0), ([[2, 4], [0, 8]], 0), ([[0, 4], [1, 8]], 0)]):
-        iota(T.fi[:, 32 * i:32 * i + 32], pattern, 0, ch, "fi%d" % i, **fl_ok)
-    iota(T.ii[:, 16:26], [[0, 5], [2, 2]], 0, 0, "i10", **fl_ok)
-    turn(T.own[:, 0:96], T.fi[:, 0:96], ["fi0", "fi1", "fi2"], ["owa"], True)
-    turn_of[0] = "prep"
-    for i, (pattern, ch) in enumerate([([[0, 2], [1, 16]], 0), ([[1, 2], [0, 16]], 0), ([[16, 2], [0, 16]], 1),
-                                       ([[16, 2], [112, 16]], 1)], 3):
-        iota(T.fi[:, 32 * i:32 * i + 32], pattern, 0, ch, "fi%d" % i, **fl_ok)
-    turn(T.own[:, 96:224], T.fi[:, 96:224], ["fi%d" % i for i in range(3, 7)], ["owb"], True)
-    iota(T.ii[:, 32:35], [[-2, 3]], 5, 0, "i3", **fl_ok)
-    iota(T.ii[:, 0:16], [[7, 16]], 0, 0, "i16", **fl_ok)
-    iota(T.seg[:, :], [[0, NT], [1, 3]], 0, 0, "seg", **fl_ok)
-    iota(T.ot[:, 0:512], [[0, 512]], 1, 0, ["one", "oneb"], **fl_ok)
-    iota(T.tri0[:, :], [[16, 7], [112, 16]], 0, 0, "tri0", **fl_ok)
-    turn_of[0] = "early"
-    clear(T.rtt[:, 16:512], "rtz")
+    LO, HI, M7, BASE, P15, ODD, HIGH, ENT = (T.own[:, 32 * i:32 * i + 1] for i in range(8))
+    fill(T.fi[:, 0:64], -1.0, ["fi0", "fi1"])
+    iota(T.ex[:, 0:128], [[0, 4], [1, 4], [0, 8]], 0, 0, "ex")
+    iota(T.fi[:, 1:17], [[0, 4], [1, 4]], 0, 1, "fi0")
+    iota(T.fi[:, 33:49], [[1, 4], [1, 4]], 1, 1, "fi1")
+    turn(T.own[:, 0:64], T.fi[:, 0:64], ["fi0", "fi1"], ["owa"])
+    clear(T.rct[:, 0:504], "rcy")
+    fill(T.rct[:, 504:1088], 0.0, ["rcz"])
+    ts(T.ex[:, 128:256], T.ex[:, 0:128], LO, None, A.is_equal, None, ["ex", "owa"], ["ex1"])
+    ts(T.ex[:, 256:384], T.ex[:, 0:128], HI, None, A.is_equal, None, ["ex", "owa"], ["ex2"])
+    tt(T.rct[:, 0:508:4], T.ex[:, 128:255], T.ex[:, 256:383], A.subtract, ["ex1", "ex2", "rcy", "rcz"], ["rc0"])
     clear(T.xt[:, 768:776], "xz")
-    turn_of[0] = "prep"
+    clear(T.bt[:, 0:384], "bz0")
+    clear(T.bt[:, 384:768], "bz1")
+    clear(T.m[:, 0:2], "mz")
+    for i, (pattern, base, ch) in enumerate([([[0, 4], [-2, 8]], 0, 0), ([[0, 2], [7, 8], [3, 2]], NT // 2, 0),
+                                             ([[0, 2], [1, 16]], 0, 0), ([[1, 2], [0, 16]], 0, 0),
+                                             ([[16, 2], [0, 16]], 0, 1), ([[16, 2], [112, 16]], 0, 1)], 2):
+        iota(T.fi[:, 32 * i:32 * i + 32], pattern, base, ch, "fi%d" % i)
+    turn(T.own[:, 64:128], T.fi[:, 64:128], ["fi2", "fi3"], ["owc"])
+    turn(T.own[:, 128:256], T.fi[:, 128:256], ["fi%d" % i for i in range(4, 8)], ["owb"])
+    iota(T.sb[:, :], [[14, 16]], 1, 0, "sb")
+    fill(T.ot[:, 0:516], 1.0, ["one", "oneb", "ot1_0"])
+    iota(T.tri0[:, :], [[16, 7], [112, 16]], 0, 0, "tri0")
     clear(T.gt[:, 768:776], "gz")
-    turn_of[0] = "early"
-    ts(T.rl[:, 0:10], T.ii[:, 16:26], E3, None, A.add, None, ["i10", "owa"], ["rl"])
-    turn_of[0] = "prep"
-    ts(T.tie[:, 0:3], T.ii[:, 32:35], TIE2, TINY, A.subtract, A.mult, ["i3", "owa"], ["tie"])
-    ts(T.sb[:, :], T.ii[:, 0:16], P7, 0.5, A.add, A.add, ["i16", "owa"], ["sb"])
-    ts(pf(9), P15, 3.5, 0.5 * NT, A.mult, A.add, ["owb"], ["pf9"])
     ts(pf(17), HIGH, float(CP), 2048.0, A.is_ge, A.mult, ["owb"], ["pf17"])
     ts(pf(18), pf(17), ENT, None, A.add, None, ["pf17", "owb"], ["pf18"])
     ts(T.tri[:, :], T.tri0[:, :], pf(18), BELOW - 1.0, A.is_lt, A.mult, ["tri0", "pf18"], ["tri1"])
-    ts(T.tri[:, :], T.tri[:, :], 1.0, None, A.add, None, ["tri1"], ["tri"])
-    for b in range(4):
-        clear(T.et[:, 512 * b:512 * b + 512], "ez%d" % b)
-    run("G", lambda e: e.affine_select(T.idn[:, :], T.ot[:, 0:128], [[-1, 128]], A.is_equal, 0.0, 0, 1), ["one"], ["idn"], 0.4)
-    iota(T.idr[:, :], [[1, 128]], -CP, 0, "idr", **fl_ok)
-    iota(T.k4[:, :], [[0, 8], [1, 16], [16, 4]], 0, 0, "k4", **fl_ok)
-    iota(T.vals[:, :], [[1, CR + 2]], 0, 0, "vals", **fl_ok)
+    act(T.tri[:, :], T.tri[:, :], F.Copy, ["tri1"], ["tri"], bias=1.0)
+    run("G", lambda e: e.affine_select(T.et[:, :], T.ot[:, 0:516], [[-1, 516]], A.is_equal, 0.0, 3, 4),
+        ["one", "oneb", "ot1_0"], ["et"])
+    iota(T.idr[:, :], [[1, 128]], -CP, 0, "idr")
+    iota(T.k4[:, :], [[16, 3], [0, 8], [1, 16]], 0, 0, "k4")
+    iota(T.vals[:, :], [[1, CR + 2]], 0, 0, "vals")
 
-    turn_of[0] = "route"
-    quant("rq", 0, 128, "rtt", 0, 512, ["rtt", "rtz"], ["rq"])
-    pick("rp", 0, 160, "rq", 0, 128, T.rl[:, 0:10], ["rq", "rl"], "rp")
+    for d in (1, 2, 3):
+        n, c = 16 - 4 * d, 16 * d - 12
+        act(T.rct[:, 504 + c:504 + c + n], T.rtt[:, 4 * d:16], F.Copy, ["rtt", "rcz"], ["rb%d" % d], scale=-1.0)
+        cp(T.rct[:, 576 + c:576 + c + n], T.rtt[:, 0:n], ["rtt", "rcz"], ["rc%d" % d])
+    quant("rq", 0, 272, "rct", 0, 1088, ["rc0"] + [n % d for n in ("rb%d", "rc%d") for d in (1, 2, 3)], ["rq"])
     quant("xq", 0, 194, "xt", 0, 776, ["xt", "xz"], ["xq"])
-    for r in range(4):
-        mm(T.pz[:, 512 * r:512 * r + NT], "rp", 8 * r, "xq", 0, NT, True, True, ["rp", "rps", "xq"], ["*z%d" % r])
-    act(T.s0[:, :], T.pz[:, 0:NT], F.Copy, ["*z0"], ["s0"])
-    for r in (1, 2, 3):
-        a = NT * (r - 1)
-        tt(T.dd[:, a:a + NT], T.s0[:, :], T.pz[:, 512 * r:512 * r + NT], A.subtract, ["s0", "*z%d" % r], ["dd%d" % r], True)
-        act(T.sg[:, r - 1:3 * NT:3], T.dd[:, a:a + NT], F.Sign, ["dd%d" % r, "tie"], ["sg%d" % r], bias=T.tie[:, r - 1:r])
-    scan(T.ss[:, :], T.seg[:, :], T.sg[:, :], A.mult, ["seg", "sg1", "sg2", "sg3"], ["ss"])
-    ts(T.m[:, :], T.ss[:, 2:3 * NT:3], 0.0, None, A.is_gt, None, ["ss"], ["m"], True)
-    scan(T.pref[:, :], T.m[:, :], T.nt[:, 0:NT], A.add, ["m", "nt"], ["pref"])
+    mm(T.px[:, 0:NT], "rq", 144, "xq", 0, NT, True, False, ["rq", "xq"], ["*x0"])
+    mm(T.px[:, 0:NT], "rq", 126, "xq", 0, NT, False, True, ["rq", "xq"], ["*x0"])
+    ts(T.bt[:, 0:768:4], T.px[:, 0:NT], 0.0, None, A.is_ge, None, ["*x0", "bz0", "bz1"], ["bt"])
+    quant("bq", 0, NT, "bt", 0, 768, ["bt"], ["bq"])
+    mm(T.px[:, 512:512 + NT], "rq", 0, "bq", 0, NT, True, True, ["rq", "bq"], ["*x1"])
+    ts(T.m[:, 2:2 + NT], T.px[:, 512:512 + NT], 2.5, None, A.is_gt, None, ["*x1"], ["m"])
+    scan(T.pref[:, :], T.m[:, 2:2 + NT], T.m[:, 1:1 + NT], ["m", "mz", "owc"], ["pref"], M7)
 
     def piece(i, t):
         return T.le[:, NT * i + 7 * t:NT * i + NT]
 
     for t in range(NS):
-        act(piece(t, t), T.pref[:, 7 * t:NT], F.Sign, ["pref", "sb"], ["cn%d" % t], bias=T.sb[:, t:t + 1], scale=-1.0,
-            accum_out=T.cn[:, t:t + 1])
+        a = 7 * t // 2
+        act(T.le[:, NT * t + a:NT * t + NT // 2], T.pref[:, 2 * a + 1:NT:2], F.Sign, ["pref", "sb"], ["cn%d" % t],
+            bias=T.sb[:, t:t + 1], scale=-1.0, accum_out=T.cn[:, t:t + 1])
     for t in range(NS, 16):
-        ts(piece(t, t), T.pref[:, 7 * t:NT], T.sb[:, t:t + 1], 2.0, A.is_le, A.mult, ["pref", "sb"], ["le%d" % t], True)
+        ts(piece(t, t), T.pref[:, 7 * t:NT], 14.0 * t + 1, None, A.is_lt, None, ["pref"], ["le%d" % t])
     for t in range(NS, 16):
-        scan(piece(t + 16 - NS, t), piece(t, t), T.nt[:, 0:NT - 7 * t], A.add, ["le%d" % t, "nt"], ["ls%d" % t],
-             float(7 * t - NT))
+        scan(piece(t + 16 - NS, t), piece(t, t), T.nt[:, 0:NT - 7 * t], ["le%d" % t, "nt"], ["ls%d" % t],
+             float(7 * t - NT // 2 - 7 * t // 2))
     mine, last = ["cn%d" % t for t in range(NS)], T.le[:, NT * 17 - 1:NT * (32 - NS):NT]
     act(T.cn[:, 16:16 + NS], T.cn[:, 0:NS], F.Copy, mine, ["cnd"])
     for c in (0, 16):
         cp(T.cn[:, c + NS:c + 16], last, ["ls%d" % t for t in range(NS, 16)], ["cnl%d" % c])
     turn(T.cnt[:, :], T.cn[:, :], mine + ["cnd", "cnl0", "cnl16"], ["cnt"])
-    ts(T.off[:, :], T.cnt[:, :], 0.5, pf(9), A.mult, A.add, ["cnt", "pf9"], ["off"])
-    turn_of[0] = "prep"
+    ts(T.off[:, :], T.cnt[:, :], BASE, None, A.add, None, ["cnt", "owc"], ["off"])
+    act(T.win[:, :], T.px[:, 512:512 + NT], F.Copy, ["*x1"], ["win"])
     quant("gq", 0, 194, "gt", 0, 776, ["gt", "gz"], ["gq"])
 
-    def take(k):
-        o = T.off[:, 8 * (rank ^ k):8 * (rank ^ k) + 7]
-        d = ("sc%d" if k else "lc%d") % k
-
-        def part(c, src, key):
-            cost, r = 1.5 * CP * CY, [src, "off"]
-            cp(T[d][:, c:c + CP].bitcast(dt.uint32), T[src][:, 0:194].bitcast(dt.uint32).indirect(o), r, [d + key], 0.05 + cost)
-            act(T[d + "s"][:, c:c + CP], T[src + "s"][:, 0:194].indirect(o), F.Copy, r, [d + key + "s"], 0.065 + cost)
-        part(CP, "xq", "x")
-        part(0, "gq", "g")
-
-    turn_of[0] = "out"
-    out = {}
+    for k in (1, 2, 3, 0):
+        d, o = ("sc%d" if k else "lc%d") % k, T.off[:, 8 * (rank ^ k):8 * (rank ^ k) + 7]
+        pick(d, CP, CP, "xq", 0, 194, o, ["xq", "off"], d + "x")
+        pick(d, 0, CP, "gq", 0, 194, o, ["gq", "off"], d + "g")
+    for w in OPT["out"].split():
+        to = [int(c) for c in w[1:]]
+        if w[0] == "s":
+            send([(k, T["lc%ds" % k][:, 0:2 * CP], T["sc%ds" % k][:, 0:2 * CP], share(to)[k]) for k in to], "ax%d",
+                 [n % k for k in to for n in ("sc%dxs", "sc%dgs")])
+        else:
+            send([(k, codes("lc%d" % k, 0, 2 * CP), codes("sc%d" % k, 0, 2 * CP), share(to)[k]) for k in to], "ax%d",
+                 [n % k for k in to for n in ("sc%dx", "sc%dg")])
     for k in (1, 2, 3):
-        take(k)
-        out[k] = send([(k, codes("lc%d" % k, 0, 2 * CP), codes("sc%d" % k, 0, 2 * CP), eng[k])], "ax%d",
-                      ["sc%dx" % k, "sc%dg" % k])
-    b = send([(k, T["lc%ds" % k][:, 0:2 * CP], T["sc%ds" % k][:, 0:2 * CP], half[k]) for k in (2, 3, 1)], "ax%d",
-             [n % k for k in (2, 3, 1) for n in ("sc%dxs", "sc%dgs")])
-    for k in (1, 2, 3):
-        arrive("ax%d" % k, len(eng[k]) + len(half[k]), ["lc%d" % k], [out[k], b], OUT[k])
-    turn_of[0] = "k0"
-    take(0)
+        arrive("ax%d" % k, ["lc%d" % k])
+    dma("Y", "dv", T.vt[:, :], T.v[:, :], ["lc1"], ["vt"])
     came = {k: ["lc%d" % k] for k in (1, 2, 3)}
     came[0] = ["lc0x", "lc0g", "lc0xs", "lc0gs"]
 
-    turn_of[0] = "prep"
     for b in range(4):
-        act(T.et[:, 512 * b + b:512 * b + 512:4], T.idn[:, :], F.Copy, ["idn", "ez%d" % b], ["et%d" % b])
-    quant("eq", 0, 512, "et", 0, 2048, ["et0", "et1", "et2", "et3"], ["eq"])
-    quant("wq", 0, 512, "wt", 0, 2048, ["wt"], ["wq"])
-    quant("uq", 0, 512, "ut", 0, 2048, ["ut"], ["uq"])
+        quant("eq", 128 * b, 128 * b + 128, "et", 3 - b, 515 - b, ["et"], ["eq%d" % b])
+    quant("wq", 0, 256, "wt", 0, 1024, ["wt"], ["wq0", "wq1"])
+    quant("wq", 256, 512, "wt", 1024, 2048, ["wt"], ["wq2", "wq3"])
+    quant("uq", 0, 256, "ut", 0, 1024, ["ut"], ["uq0", "uq1"])
+    quant("uq", 256, 512, "ut", 1024, 2048, ["ut"], ["uq2", "uq3"])
     quant("vq", 0, 128, "vt", 0, 512, ["vt"], ["vq"])
     for t in range(4):
         act(T.ppt[:, t:512:4], T.nt[:, 0:128], F.Identity, ["nt", "prt"], ["ppt%d" % t], bias=T.prt[:, t:t + 1])
     quant("pp", 0, 128, "ppt", 0, 512, ["ppt%d" % t for t in range(4)], ["pp"])
     for t, v in ((0, -256.0), (1, 160.0), (2, -1.0), (3, 0.0)):
-        act(T.wnt[:, t:512:4], T.ot[:, 0:128], F.Copy, ["one"], ["wnt%d" % t], scale=v)
+        act(T.wnt[:, t:512:4], T.nt[:, 0:128], F.Copy, ["nt"], ["wnt%d" % t], bias=v)
     quant("wn", 0, 128, "wnt", 0, 512, ["wnt%d" % t for t in range(4)], ["wn"])
-    clear(T.pt[:, 0:512], "pt0")
-    clear(T.pt[:, 512:1024], "pt1")
+    clear(T.pt[:, 0:272], "pt0")
+    clear(T.pt[:, 272:528], "pt1")
     ts(T.pt[:, 0:11:5], T.nt[:, 0:3], HIGH, None, A.add, None, ["nt", "owb", "pt0"], ["pth"])
-    ts(T.pt[:, 512:523:5], T.nt[:, 0:3], P15, None, A.add, None, ["nt", "owb", "pt1"], ["ptl"])
-    quant("cq", 0, 256, "pt", 0, 1024, ["pt0", "pt1", "pth", "ptl"], ["cq"])
+    ts(T.pt[:, 16:27:5], T.nt[:, 0:3], P15, None, A.add, None, ["nt", "owb", "pt0"], ["ptl"])
+    quant("cq", 0, 132, "pt", 0, 528, ["pt0", "pt1", "pth", "ptl"], ["cq"])
     for k in range(4):
         clear(T.mt[:, 512 * k + 448:512 * k + 512], "mz%d" % k)
         clear(T.dxt[:, 512 * k + 448:512 * k + 512], "dz%d" % k)
+        if k:
+            clear(T.ot[:, 512 * k + 7:512 * k + 512:4], "ot%d_3" % k)
+    fill(T.ot[:, 1027:2051:512], 0.0, ["ot23"])
     fill(pf(12), EPS, ["eps"])
 
-    def bank(k, x):
-        return (T.px if k % 2 else T.pz), 512 * x, "*%s%d" % ("zx"[k % 2], x)
+    def bank(h, x):
+        return T["p" + h], 512 * x, "*%s%d" % (h, x)
 
-    def stage1(k):
+    def stage1(k, h):
         lc, c = "lc%d" % k, came[k]
         for b in range(4):
-            ps, x, key = bank(k, b % 2)
-            mm(ps[:, x:x + 128], "wq", 128 * b, lc, 96, 128, True, True, ["wq"] + c, [key])
+            ps, x, key = bank(h, b % 2)
+            mm(ps[:, x:x + 128], "wq", 128 * b, lc, 96, 128, True, True, ["wq%d" % b] + c, [key])
             o = 448 * k + CP * b
-            if b == 3:
+            if b >= int(OPT["mv"][k]):
                 ts(T.mk[:, o:o + CP], ps[:, x + 16:x + 128], 0.0, None, A.is_gt, None, [key], ["mk%d_%d" % (k, b)])
             else:
                 act(T.sm[:, o:o + CP], ps[:, x + 16:x + 128], F.Sign, [key], ["sm%d_%d" % (k, b)])
                 act(T.mk[:, o:o + CP], T.sm[:, o:o + CP], F.Relu, ["sm%d_%d" % (k, b)], ["mk%d_%d" % (k, b)])
-            ps, x, key = bank(k, 2 + b % 2)
-            mm(ps[:, x:x + 128], "eq", 128 * b, lc, 0, 128, True, True, ["eq"] + c, [key])
+            ps, x, key = bank(h, 2 + b % 2)
+            mm(ps[:, x:x + 128], "eq", 128 * b, lc, 0, 128, True, True, ["eq%d" % b] + c, [key])
             tt(T.mt[:, 512 * k + b:512 * k + 448:4], T.mk[:, o:o + CP], ps[:, x:x + CP], A.mult,
-               ["mk%d_%d" % (k, b), key], ["mt%d_%d" % (k, b)], True)
+               ["mk%d_%d" % (k, b), key], ["mt%d_%d" % (k, b)])
         quant("qm", 128 * k, 128 * k + 128, "mt", 512 * k, 512 * k + 512,
               ["mz%d" % k] + ["mt%d_%d" % (k, b) for b in range(4)], ["qm%d" % k])
 
-    def stage2(k):
-        m, rk, one_hot = "qm%d" % k, T.rk[:, 4 * k:4 * k + 1], T.ot[:, 512 * k:512 * k + 512]
-        pc, xc, kc = bank(k, 1)
-        pr, xr, kr = bank(k, 0)
+    def stage2(k, h):
+        m, rk = "qm%d" % k, T.rx[:, 448 + CP * k + CP - 1:448 + CP * k + CP]
+        pc, xc, kc = bank(h, 1)
+        pr, xr, kr = bank(h, 0)
         mm(pc[:, xc:xc + 128], "qm", 128 * k, "pp", 0, 128, True, True, [m, "pp"], [kc])
         mm(pr[:, xr:xr + 128], "pp", 0, "qm", 128 * k, 128, True, True, [m, "pp"], [kr])
         act(T.ca[:, 4 * k:4 * k + 1], pc[:, xc:xc + 1], F.Abs, [kc, "eps"], ["ca%d" % k], bias=pf(12))
-        s, sd, sx = (slice(c + CP * k, c + CP * k + CP) for c in (0, 448, 896))
+        s, sd = (slice(c + CP * k, c + CP * k + CP) for c in (0, 448))
         act(T.ra[:, s], pr[:, xr:xr + CP], F.Abs, [kr, "eps"], ["ra%d" % k], bias=pf(12))
         act(T.ra[:, sd], T.tri[:, :], F.Copy, ["tri", "ca%d" % k], ["rd%d" % k], scale=T.ca[:, 4 * k:4 * k + 1])
         if k:
-            tt(T.ra[:, sx], T.ra[:, s], T.ra[:, sd], A.is_gt, ["rd%d" % k, "ra%d" % k], ["rx%d" % k])
-            run("V", lambda e: e.tensor_reduce(rk, T.ra[:, sx], AxisListType.X, A.add), ["rx%d" % k], ["rk%d" % k], 0.11)
-            ts(one_hot, T.k4[:, :], rk, None, A.is_equal, None, ["k4", "rk%d" % k], ["ot%d" % k], True)
+            tt(T.rx[:, s], T.ra[:, s], T.ra[:, sd], A.is_gt, ["rd%d" % k, "ra%d" % k], ["rx%d" % k])
+            scan(T.rx[:, sd], T.rx[:, s], T.nt[:, 0:CP], ["rx%d" % k, "nt"], ["rk%d" % k])
+            for t in range(3):
+                ts(T.ot[:, 512 * k + t:512 * k + 512:4], T.k4[:, 128 * t:128 * t + 128], rk, None, A.is_equal, None,
+                   ["k4", "rk%d" % k], ["ot%d_%d" % (k, t)])
         else:
-            tt(T.ot[:, 0:448:4], T.ra[:, s], T.ra[:, sd], A.is_gt, ["rd0", "ra0"], ["ot0", "one"])
-        quant("qo", 128 * k, 128 * k + 128, "ot", 512 * k, 512 * k + 512, ["ot%d" % k], ["qo%d" % k])
+            tt(T.ot[:, 0:448:4], T.ra[:, s], T.ra[:, sd], A.is_gt, ["rd0", "ra0"], ["ot0_0", "one"])
+        quant("qo", 128 * k, 128 * k + 128, "ot", 512 * k, 512 * k + 512,
+              ["ot23"] + ["ot%d_%d" % (k, t) for t in range(4 if k else 1)], ["qo%d" % k])
         for b, y in ((0, 2), (1, 3), (2, 1), (3, 0)):
-            ps, x, key = bank(k, y)
-            mm(ps[:, x:x + 128], "uq", 128 * b, "qm", 128 * k, 128, True, True, ["uq", m], [key])
+            ps, x, key = bank(h, y)
+            mm(ps[:, x:x + 128], "uq", 128 * b, "qm", 128 * k, 128, True, True, ["uq%d" % b, m], [key])
             act(T.dxt[:, 512 * k + b:512 * k + 448:4], ps[:, x:x + CP], F.Copy, [key], ["dt%d_%d" % (k, b)], scale=0.0625)
 
-    def stage3(k):
-        ps, x, key = bank(k, 2)
+    def stage3(k, h):
+        ps, x, key = bank(h, 2)
         quant("qd", 128 * k, 128 * k + 128, "dxt", 512 * k, 512 * k + 512,
               ["dz%d" % k] + ["dt%d_%d" % (k, b) for b in range(4)], ["qd%d" % k])
         if not k:
             mm(ps[:, x:x + 128], "wn", 0, "qo", 0, 128, True, True, ["qo0", "wn"], [key])
-            tt(T.tab[:, 0:CP], T.idr[:, 0:CP], ps[:, x:x + CP], A.max, ["idr", key], ["tab0"], True)
+            tt(T.tab[:, 0:CP], T.idr[:, 0:CP], ps[:, x:x + CP], A.max, ["idr", key], ["tab0"])
             return
         if k == 3:
-            a = send([(3, codes("ld3", 0, CP + 2), codes("qd", 384, 386 + CP), eng[3])], "ar%d", ["qd3"])
-            b = send([(3, T.ld3s[:, 0:CP + 2], T.qds[:, 384:386 + CP], eng[3])], "ar%d", ["qd3"])
-            arrive("ar3", 2 * len(eng[3]), ["ld3", "ld3s"], [a, b], BACK)
+            send([(3, codes("ld3", 0, CP + 2), codes("qd", 384, 386 + CP), eng[3])], "ar%d", ["qd3"])
+            send([(3, T.ld3s[:, 0:CP + 2], T.qds[:, 384:386 + CP], eng[3])], "ar%d", ["qd3"])
         for c in (0, 1):
-            mm(ps[:, x:x + 128], "qo", 128 * k, "cq", 128 * c, 128, c == 0, c == 1, ["qo%d" % k, "cq"], [key])
+            mm(ps[:, x:x + 128], "qo", 128 * k, "cq", 4 * c, 128, c == 0, c == 1, ["qo%d" % k, "cq"], [key])
         cp(T.lo[:, 8 * k:8 * k + 3], ps[:, x:x + 3], [key], ["lo%d" % k])
         if k < 3:
-            d, (c, z, h) = "sd%d" % k, {1: (0, 0, 0), 2: (176, 128, 66)}[k]
-            pick("nq", c, CR, "qd", 128 * k, 128 * k + 128, T.lo[:, 8 * k:8 * k + 3], ["qd%d" % k, "lo%d" % k], d)
-        if k != 2:
-            to = (1,) if k == 1 else (2, 3)
-            a = send([(j, T.ll[:, 8 * j:8 * j + 3], T.lo[:, 8 * j:8 * j + 3], half[j]) for j in to], "al%d",
-                     ["lo%d" % j for j in to])
-            for j in to:
-                arrive("al%d" % j, len(half[j]), ["ll%d" % j], [a], BACK - 0.5)
-        if k < 3:
-            b = send([(k, codes("ld%d" % k, h, h + 24), codes("nq", c, c + 24), eng[k][0:2]),
-                      (k, codes("ld%d" % k, h + 24, h + 48), codes("nq", c + 24, c + 48), eng[k][2:4]),
-                      (k, T["ld%ds" % k][:, h + z - c:h + z - c + 96], T.nqs[:, z:z + 96], eng[k][4:8])], "ar%d",
-                     [d, d + "s", "nq"])
-            arrive("ar%d" % k, len(eng[k]), ["ld%d" % k, "ld%ds" % k], [b], BACK)
+            pick("nq", 176 * k - 176, CR, "qd", 128 * k, 128 * k + 128, T.lo[:, 8 * k:8 * k + 3],
+                 ["qd%d" % k, "lo%d" % k], "sd%d" % k)
 
-    turn_of[0] = "look"
     fill(T.tab[:, 0:384], 0.0, ["tab0", "tab2", "tab3"])
     fill(T.tab[:, 384:512], float(CR), ["tab1"])
-    for k in range(4):
-        turn_of[0] = "k%d" % k
-        stage1(k)
-        turn_of[0] = "k%db" % k
-        stage2(k)
-        turn_of[0] = "k%dc" % k
-        stage3(k)
+    for k in [int(c) for c in OPT["seq"]]:
+        stage1(k, OPT["bank"][k])
+        stage2(k, OPT["bank"][k])
+        stage3(k, OPT["bank"][k])
+    at = {1: (0, 0, 0, 0), 2: (176, 66, 128, 174)}
+    for w in OPT["back"].split():
+        to = [int(c) for c in w[1:]]
+        es = share(to)
+        if w[0] == "l":
+            send([(j, T.ll[:, 8 * j:8 * j + 3], T.lo[:, 8 * j:8 * j + 3], es[j]) for j in to], "al%d", ["lo%d" % j for j in to])
+        elif w[0] == "t":
+            k = to[0]
+            c, h, z, _y = at[k]
+            send([(k, codes("ld%d" % k, h, h + 24), codes("nq", c, c + 24), eng[k][0:2]),
+                  (k, codes("ld%d" % k, h + 24, h + 48), codes("nq", c + 24, c + 48), eng[k][2:4]),
+                  (k, T["ld%ds" % k][:, h + z - c:h + z - c + 96], T.nqs[:, z:z + 96], eng[k][4:8])], "ar%d",
+                 ["sd%d" % k, "sd%ds" % k, "nq"])
+        elif w[0] == "c":
+            send([(k, codes("ld%d" % k, at[k][1], at[k][1] + CR), codes("nq", at[k][0], at[k][0] + CR), es[k]) for k in to],
+                 "ar%d", ["sd%d" % k for k in to])
+        else:
+            send([(k, T["ld%ds" % k][:, 64 * k - 64:64 * k - 14], T.nqs[:, at[k][3]:at[k][3] + 50], es[k]) for k in to],
+                 "ar%d", ["nq"] + ["sd%ds" % k for k in to])
+    for k in (1, 2, 3):
+        arrive("al%d" % k, ["ll%d" % k])
+        arrive("ar%d" % k, ["ld%d" % k])
 
-    turn_of[0] = "look"
-    h1, h2, h3, h4, h5, h6, h7, h8, h9, h10 = (T.hh[:, 24 * i:24 * i + 24] for i in range(10))
-    cp(T.win[:, :], T.ss[:, 2:3 * NT:3], ["ss"], ["win"], el(NT // 2))
+    h1, h2, h3, h4, h5, h6, h7, h8, h9 = (T.hh[:, 24 * i:24 * i + 24] for i in range(9))
     turn(T.tv[:, 0:NT], T.win[:, :], ["win"], ["tw"])
     turn(T.tv[:, NT:2 * NT], T.pref[:, :], ["pref"], ["tp"])
-    tw, tp = T.tv[:, 0:NT:8], T.tv[:, NT:2 * NT:8]
-    ts(h1, tw, 0.0, None, A.is_gt, None, ["tw"], ["h1"])
-    ts(h2, tp, float(CP), None, A.is_le, None, ["tp"], ["h2"])
-    ts(h6, tw, 4.0, 1.0, A.is_lt, A.add, ["tw"], ["h6"])
-    tt(h4, h1, h2, A.mult, ["h1", "h2"], ["h4"])
-    ts(h7, tp, 1.0 / 7, -4.0 / 7, A.mult, A.add, ["tp"], ["h7"])
-    ts(h8, h7, WHOLE, WHOLE, A.add, A.subtract, ["h7"], ["h8"])
-    ts(h9, h8, -111.0, -16.0 - CP, A.mult, A.add, ["h8"], ["h9"])
-    act(h10, tp, F.Copy, ["tp"], ["h10"], scale=16.0)
-    tt(h3, h9, h10, A.add, ["h9", "h10"], ["h3"])
+    tw, tp = T.tv[:, 0:NT:8], T.tv[:, NT + 3:2 * NT:8]
+    ts(h1, tw, 2.5, 2.0 * CP + 2, A.is_gt, A.mult, ["tw"], ["h1"])
+    ts(h6, tw, 3.5, 1.0, A.is_lt, A.add, ["tw"], ["h6"])
+    act(h2, tp, F.Copy, ["tp"], ["h2"], bias=8.0)
+    tt(h4, h2, h1, A.is_lt, ["h1", "h2"], ["h4"])
+    ts(h7, tp, 0.999 / 14, WHOLE, A.mult, A.add, ["tp"], ["h7"])
+    ts(h8, h7, WHOLE, -111.0, A.subtract, A.mult, ["h7"], ["h8"])
+    act(h9, tp, F.Copy, ["tp"], ["h9"], scale=8.0, bias=40.0 - CP)
+    tt(h3, h8, h9, A.add, ["h8", "h9"], ["h3"])
     tt(h5, h4, h3, A.mult, ["h4", "h3"], ["h5"])
     ts(pf(10), ODD, -1.0, 1.0, A.mult, A.add, ["owb"], ["pf10"])
     for k in (0, 1, 2, 3):
@@ -442,32 +418,30 @@ def rank_program(g, core, T, topo):
         s, s1 = slice(192 * k, 192 * k + 192), slice(768 + 192 * k, 960 + 192 * k)
         lst, g1 = T.ll[:, 8 * k:8 * k + 3], T.gg[:, 768 + 192 * k:960 + 192 * k:16]
         if k in (1, 2):
-            cp(tab.indirect(lst), T.vals[:, 2 * k - 2:2 * k - 2 + CR], ["vals", "ll%d" % k], ["tab%d" % k], 0.23)
+            cp(tab.indirect(lst), T.vals[:, 2 * k - 2:2 * k - 2 + CR], ["vals", "ll%d" % k], ["tab%d" % k])
         elif k:
-            cp(tab.indirect(lst), T.ot[:, 448:448 + CR], ["oneb", "ll3"], ["tab3"], 0.23)
-            act(T.gid[:, :], T.idr[:, :].indirect(offt), F.Copy, ["idr"] + ko, ["gid"], 0.35)
+            cp(tab.indirect(lst), T.ot[:, 448:448 + CR], ["oneb", "ll3"], ["tab3"])
+            act(T.gid[:, :], T.idr[:, :].indirect(offt), F.Copy, ["idr"] + ko, ["gid"])
         if k == 3:
-            run("V", lambda e: e.tensor_tensor(T.gg[:, s], tab.indirect(offt), T.gid[:, :], A.mult),
-                ["tab3", "gid"] + ko, ["gr03"], 0.35)
+            tt(T.gg[:, s], tab.indirect(offt), T.gid[:, :], A.mult, ["tab3", "gid"] + ko, ["gr03"])
         else:
-            act(T.gg[:, s], tab.indirect(offt), F.Copy, ["tab%d" % k] + ko, ["gr0%d" % k], 0.35)
+            act(T.gg[:, s], tab.indirect(offt), F.Copy, ["tab%d" % k] + ko, ["gr0%d" % k])
         turn(T.gg[:, s1], T.gg[:, s], ["gr0%d" % k], ["gr1%d" % k])
         if k in (1, 2):
             cp(of, g1, ["gr1%d" % k], ["hof%d" % k])
-            pick(zc, 0, NT, "ld%d" % k, 64 * k - 64, 64 * k - 14, of, ["hof%d" % k, "ld%d" % k, "ld%ds" % k, "ldz"], zc)
+            pick(zc, 0, NT, "ld%d" % k, 64 * k - 64, 64 * k - 14, of, ["hof%d" % k, "ld%d" % k, "ldz"], zc)
         else:
             ts(of, g1, 0.0, float(CP), A.min, A.add, ["gr1%d" % k], ["hof%d" % k])
             if k:
-                pick(zc, 0, NT, "ld3", 0, CP + 2, of, ["hof3", "ld3", "ld3s"], zc)
+                pick(zc, 0, NT, "ld3", 0, CP + 2, of, ["hof3", "ld3"], zc)
             else:
                 pick(zc, 0, NT, "qd", 0, 128, of, ["hof0", "qd0"], zc)
         for b in range(4):
-            mm(T.pz[:, 512 * b:512 * b + NT], "eq", 128 * b, zc, 0, NT, first, last, ["eq", zc, zc + "s"], ["*z%d" % b])
+            ps, x, key = bank(OPT["sum"], b)
+            mm(ps[:, x:x + NT], "eq", 128 * b, zc, 0, NT, first, last, ["eq%d" % b, zc, zc + "s"], [key])
 
-    for k in range(4):
-        turn_of[0] = "h%d" % k
-        home(k, k == 0, k == 3)
-    turn_of[0] = "ct"
+    for i, k in enumerate([int(c) for c in OPT["seq"]]):
+        home(k, i == 0, i == 3)
     ts(T.ff[:, 0:24], T.hof[:, 0:24], CP - 0.5, None, A.is_lt, None, ["hof0", "hof3"], ["fl0"])
     ts(T.ff[:, 24:36], T.hof[:, 24:36], CR - 0.5, None, A.is_lt, None, ["hof1"], ["fl1"])
     ts(T.ff[:, 36:48], T.hof[:, 36:48], 1.0, None, A.is_gt, None, ["hof2"], ["fl2"])
@@ -476,67 +450,26 @@ def rank_program(g, core, T, topo):
     tt(T.ff[:, 96:120], T.ff[:, 48:72], T.ff[:, 72:96], A.add, ["fw"], ["fs"])
     tt(T.ff[:, 120:132], T.ff[:, 96:108], T.ff[:, 108:120], A.add, ["fs"], ["ft"])
     tt(T.cs[:, 0:6], T.ff[:, 120:132:2], T.ff[:, 121:132:2], A.add, ["ft", "csz"], ["cs"])
-    turn(T.cst[0:32, :], T.cs[0:32, :], ["cs", "csz"], ["cst"], True)
+    turn(T.cst[0:32, :], T.cs[0:32, :], ["cs", "csz"], ["cst"])
 
-    turn_of[0] = ""
     for b in range(4):
-        move = (T.zt[:, b:768:4], T.pz[:, 512 * b:512 * b + NT])
+        ps, x, key = bank(OPT["sum"], b)
         if b % 2:
-            cp(move[0], move[1], ["*z%d" % b], ["zt%d" % b])
+            cp(T.zt[:, b:768:4], ps[:, x:x + NT], [key], ["zt%d" % b])
         else:
-            act(move[0], move[1], F.Copy, ["*z%d" % b], ["zt%d" % b])
+            act(T.zt[:, b:768:4], ps[:, x:x + NT], F.Copy, [key], ["zt%d" % b])
     quant("zq", 0, 192, "zt", 0, 768, ["zt0", "zt1", "zt2", "zt3"], ["zq"])
-    mm(T.px[:, 0:NT], "vq", 0, "zq", 0, NT, True, True, ["vq", "zq"], ["*x0"])
-    cp(T.ysb[:, :], T.px[:, 0:NT], ["*x0"], ["ysb"])
-    dma("Y", "doy", T.ct[0:1, 0:NT], T.cst[0:6, 0:32], ["cst"], [], 2.0)
-    dma("Y", "doy", T.oc[:, 0:768], T.zq[:, 0:NT].bitcast(dt.uint8), ["zq"], [], 2.0)
+    ps, x, key = bank("zx".replace(OPT["sum"], ""), 0)
+    mm(ps[:, 0:NT], "vq", 0, "zq", 0, NT, True, True, ["vq", "zq"], [key])
+    cp(T.ysb[:, :], ps[:, 0:NT], [key], ["ysb"])
+    dma("Y", "doy", T.ct[0:1, 0:NT], T.cst[0:6, 0:32], ["cst"], [])
+    dma("Y", "doy", T.oc[:, 0:768], T.zq[:, 0:NT].bitcast(dt.uint8), ["zq"], [])
     for i in range(4):
         q, s = ("S", "dos") if i < 3 else ("Y", "doy")
-        dma(q, s, T.osc[4 * i:4 * i + 4, 0:NT], T.zqs[32 * i:32 * i + 4, 0:NT], ["zq"], [], 2.0)
-    dma("Y", "doy", T.y[:, :], T.ysb[:, :], ["ysb"], [], 2.0)
+        dma(q, s, T.osc[4 * i:4 * i + 4, 0:NT], T.zqs[32 * i:32 * i + 4, 0:NT], ["zq"], [])
+    dma("Y", "doy", T.y[:, :], T.ysb[:, :], ["ysb"], [])
 
-    n = len(tasks)
-    follow = [[] for _i in range(n)]
-    for i, t in enumerate(tasks):
-        for j in t["before"]:
-            follow[j].append(i)
-    rest = [0.0] * n
-    for i in range(n - 1, -1, -1):
-        far = max([rest[j] + (HOP if tasks[j]["before"][i] else 0.0) for j in follow[i]] or [0.0])
-        rest[i] = max(far, 0.0) + tasks[i]["cost"] + tasks[i]["late"] + tasks[i]["ahead"]
-    left = [len(t["before"]) for t in tasks]
-    ready = [0.0] * n
-    free = {q: 0.0 for q in ("V", "S", "P", "G", "Y", None)}
-    able = [i for i in range(n) if not left[i]]
-    order = []
-    while able:
-        best = None
-        for q in free:
-            mine = sorted(i for i in able if tasks[i]["q"] == q)
-            if not mine:
-                continue
-            at = max(free[q], min(ready[i] for i in mine)) if q else min(ready[i] for i in mine)
-            pool = [i for i in mine if ready[i] <= at + 1e-9]
-            i = min(pool) if q == "Y" else max(pool, key=lambda j: rest[j])
-            for j in mine:
-                if q not in ("Y", None) and ready[j] < at + HOLD * tasks[i]["cost"] and rest[j] > rest[i] + GAP:
-                    i = j
-            at = max(at, ready[i])
-            if best is None or at < best[0]:
-                best = (at, i)
-        at, i = best
-        t = tasks[i]
-        able.remove(i)
-        order.append(i)
-        if t["q"]:
-            free[t["q"]] = at + t["cost"]
-        done = at + t["cost"] + t["late"]
-        for j in follow[i]:
-            ready[j] = max(ready[j], done + HOP if tasks[j]["before"][i] else at + t["cost"])
-            left[j] -= 1
-            if not left[j]:
-                able.append(j)
-
+    order = [int(w) for w in ORDER.split()] or range(len(tasks))
     waited, token = {}, {}
 
     def need(q, tok):

@@ -5,14 +5,14 @@ NT, CP, CR = 192, 112, 48
 EPS = 2.0 ** -120
 BELOW = 1.0 - 2.0 ** -24
 WHOLE = 1.5 * 2.0 ** 23
-OPT = {"ns": 9, "out": "c13 s13 c2 s2", "back": "l13 l2 t1 c2 s2", "mv": "3333", "seq": "0312", "bank": "zxzz", "sum": "x"}
-ORDER = "27 0 28 10 26 12 32 29 6 33 149 364 148 7 13 16 31 151 14 150 11 25 40 34 24 127 15 20 23 145 35 17 18 36 133 147 1 2 3 4 5 19 49 47 45 142 139 132 135 46 44 48 138 22 21 128 130 50 51 37 52 53 115 134 347 38 54 55 56 30 116 113 57 88 58 136 69 71 73 72 74 68 70 76 81 78 79 75 77 80 337 84 83 65 61 67 64 63 62 60 59 66 129 82 85 86 89 91 99 97 123 87 122 102 98 92 344 90 104 100 101 117 103 342 118 39 143 125 96 114 336 93 152 157 153 124 126 155 158 160 162 167 154 159 163 137 164 156 161 339 165 131 168 166 169 170 171 172 173 119 120 343 349 144 94 174 179 181 175 176 340 182 180 95 8 9 41 105 106 42 108 111 109 185 183 141 184 186 177 338 341 345 178 346 187 348 356 350 362 107 43 110 240 235 238 241 353 236 195 190 112 196 191 242 237 197 192 250 188 189 251 239 205 198 199 193 200 245 207 365 201 146 202 206 194 360 366 208 367 203 243 204 244 248 252 246 247 369 363 209 210 211 212 221 223 225 249 253 368 254 213 214 222 224 226 227 228 256 255 266 285 280 288 357 257 259 258 286 281 287 215 358 216 229 282 375 219 218 217 220 232 233 295 290 260 261 234 283 231 230 291 292 267 289 262 263 264 297 284 272 293 296 265 298 270 271 273 140 294 299 275 276 268 269 300 277 274 302 301 303 304 278 305 306 307 309 308 310 352 335 325 279 372 313 317 311 315 370 355 312 316 318 320 321 314 319 322 324 323 334 330 385 374 354 327 331 326 332 328 121 376 377 351 386 387 329 333 378 379 361 380 359 405 388 395 396 397 373 384 383 381 390 389 371 382 393 391 394 392 398 406 407 399 408 409 410 400 402 403 415 414 404 411 416 412 420 401 413 417 424 421 425 423 422 418 419 426"
+OPT = {"ns": 9, "out": "c13 s13 c2 s2", "back": "l13 l2 u1 w2", "mv": "3322", "seq": "0312"}
+ORDER = "6 27 10 29 28 0 151 7 16 145 35 33 15 144 13 12 26 31 20 11 1 2 3 4 5 147 129 141 14 48 44 46 36 17 18 149 19 47 49 45 344 50 51 52 53 139 21 25 24 40 146 128 22 127 8 32 43 34 113 30 116 54 37 55 114 88 130 56 132 23 143 133 57 135 58 38 74 72 73 68 71 70 69 81 78 79 77 80 76 75 334 84 83 87 65 61 67 63 60 62 59 66 64 82 39 333 85 86 336 97 91 89 99 138 90 102 98 104 100 125 92 94 101 358 339 117 134 103 137 96 118 41 157 152 158 341 162 163 153 9 115 93 95 169 167 337 346 120 155 165 164 168 160 166 356 123 159 170 154 122 161 156 124 136 171 183 352 140 340 105 106 109 185 142 186 335 126 172 173 174 176 107 119 342 179 131 350 175 184 180 195 190 200 108 150 338 343 148 177 353 111 196 284 359 347 357 355 289 201 349 279 293 361 285 280 286 191 281 290 294 291 292 287 202 295 42 282 288 203 207 205 198 193 296 197 192 283 204 297 298 372 206 299 300 301 302 313 315 314 316 309 310 199 194 311 110 112 208 345 209 312 210 211 303 178 304 249 317 212 245 306 305 240 251 213 307 214 235 247 243 215 308 216 250 246 241 236 218 217 219 252 248 242 318 244 237 223 227 238 320 225 321 239 220 322 253 221 230 231 224 228 226 232 222 229 233 254 256 255 257 188 258 360 348 319 269 267 181 189 259 260 263 262 261 234 182 265 264 362 271 272 270 268 266 354 274 187 363 364 275 332 276 273 351 277 365 278 323 331 327 382 371 383 366 325 328 324 329 373 326 374 384 375 402 385 376 377 368 392 393 403 121 387 370 367 381 379 369 380 378 386 389 391 390 388 330 394 395 397 404 396 405 406 407 399 411 408 400 401 413 409 417 412 398 410 414 415 419 418 422 420 421 416 423"
 TAB = {0: 0, 2: 1, 3: 2, 1: 3}
 POS = {0: 0, 3: 1, 1: 2, 2: 3}
 
 SCRATCH = {
     "xt": ("sbuf", [128, 776], "bfloat16"), "gt": ("sbuf", [128, 776], "bfloat16"),
-    "rtt": ("sbuf", [128, 16], "bfloat16"), "prt": ("sbuf", [128, 16], "bfloat16"), "nt": ("sbuf", [128, 512], "bfloat16"),
+    "rtt": ("sbuf", [128, 16], "bfloat16"), "prt": ("sbuf", [128, 16], "bfloat16"), "nt": ("sbuf", [128, 576], "bfloat16"),
     "wt": ("sbuf", [128, 2048], "bfloat16"), "ut": ("sbuf", [128, 2048], "bfloat16"), "ppt": ("sbuf", [128, 512], "bfloat16"),
     "vt": ("sbuf", [128, 512], "bfloat16"), "et": ("sbuf", [128, 516], "bfloat16"), "wnt": ("sbuf", [128, 512], "bfloat16"),
     "pt": ("sbuf", [128, 528], "bfloat16"), "zt": ("sbuf", [128, 768], "bfloat16"),
@@ -36,11 +36,11 @@ SCRATCH = {
     "pz": ("psum", [128, 2048], "float32"), "px": ("psum", [128, 2048], "float32"),
 }
 _CODES = [("xq", 194), ("gq", 194), ("rq", 272), ("bq", 192), ("pp", 128), ("wq", 512), ("uq", 512), ("wn", 128),
-          ("vq", 128), ("eq", 512), ("cq", 132), ("zq", 192), ("qm", 512), ("qd", 512), ("qo", 512), ("nq", 224)]
+          ("vq", 128), ("eq", 512), ("cq", 132), ("zq", 192), ("qm", 512), ("qd", 512), ("qo", 512), ("nq", 240)]
 for _k in range(4):
     _CODES += [("lc%d" % _k, 224), ("zc%d" % _k, 192)]
     if _k:
-        _CODES += [("sc%d" % _k, 224), ("ld%d" % _k, 128)]
+        _CODES += [("sc%d" % _k, 224), ("ld%d" % _k, 224)]
 for _n, _w in _CODES:
     SCRATCH[_n] = ("sbuf", [128, _w], "float8_e4m3fn_x4")
     SCRATCH[_n + "s"] = ("sbuf", [128, _w], "uint8")
@@ -74,12 +74,21 @@ def rank_program(g, core, T, topo):
             for i in read.get(k, []):
                 before[i] = before.get(i, False) or tasks[i]["q"] != q
         n = len(tasks)
-        tasks.append({"q": q, "call": call, "before": before, "sem": sem, "inc": inc})
+        tasks.append({"q": q, "call": call, "before": before, "sem": sem, "inc": inc,
+                      "use": [k for k in reads + writes if k[0] == "*"]})
         for k in reads:
             read.setdefault(k, []).append(n)
         for k in writes:
             wrote[k], read[k] = n, []
         return n
+
+    place = {}
+
+    def at(a):
+        if not isinstance(a, tuple):
+            return a
+        i = place[a[0]]
+        return (T.pz, T.px)[i // 4][:, 512 * (i % 4) + a[1]:512 * (i % 4) + a[2]]
 
     def run(q, call, reads, writes):
         return task(q, call, reads, writes, "c" + q)
@@ -89,18 +98,18 @@ def rank_program(g, core, T, topo):
 
     def ts(out, in0, s1, s2, o0, o1, reads, writes):
         if o1 is None:
-            run("V", lambda e: e.tensor_scalar(out, in0, s1, None, o0), reads, writes)
+            run("V", lambda e: e.tensor_scalar(out, at(in0), s1, None, o0), reads, writes)
         else:
-            run("V", lambda e: e.tensor_scalar(out, in0, s1, s2, o0, o1), reads, writes)
+            run("V", lambda e: e.tensor_scalar(out, at(in0), s1, s2, o0, o1), reads, writes)
 
     def tt(out, a, b, op, reads, writes):
-        run("V", lambda e: e.tensor_tensor(out, a, b, op), reads, writes)
+        run("V", lambda e: e.tensor_tensor(out, a, at(b), op), reads, writes)
 
     def scan(out, a, b, reads, writes, start=0.0):
         run("V", lambda e: e.tensor_tensor_scan(out, a, b, start, A.add, A.add), reads, writes)
 
     def cp(out, a, reads, writes):
-        run("V", lambda e: e.tensor_copy(out, a), reads, writes)
+        run("V", lambda e: e.tensor_copy(out, at(a)), reads, writes)
 
     def turn(out, a, reads, writes):
         run("V", lambda e: e.transpose(out, a), reads, writes)
@@ -109,7 +118,7 @@ def rank_program(g, core, T, topo):
         run("V", lambda e: e.memset(ap, v), [], writes)
 
     def act(out, a, f, reads, writes, **kw):
-        run("S", lambda e: e.activation(out, a, f, **kw), reads, writes)
+        run("S", lambda e: e.activation(out, at(a), f, **kw), reads, writes)
 
     def clear(ap, key):
         act(ap, T.nt[:, 0:ap.shape[1]], F.Copy, ["nt"], [key])
@@ -118,9 +127,9 @@ def rank_program(g, core, T, topo):
         o, s, i = T[q][:, a:b], T[q + "s"][:, a:b], T[tile][:, c:d]
         run("V", lambda e: e.quantize_mx(o, s, i), reads, writes)
 
-    def mm(out, l, la, r, ra, n, start, stop, reads, writes):
+    def mm(use, l, la, r, ra, n, start, stop, reads):
         w, ws, x, xs = T[l][:, la:la + 128], T[l + "s"][:, la:la + 128], T[r][:, ra:ra + n], T[r + "s"][:, ra:ra + n]
-        run("P", lambda e: e.matmul_mx(out, w, ws, x, xs, start, stop), reads, writes)
+        run("P", lambda e: e.matmul_mx(at((use, 0, n)), w, ws, x, xs, start, stop), reads, [use])
 
     def pick(dst, c, n, src, a, b, offs, reads, key):
         cp(T[dst][:, c:c + n].bitcast(dt.uint32), T[src][:, a:b].bitcast(dt.uint32).indirect(offs), reads, [key])
@@ -175,9 +184,9 @@ def rank_program(g, core, T, topo):
     dma("Y", "dub", T.ut[:, :], T.ub[:, :], [], ["ut"])
 
     fill(T.nt[:, :], 0.0, ["nt"])
-    quant("nq", 48, 176, "nt", 0, 512, ["nt"], ["nq"])
-    send([(k, codes("ld%d" % k, z, z + 2), codes("nq", c, c + 2), eng[k]) for k, z, c in ((2, 64, 174), (1, 48, 48))],
-         "az", ["nq"])
+    quant("nq", 48, 192, "nt", 0, 576, ["nt"], ["nq"])
+    send([(2, codes("ld2", 160, 161), codes("nq", 191, 192), eng[2]), (1, codes("ld1", 48, 49), codes("nq", 48, 49), eng[1][0:4]),
+          (1, T.ld1s[:, 48:52], T.nqs[:, 48:52], eng[1][4:8])], "az", ["nq"])
     arrive("az", ["ldz"])
 
     def pf(i):
@@ -224,12 +233,12 @@ def rank_program(g, core, T, topo):
         cp(T.rct[:, 576 + c:576 + c + n], T.rtt[:, 0:n], ["rtt", "rcz"], ["rc%d" % d])
     quant("rq", 0, 272, "rct", 0, 1088, ["rc0"] + [n % d for n in ("rb%d", "rc%d") for d in (1, 2, 3)], ["rq"])
     quant("xq", 0, 194, "xt", 0, 776, ["xt", "xz"], ["xq"])
-    mm(T.px[:, 0:NT], "rq", 144, "xq", 0, NT, True, False, ["rq", "xq"], ["*x0"])
-    mm(T.px[:, 0:NT], "rq", 126, "xq", 0, NT, False, True, ["rq", "xq"], ["*x0"])
-    ts(T.bt[:, 0:768:4], T.px[:, 0:NT], 0.0, None, A.is_ge, None, ["*x0", "bz0", "bz1"], ["bt"])
+    mm("*d", "rq", 144, "xq", 0, NT, True, False, ["rq", "xq"])
+    mm("*d", "rq", 126, "xq", 0, NT, False, True, ["rq", "xq"])
+    ts(T.bt[:, 0:768:4], ("*d", 0, NT), 0.0, None, A.is_ge, None, ["*d", "bz0", "bz1"], ["bt"])
     quant("bq", 0, NT, "bt", 0, 768, ["bt"], ["bq"])
-    mm(T.px[:, 512:512 + NT], "rq", 0, "bq", 0, NT, True, True, ["rq", "bq"], ["*x1"])
-    ts(T.m[:, 2:2 + NT], T.px[:, 512:512 + NT], 2.5, None, A.is_gt, None, ["*x1"], ["m"])
+    mm("*w", "rq", 0, "bq", 0, NT, True, True, ["rq", "bq"])
+    ts(T.m[:, 2:2 + NT], ("*w", 0, NT), 2.5, None, A.is_gt, None, ["*w"], ["m"])
     scan(T.pref[:, :], T.m[:, 2:2 + NT], T.m[:, 1:1 + NT], ["m", "mz", "owc"], ["pref"], M7)
 
     def piece(i, t):
@@ -250,7 +259,7 @@ def rank_program(g, core, T, topo):
         cp(T.cn[:, c + NS:c + 16], last, ["ls%d" % t for t in range(NS, 16)], ["cnl%d" % c])
     turn(T.cnt[:, :], T.cn[:, :], mine + ["cnd", "cnl0", "cnl16"], ["cnt"])
     ts(T.off[:, :], T.cnt[:, :], BASE, None, A.add, None, ["cnt", "owc"], ["off"])
-    act(T.win[:, :], T.px[:, 512:512 + NT], F.Copy, ["*x1"], ["win"])
+    act(T.win[:, :], ("*w", 0, NT), F.Copy, ["*w"], ["win"])
     quant("gq", 0, 194, "gt", 0, 776, ["gt", "gz"], ["gq"])
 
     for k in (1, 2, 3, 0):
@@ -297,36 +306,32 @@ def rank_program(g, core, T, topo):
     fill(T.ot[:, 1027:2051:512], 0.0, ["ot23"])
     fill(pf(12), EPS, ["eps"])
 
-    def bank(h, x):
-        return T["p" + h], 512 * x, "*%s%d" % (h, x)
-
-    def stage1(k, h):
+    def stage1(k):
         lc, c = "lc%d" % k, came[k]
         for b in range(4):
-            ps, x, key = bank(h, b % 2)
-            mm(ps[:, x:x + 128], "wq", 128 * b, lc, 96, 128, True, True, ["wq%d" % b] + c, [key])
+            key = "*f%d%d" % (k, b)
+            mm(key, "wq", 128 * b, lc, 96, 128, True, True, ["wq%d" % b] + c)
             o = 448 * k + CP * b
             if b >= int(OPT["mv"][k]):
-                ts(T.mk[:, o:o + CP], ps[:, x + 16:x + 128], 0.0, None, A.is_gt, None, [key], ["mk%d_%d" % (k, b)])
+                ts(T.mk[:, o:o + CP], (key, 16, 128), 0.0, None, A.is_gt, None, [key], ["mk%d_%d" % (k, b)])
             else:
-                act(T.sm[:, o:o + CP], ps[:, x + 16:x + 128], F.Sign, [key], ["sm%d_%d" % (k, b)])
+                act(T.sm[:, o:o + CP], (key, 16, 128), F.Sign, [key], ["sm%d_%d" % (k, b)])
                 act(T.mk[:, o:o + CP], T.sm[:, o:o + CP], F.Relu, ["sm%d_%d" % (k, b)], ["mk%d_%d" % (k, b)])
-            ps, x, key = bank(h, 2 + b % 2)
-            mm(ps[:, x:x + 128], "eq", 128 * b, lc, 0, 128, True, True, ["eq%d" % b] + c, [key])
-            tt(T.mt[:, 512 * k + b:512 * k + 448:4], T.mk[:, o:o + CP], ps[:, x:x + CP], A.mult,
+            key = "*g%d%d" % (k, b)
+            mm(key, "eq", 128 * b, lc, 0, 128, True, True, ["eq%d" % b] + c)
+            tt(T.mt[:, 512 * k + b:512 * k + 448:4], T.mk[:, o:o + CP], (key, 0, CP), A.mult,
                ["mk%d_%d" % (k, b), key], ["mt%d_%d" % (k, b)])
         quant("qm", 128 * k, 128 * k + 128, "mt", 512 * k, 512 * k + 512,
               ["mz%d" % k] + ["mt%d_%d" % (k, b) for b in range(4)], ["qm%d" % k])
 
-    def stage2(k, h):
+    def stage2(k):
         m, rk = "qm%d" % k, T.rx[:, 448 + CP * k + CP - 1:448 + CP * k + CP]
-        pc, xc, kc = bank(h, 1)
-        pr, xr, kr = bank(h, 0)
-        mm(pc[:, xc:xc + 128], "qm", 128 * k, "pp", 0, 128, True, True, [m, "pp"], [kc])
-        mm(pr[:, xr:xr + 128], "pp", 0, "qm", 128 * k, 128, True, True, [m, "pp"], [kr])
-        act(T.ca[:, 4 * k:4 * k + 1], pc[:, xc:xc + 1], F.Abs, [kc, "eps"], ["ca%d" % k], bias=pf(12))
+        kc, kr = "*c%d" % k, "*r%d" % k
+        mm(kc, "qm", 128 * k, "pp", 0, 128, True, True, [m, "pp"])
+        mm(kr, "pp", 0, "qm", 128 * k, 128, True, True, [m, "pp"])
+        act(T.ca[:, 4 * k:4 * k + 1], (kc, 0, 1), F.Abs, [kc, "eps"], ["ca%d" % k], bias=pf(12))
         s, sd = (slice(c + CP * k, c + CP * k + CP) for c in (0, 448))
-        act(T.ra[:, s], pr[:, xr:xr + CP], F.Abs, [kr, "eps"], ["ra%d" % k], bias=pf(12))
+        act(T.ra[:, s], (kr, 0, CP), F.Abs, [kr, "eps"], ["ra%d" % k], bias=pf(12))
         act(T.ra[:, sd], T.tri[:, :], F.Copy, ["tri", "ca%d" % k], ["rd%d" % k], scale=T.ca[:, 4 * k:4 * k + 1])
         if k:
             tt(T.rx[:, s], T.ra[:, s], T.ra[:, sd], A.is_gt, ["rd%d" % k, "ra%d" % k], ["rx%d" % k])
@@ -338,54 +343,46 @@ def rank_program(g, core, T, topo):
             tt(T.ot[:, 0:448:4], T.ra[:, s], T.ra[:, sd], A.is_gt, ["rd0", "ra0"], ["ot0_0", "one"])
         quant("qo", 128 * k, 128 * k + 128, "ot", 512 * k, 512 * k + 512,
               ["ot23"] + ["ot%d_%d" % (k, t) for t in range(4 if k else 1)], ["qo%d" % k])
-        for b, y in ((0, 2), (1, 3), (2, 1), (3, 0)):
-            ps, x, key = bank(h, y)
-            mm(ps[:, x:x + 128], "uq", 128 * b, "qm", 128 * k, 128, True, True, ["uq%d" % b, m], [key])
-            act(T.dxt[:, 512 * k + b:512 * k + 448:4], ps[:, x:x + CP], F.Copy, [key], ["dt%d_%d" % (k, b)], scale=0.0625)
+        for b in range(4):
+            key = "*u%d%d" % (k, b)
+            mm(key, "uq", 128 * b, "qm", 128 * k, 128, True, True, ["uq%d" % b, m])
+            act(T.dxt[:, 512 * k + b:512 * k + 448:4], (key, 0, CP), F.Copy, [key], ["dt%d_%d" % (k, b)], scale=0.0625)
 
-    def stage3(k, h):
-        ps, x, key = bank(h, 2)
+    def stage3(k):
+        key = "*l%d" % k
         quant("qd", 128 * k, 128 * k + 128, "dxt", 512 * k, 512 * k + 512,
               ["dz%d" % k] + ["dt%d_%d" % (k, b) for b in range(4)], ["qd%d" % k])
         if not k:
-            mm(ps[:, x:x + 128], "wn", 0, "qo", 0, 128, True, True, ["qo0", "wn"], [key])
-            tt(T.tab[:, 0:CP], T.idr[:, 0:CP], ps[:, x:x + CP], A.max, ["idr", key], ["tab0"])
+            mm(key, "wn", 0, "qo", 0, 128, True, True, ["qo0", "wn"])
+            tt(T.tab[:, 0:CP], T.idr[:, 0:CP], (key, 0, CP), A.max, ["idr", key], ["tab0"])
             return
         if k == 3:
             send([(3, codes("ld3", 0, CP + 2), codes("qd", 384, 386 + CP), eng[3])], "ar%d", ["qd3"])
             send([(3, T.ld3s[:, 0:CP + 2], T.qds[:, 384:386 + CP], eng[3])], "ar%d", ["qd3"])
         for c in (0, 1):
-            mm(ps[:, x:x + 128], "qo", 128 * k, "cq", 4 * c, 128, c == 0, c == 1, ["qo%d" % k, "cq"], [key])
-        cp(T.lo[:, 8 * k:8 * k + 3], ps[:, x:x + 3], [key], ["lo%d" % k])
+            mm(key, "qo", 128 * k, "cq", 4 * c, 128, c == 0, c == 1, ["qo%d" % k, "cq"])
+        cp(T.lo[:, 8 * k:8 * k + 3], (key, 0, 3), [key], ["lo%d" % k])
         if k < 3:
-            pick("nq", 176 * k - 176, CR, "qd", 128 * k, 128 * k + 128, T.lo[:, 8 * k:8 * k + 3],
+            pick("nq", 192 * k - 192, CR, "qd", 128 * k, 128 * k + 128, T.lo[:, 8 * k:8 * k + 3],
                  ["qd%d" % k, "lo%d" % k], "sd%d" % k)
 
     fill(T.tab[:, 0:384], 0.0, ["tab0", "tab2", "tab3"])
     fill(T.tab[:, 384:512], float(CR), ["tab1"])
-    for k in [int(c) for c in OPT["seq"]]:
-        stage1(k, OPT["bank"][k])
-        stage2(k, OPT["bank"][k])
-        stage3(k, OPT["bank"][k])
-    at = {1: (0, 0, 0, 0), 2: (176, 66, 128, 174)}
+    for k in range(4):
+        stage1(k)
+        stage2(k)
+        stage3(k)
     for w in OPT["back"].split():
         to = [int(c) for c in w[1:]]
         es = share(to)
         if w[0] == "l":
             send([(j, T.ll[:, 8 * j:8 * j + 3], T.lo[:, 8 * j:8 * j + 3], es[j]) for j in to], "al%d", ["lo%d" % j for j in to])
-        elif w[0] == "t":
-            k = to[0]
-            c, h, z, _y = at[k]
-            send([(k, codes("ld%d" % k, h, h + 24), codes("nq", c, c + 24), eng[k][0:2]),
-                  (k, codes("ld%d" % k, h + 24, h + 48), codes("nq", c + 24, c + 48), eng[k][2:4]),
-                  (k, T["ld%ds" % k][:, h + z - c:h + z - c + 96], T.nqs[:, z:z + 96], eng[k][4:8])], "ar%d",
-                 ["sd%d" % k, "sd%ds" % k, "nq"])
-        elif w[0] == "c":
-            send([(k, codes("ld%d" % k, at[k][1], at[k][1] + CR), codes("nq", at[k][0], at[k][0] + CR), es[k]) for k in to],
-                 "ar%d", ["sd%d" % k for k in to])
+        elif w[0] == "u":
+            send([(1, codes("ld1", 12 * i, 12 * i + 12), codes("nq", 12 * i, 12 * i + 12), near_eng[2 * i:2 * i + 2])
+                  for i in range(4)] + [(1, T.ld1s[:, 0:CR], T.nqs[:, 0:CR], out_eng)], "ar%d", ["sd1", "sd1s"])
         else:
-            send([(k, T["ld%ds" % k][:, 64 * k - 64:64 * k - 14], T.nqs[:, at[k][3]:at[k][3] + 50], es[k]) for k in to],
-                 "ar%d", ["nq"] + ["sd%ds" % k for k in to])
+            send([(2, codes("ld2", 161, 209), codes("nq", 192, 240), eng[2][0:4]),
+                  (2, T.ld2s[:, 17:209], T.nqs[:, 48:240], eng[2][4:8])], "ar%d", ["sd2", "sd2s", "nq"])
     for k in (1, 2, 3):
         arrive("al%d" % k, ["ll%d" % k])
         arrive("ar%d" % k, ["ld%d" % k])
@@ -418,7 +415,7 @@ def rank_program(g, core, T, topo):
         s, s1 = slice(192 * k, 192 * k + 192), slice(768 + 192 * k, 960 + 192 * k)
         lst, g1 = T.ll[:, 8 * k:8 * k + 3], T.gg[:, 768 + 192 * k:960 + 192 * k:16]
         if k in (1, 2):
-            cp(tab.indirect(lst), T.vals[:, 2 * k - 2:2 * k - 2 + CR], ["vals", "ll%d" % k], ["tab%d" % k])
+            cp(tab.indirect(lst), T.vals[:, k - 1:k - 1 + CR], ["vals", "ll%d" % k], ["tab%d" % k])
         elif k:
             cp(tab.indirect(lst), T.ot[:, 448:448 + CR], ["oneb", "ll3"], ["tab3"])
             act(T.gid[:, :], T.idr[:, :].indirect(offt), F.Copy, ["idr"] + ko, ["gid"])
@@ -429,7 +426,7 @@ def rank_program(g, core, T, topo):
         turn(T.gg[:, s1], T.gg[:, s], ["gr0%d" % k], ["gr1%d" % k])
         if k in (1, 2):
             cp(of, g1, ["gr1%d" % k], ["hof%d" % k])
-            pick(zc, 0, NT, "ld%d" % k, 64 * k - 64, 64 * k - 14, of, ["hof%d" % k, "ld%d" % k, "ldz"], zc)
+            pick(zc, 0, NT, "ld%d" % k, 160 * k - 160, 160 * k - 111, of, ["hof%d" % k, "ld%d" % k, "ldz"], zc)
         else:
             ts(of, g1, 0.0, float(CP), A.min, A.add, ["gr1%d" % k], ["hof%d" % k])
             if k:
@@ -437,14 +434,13 @@ def rank_program(g, core, T, topo):
             else:
                 pick(zc, 0, NT, "qd", 0, 128, of, ["hof0", "qd0"], zc)
         for b in range(4):
-            ps, x, key = bank(OPT["sum"], b)
-            mm(ps[:, x:x + NT], "eq", 128 * b, zc, 0, NT, first, last, ["eq%d" % b, zc, zc + "s"], [key])
+            mm("*z%d" % b, "eq", 128 * b, zc, 0, NT, first, last, ["eq%d" % b, zc, zc + "s"])
 
     for i, k in enumerate([int(c) for c in OPT["seq"]]):
         home(k, i == 0, i == 3)
     ts(T.ff[:, 0:24], T.hof[:, 0:24], CP - 0.5, None, A.is_lt, None, ["hof0", "hof3"], ["fl0"])
     ts(T.ff[:, 24:36], T.hof[:, 24:36], CR - 0.5, None, A.is_lt, None, ["hof1"], ["fl1"])
-    ts(T.ff[:, 36:48], T.hof[:, 36:48], 1.0, None, A.is_gt, None, ["hof2"], ["fl2"])
+    ts(T.ff[:, 36:48], T.hof[:, 36:48], 0.5, None, A.is_gt, None, ["hof2"], ["fl2"])
     tt(T.ff[:, 48:96], T.ff[:, 0:48], T.wgt[:, :], A.mult,
        ["fl0", "fl1", "fl2"] + ["wgt%d%d" % (k, h) for k in range(4) for h in (0, 1)], ["fw"])
     tt(T.ff[:, 96:120], T.ff[:, 48:72], T.ff[:, 72:96], A.add, ["fw"], ["fs"])
@@ -453,15 +449,14 @@ def rank_program(g, core, T, topo):
     turn(T.cst[0:32, :], T.cs[0:32, :], ["cs", "csz"], ["cst"])
 
     for b in range(4):
-        ps, x, key = bank(OPT["sum"], b)
+        key = "*z%d" % b
         if b % 2:
-            cp(T.zt[:, b:768:4], ps[:, x:x + NT], [key], ["zt%d" % b])
+            cp(T.zt[:, b:768:4], (key, 0, NT), [key], ["zt%d" % b])
         else:
-            act(T.zt[:, b:768:4], ps[:, x:x + NT], F.Copy, [key], ["zt%d" % b])
+            act(T.zt[:, b:768:4], (key, 0, NT), F.Copy, [key], ["zt%d" % b])
     quant("zq", 0, 192, "zt", 0, 768, ["zt0", "zt1", "zt2", "zt3"], ["zq"])
-    ps, x, key = bank("zx".replace(OPT["sum"], ""), 0)
-    mm(ps[:, 0:NT], "vq", 0, "zq", 0, NT, True, True, ["vq", "zq"], [key])
-    cp(T.ysb[:, :], ps[:, 0:NT], [key], ["ysb"])
+    mm("*y", "vq", 0, "zq", 0, NT, True, True, ["vq", "zq"])
+    cp(T.ysb[:, :], ("*y", 0, NT), ["*y"], ["ysb"])
     dma("Y", "doy", T.ct[0:1, 0:NT], T.cst[0:6, 0:32], ["cst"], [])
     dma("Y", "doy", T.oc[:, 0:768], T.zq[:, 0:NT].bitcast(dt.uint8), ["zq"], [])
     for i in range(4):
@@ -470,7 +465,11 @@ def rank_program(g, core, T, topo):
     dma("Y", "doy", T.y[:, :], T.ysb[:, :], ["ysb"], [])
 
     order = [int(w) for w in ORDER.split()] or range(len(tasks))
-    waited, token = {}, {}
+    waited, token, users, idle = {}, {}, {}, [(i, []) for i in range(8)]
+    for i, t in enumerate(tasks):
+        for k in t["use"]:
+            users.setdefault(k, []).append(i)
+    todo = {k: len(v) for k, v in users.items()}
 
     def need(q, tok):
         if waited.get((q, tok[0]), 0) < tok[1]:
@@ -482,6 +481,13 @@ def rank_program(g, core, T, topo):
         if t["q"] is None:
             token[i] = (t["sem"], t["inc"])
             continue
+        for k in t["use"]:
+            if k not in place:
+                place[k], old = idle.pop(0)
+                t["before"].update({j: True for j in old})
+            todo[k] -= 1
+            if not todo[k]:
+                idle.append((place[k], [j for j in users[k] if tasks[j]["q"] != "P"]))
         best = {}
         for j, full in t["before"].items():
             if full:

@@ -5,22 +5,22 @@ NT, CP, CR = 192, 112, 48
 EPS = 2.0 ** -120
 BELOW = 1.0 - 2.0 ** -24
 WHOLE = 1.5 * 2.0 ** 23
-OPT = {"ns": 9, "out": "c13 s13 c2 s2", "back": "l13 l2 u1 w2", "mv": "3322", "seq": "0312"}
-ORDER = "6 27 10 29 28 0 151 7 16 145 35 33 15 144 13 12 26 31 20 11 1 2 3 4 5 147 129 141 14 48 44 46 36 17 18 149 19 47 49 45 344 50 51 52 53 139 21 25 24 40 146 128 22 127 8 32 43 34 113 30 116 54 37 55 114 88 130 56 132 23 143 133 57 135 58 38 74 72 73 68 71 70 69 81 78 79 77 80 76 75 334 84 83 87 65 61 67 63 60 62 59 66 64 82 39 333 85 86 336 97 91 89 99 138 90 102 98 104 100 125 92 94 101 358 339 117 134 103 137 96 118 41 157 152 158 341 162 163 153 9 115 93 95 169 167 337 346 120 155 165 164 168 160 166 356 123 159 170 154 122 161 156 124 136 171 183 352 140 340 105 106 109 185 142 186 335 126 172 173 174 176 107 119 342 179 131 350 175 184 180 195 190 200 108 150 338 343 148 177 353 111 196 284 359 347 357 355 289 201 349 279 293 361 285 280 286 191 281 290 294 291 292 287 202 295 42 282 288 203 207 205 198 193 296 197 192 283 204 297 298 372 206 299 300 301 302 313 315 314 316 309 310 199 194 311 110 112 208 345 209 312 210 211 303 178 304 249 317 212 245 306 305 240 251 213 307 214 235 247 243 215 308 216 250 246 241 236 218 217 219 252 248 242 318 244 237 223 227 238 320 225 321 239 220 322 253 221 230 231 224 228 226 232 222 229 233 254 256 255 257 188 258 360 348 319 269 267 181 189 259 260 263 262 261 234 182 265 264 362 271 272 270 268 266 354 274 187 363 364 275 332 276 273 351 277 365 278 323 331 327 382 371 383 366 325 328 324 329 373 326 374 384 375 402 385 376 377 368 392 393 403 121 387 370 367 381 379 369 380 378 386 389 391 390 388 330 394 395 397 404 396 405 406 407 399 411 408 400 401 413 409 417 412 398 410 414 415 419 418 422 420 421 416 423"
+OPT = {"ns": 9, "out": "c13 s123 c2", "back": "l13 w13 l2 w2", "mv": "3322", "seq": "0312"}
+ORDER = "0 158 27 13 7 12 157 18 17 14 8 15 154 137 24 22 1 2 3 4 5 6 26 9 16 20 19 35 46 48 50 21 47 49 51 52 29 53 370 23 146 152 25 61 28 30 159 160 54 55 36 56 32 31 10 62 63 142 37 64 57 58 65 141 98 59 66 67 68 33 69 353 84 85 80 83 82 81 87 79 90 88 89 91 92 86 151 60 38 34 71 77 73 78 76 70 45 72 75 74 155 93 42 43 44 95 94 343 96 342 97 344 107 101 109 99 348 113 346 111 349 345 148 110 100 132 104 350 347 124 125 106 102 108 153 112 367 126 127 351 105 103 352 114 131 139 166 156 363 11 167 147 369 171 178 161 168 355 172 173 149 123 176 177 362 129 169 358 128 174 122 133 134 164 175 143 135 361 170 366 39 115 116 118 162 163 199 165 136 138 354 140 179 150 144 364 360 200 204 214 117 209 180 368 216 207 202 212 205 40 359 215 145 120 288 302 210 201 119 206 211 217 203 208 213 300 298 293 304 296 291 121 303 218 299 305 219 301 41 289 290 292 294 295 297 220 236 234 182 221 232 244 258 222 223 356 235 184 254 306 307 308 245 247 237 246 309 256 224 225 249 310 259 255 227 228 226 318 320 322 248 257 311 312 250 252 260 251 323 324 321 181 229 319 233 183 325 313 253 261 316 315 314 239 240 230 262 263 185 317 327 328 326 241 186 231 264 365 357 329 278 265 274 276 238 332 187 267 266 190 280 197 243 268 192 242 331 269 330 272 271 270 198 273 130 279 275 277 281 188 283 284 194 282 285 191 340 336 371 287 372 286 195 193 373 410 189 390 391 196 380 374 392 393 381 382 383 375 376 377 333 334 335 411 378 379 341 384 385 337 395 338 339 400 394 389 387 397 399 386 396 388 398 401 402 403 405 412 404 413 414 415 409 408 407 421 419 420 416 417 425 406 418 422 427 426 430 428 429 423 424 431"
 TAB = {0: 0, 2: 1, 3: 2, 1: 3}
-POS = {0: 0, 3: 1, 1: 2, 2: 3}
+RUN = {1: (0, 0, 0, 0), 3: (192, 162, 48, 18), 2: (384, 162, 240, 18)}
 
 SCRATCH = {
-    "xt": ("sbuf", [128, 776], "bfloat16"), "gt": ("sbuf", [128, 776], "bfloat16"),
+    "xt": ("sbuf", [128, 1024], "bfloat16"), "gt": ("sbuf", [128, 776], "bfloat16"),
     "rtt": ("sbuf", [128, 16], "bfloat16"), "prt": ("sbuf", [128, 16], "bfloat16"), "nt": ("sbuf", [128, 576], "bfloat16"),
     "wt": ("sbuf", [128, 2048], "bfloat16"), "ut": ("sbuf", [128, 2048], "bfloat16"), "ppt": ("sbuf", [128, 512], "bfloat16"),
     "vt": ("sbuf", [128, 512], "bfloat16"), "et": ("sbuf", [128, 516], "bfloat16"), "wnt": ("sbuf", [128, 512], "bfloat16"),
     "pt": ("sbuf", [128, 528], "bfloat16"), "zt": ("sbuf", [128, 768], "bfloat16"),
     "fi": ("sbuf", [128, 256], "float32"), "own": ("sbuf", [128, 256], "float32"), "pf": ("sbuf", [128, 24], "float32"),
     "sb": ("sbuf", [128, 16], "float32"), "rct": ("sbuf", [128, 1088], "bfloat16"), "ex": ("sbuf", [128, 384], "bfloat16"),
-    "bt": ("sbuf", [128, 768], "bfloat16"), "rx": ("sbuf", [128, 896], "bfloat16"),
+    "bt": ("sbuf", [128, 1024], "bfloat16"), "rx": ("sbuf", [128, 896], "bfloat16"),
     "tri0": ("sbuf", [128, 112], "float32"), "tri": ("sbuf", [128, 112], "float32"),
-    "idr": ("sbuf", [128, 128], "bfloat16"), "gid": ("sbuf", [128, 192], "bfloat16"),
+    "idr": ("sbuf", [128, 128], "bfloat16"),
     "vals": ("sbuf", [128, 50], "bfloat16"), "k4": ("sbuf", [128, 384], "bfloat16"),
     "win": ("sbuf", [128, 192], "bfloat16"), "m": ("sbuf", [128, 200], "bfloat16"), "pref": ("sbuf", [128, 192], "bfloat16"),
     "le": ("sbuf", [128, 192 * 26], "bfloat16"),
@@ -35,8 +35,8 @@ SCRATCH = {
     "ca": ("sbuf", [128, 16], "float32"),
     "pz": ("psum", [128, 2048], "float32"), "px": ("psum", [128, 2048], "float32"),
 }
-_CODES = [("xq", 194), ("gq", 194), ("rq", 272), ("bq", 192), ("pp", 128), ("wq", 512), ("uq", 512), ("wn", 128),
-          ("vq", 128), ("eq", 512), ("cq", 132), ("zq", 192), ("qm", 512), ("qd", 512), ("qo", 512), ("nq", 240)]
+_CODES = [("xq", 256), ("gq", 194), ("rq", 272), ("bq", 256), ("pp", 128), ("wq", 512), ("uq", 512), ("wn", 128),
+          ("vq", 128), ("eq", 512), ("cq", 132), ("zq", 192), ("qm", 512), ("qd", 512), ("qo", 512), ("nq", 432)]
 for _k in range(4):
     _CODES += [("lc%d" % _k, 224), ("zc%d" % _k, 192)]
     if _k:
@@ -45,7 +45,7 @@ for _n, _w in _CODES:
     SCRATCH[_n] = ("sbuf", [128, _w], "float8_e4m3fn_x4")
     SCRATCH[_n + "s"] = ("sbuf", [128, _w], "uint8")
 
-SEMAPHORES = ["cV", "cS", "cP", "cG", "dx", "dgr", "drt", "dpr", "dw", "dub", "dv", "doy", "dos", "left", "az"]
+SEMAPHORES = ["cV", "cS", "cP", "cG", "dx", "dy", "dgr", "drt", "dpr", "dw", "dub", "dv", "doy", "dos", "left", "az"]
 for _k in (1, 2, 3):
     SEMAPHORES += ["ax%d" % _k, "al%d" % _k, "ar%d" % _k]
 
@@ -177,16 +177,18 @@ def rank_program(g, core, T, topo):
         return T[name][:, a:b].bitcast(dt.uint8)
 
     dma("S", "drt", T.rtt[:, 0:16], T.rt[:, 0:16], [], ["rtt"])
-    dma("Y", "dx", T.xt[:, 0:768], T.x[:, :], [], ["xt"])
+    dma("Y", "dx", T.xt[:, 0:512], T.x[:, 0:512], [], ["xt0"])
+    dma("Y", "dy", T.xt[:, 512:768], T.x[:, 512:768], [], ["xt1"])
     dma("Y", "dgr", T.gt[:, 0:768], T.gr[:, :], [], ["gt"])
     dma("Y", "dw", T.wt[:, :], T.w[:, :], [], ["wt"])
     dma("Y", "dpr", T.prt[:, 0:8], T.pr[:, 0:8], [], ["prt"])
     dma("Y", "dub", T.ut[:, :], T.ub[:, :], [], ["ut"])
 
     fill(T.nt[:, :], 0.0, ["nt"])
-    quant("nq", 48, 192, "nt", 0, 576, ["nt"], ["nq"])
-    send([(2, codes("ld2", 160, 161), codes("nq", 191, 192), eng[2]), (1, codes("ld1", 48, 49), codes("nq", 48, 49), eng[1][0:4]),
-          (1, T.ld1s[:, 48:52], T.nqs[:, 48:52], eng[1][4:8])], "az", ["nq"])
+    quant("nq", 48, 192, "nt", 0, 576, ["nt"], ["nqa"])
+    quant("nq", 240, 384, "nt", 0, 576, ["nt"], ["nqb"])
+    send([(k, codes("ld%d" % k, z, z + 2), codes("nq", c, c + 2), half[k])
+          for k, z, c in ((1, 48, 48), (3, 160, 190), (2, 160, 382))], "az", ["nqa", "nqb"])
     arrive("az", ["ldz"])
 
     def pf(i):
@@ -203,9 +205,9 @@ def rank_program(g, core, T, topo):
     ts(T.ex[:, 128:256], T.ex[:, 0:128], LO, None, A.is_equal, None, ["ex", "owa"], ["ex1"])
     ts(T.ex[:, 256:384], T.ex[:, 0:128], HI, None, A.is_equal, None, ["ex", "owa"], ["ex2"])
     tt(T.rct[:, 0:508:4], T.ex[:, 128:255], T.ex[:, 256:383], A.subtract, ["ex1", "ex2", "rcy", "rcz"], ["rc0"])
-    clear(T.xt[:, 768:776], "xz")
-    clear(T.bt[:, 0:384], "bz0")
-    clear(T.bt[:, 384:768], "bz1")
+    clear(T.xt[:, 768:1024], "xz")
+    clear(T.bt[:, 0:512], "bz0")
+    clear(T.bt[:, 512:1024], "bz1")
     clear(T.m[:, 0:2], "mz")
     for i, (pattern, base, ch) in enumerate([([[0, 4], [-2, 8]], 0, 0), ([[0, 2], [7, 8], [3, 2]], NT // 2, 0),
                                              ([[0, 2], [1, 16]], 0, 0), ([[1, 2], [0, 16]], 0, 0),
@@ -232,14 +234,17 @@ def rank_program(g, core, T, topo):
         act(T.rct[:, 504 + c:504 + c + n], T.rtt[:, 4 * d:16], F.Copy, ["rtt", "rcz"], ["rb%d" % d], scale=-1.0)
         cp(T.rct[:, 576 + c:576 + c + n], T.rtt[:, 0:n], ["rtt", "rcz"], ["rc%d" % d])
     quant("rq", 0, 272, "rct", 0, 1088, ["rc0"] + [n % d for n in ("rb%d", "rc%d") for d in (1, 2, 3)], ["rq"])
-    quant("xq", 0, 194, "xt", 0, 776, ["xt", "xz"], ["xq"])
-    mm("*d", "rq", 144, "xq", 0, NT, True, False, ["rq", "xq"])
-    mm("*d", "rq", 126, "xq", 0, NT, False, True, ["rq", "xq"])
-    ts(T.bt[:, 0:768:4], ("*d", 0, NT), 0.0, None, A.is_ge, None, ["*d", "bz0", "bz1"], ["bt"])
-    quant("bq", 0, NT, "bt", 0, 768, ["bt"], ["bq"])
-    mm("*w", "rq", 0, "bq", 0, NT, True, True, ["rq", "bq"])
-    ts(T.m[:, 2:2 + NT], ("*w", 0, NT), 2.5, None, A.is_gt, None, ["*w"], ["m"])
-    scan(T.pref[:, :], T.m[:, 2:2 + NT], T.m[:, 1:1 + NT], ["m", "mz", "owc"], ["pref"], M7)
+    for h, n in ((0, 128), (1, NT - 128)):
+        c, d, w = 128 * h, "*d%d" % h, "*w%d" % h
+        quant("xq", c, c + 128, "xt", 4 * c, 4 * c + 512, ["xt%d" % h, "xz"], ["xq%d" % h])
+        mm(d, "rq", 144, "xq", c, 128, True, False, ["rq", "xq%d" % h])
+        mm(d, "rq", 126, "xq", c, 128, False, True, ["rq", "xq%d" % h])
+        ts(T.bt[:, 4 * c:4 * (c + n):4], (d, 0, n), 0.0, None, A.is_ge, None, [d, "bz%d" % h], ["bt%d" % h])
+        quant("bq", c, c + 128, "bt", 4 * c, 4 * c + 512, ["bt%d" % h], ["bq%d" % h])
+        mm(w, "rq", 0, "bq", c, 128, True, True, ["rq", "bq%d" % h])
+        ts(T.m[:, 2 + c:2 + c + n], (w, 0, n), 2.5, None, A.is_gt, None, [w], ["m%d" % h])
+        act(T.win[:, c:c + n], (w, 0, n), F.Copy, [w], ["win%d" % h])
+    scan(T.pref[:, :], T.m[:, 2:2 + NT], T.m[:, 1:1 + NT], ["m0", "m1", "mz", "owc"], ["pref"], M7)
 
     def piece(i, t):
         return T.le[:, NT * i + 7 * t:NT * i + NT]
@@ -259,12 +264,11 @@ def rank_program(g, core, T, topo):
         cp(T.cn[:, c + NS:c + 16], last, ["ls%d" % t for t in range(NS, 16)], ["cnl%d" % c])
     turn(T.cnt[:, :], T.cn[:, :], mine + ["cnd", "cnl0", "cnl16"], ["cnt"])
     ts(T.off[:, :], T.cnt[:, :], BASE, None, A.add, None, ["cnt", "owc"], ["off"])
-    act(T.win[:, :], ("*w", 0, NT), F.Copy, ["*w"], ["win"])
     quant("gq", 0, 194, "gt", 0, 776, ["gt", "gz"], ["gq"])
 
     for k in (1, 2, 3, 0):
         d, o = ("sc%d" if k else "lc%d") % k, T.off[:, 8 * (rank ^ k):8 * (rank ^ k) + 7]
-        pick(d, CP, CP, "xq", 0, 194, o, ["xq", "off"], d + "x")
+        pick(d, CP, CP, "xq", 0, 194, o, ["xq0", "xq1", "off"], d + "x")
         pick(d, 0, CP, "gq", 0, 194, o, ["gq", "off"], d + "g")
     for w in OPT["out"].split():
         to = [int(c) for c in w[1:]]
@@ -356,15 +360,10 @@ def rank_program(g, core, T, topo):
             mm(key, "wn", 0, "qo", 0, 128, True, True, ["qo0", "wn"])
             tt(T.tab[:, 0:CP], T.idr[:, 0:CP], (key, 0, CP), A.max, ["idr", key], ["tab0"])
             return
-        if k == 3:
-            send([(3, codes("ld3", 0, CP + 2), codes("qd", 384, 386 + CP), eng[3])], "ar%d", ["qd3"])
-            send([(3, T.ld3s[:, 0:CP + 2], T.qds[:, 384:386 + CP], eng[3])], "ar%d", ["qd3"])
         for c in (0, 1):
             mm(key, "qo", 128 * k, "cq", 4 * c, 128, c == 0, c == 1, ["qo%d" % k, "cq"])
         cp(T.lo[:, 8 * k:8 * k + 3], (key, 0, 3), [key], ["lo%d" % k])
-        if k < 3:
-            pick("nq", 192 * k - 192, CR, "qd", 128 * k, 128 * k + 128, T.lo[:, 8 * k:8 * k + 3],
-                 ["qd%d" % k, "lo%d" % k], "sd%d" % k)
+        pick("nq", RUN[k][0], CR, "qd", 128 * k, 128 * k + 128, T.lo[:, 8 * k:8 * k + 3], ["qd%d" % k, "lo%d" % k], "sd%d" % k)
 
     fill(T.tab[:, 0:384], 0.0, ["tab0", "tab2", "tab3"])
     fill(T.tab[:, 384:512], float(CR), ["tab1"])
@@ -377,18 +376,20 @@ def rank_program(g, core, T, topo):
         es = share(to)
         if w[0] == "l":
             send([(j, T.ll[:, 8 * j:8 * j + 3], T.lo[:, 8 * j:8 * j + 3], es[j]) for j in to], "al%d", ["lo%d" % j for j in to])
-        elif w[0] == "u":
-            send([(1, codes("ld1", 12 * i, 12 * i + 12), codes("nq", 12 * i, 12 * i + 12), near_eng[2 * i:2 * i + 2])
-                  for i in range(4)] + [(1, T.ld1s[:, 0:CR], T.nqs[:, 0:CR], out_eng)], "ar%d", ["sd1", "sd1s"])
-        else:
-            send([(2, codes("ld2", 161, 209), codes("nq", 192, 240), eng[2][0:4]),
-                  (2, T.ld2s[:, 17:209], T.nqs[:, 48:240], eng[2][4:8])], "ar%d", ["sd2", "sd2s", "nq"])
+            continue
+        parts = []
+        for k in to:
+            c, h, z, y = RUN[k]
+            n = len(es[k]) // 2
+            parts += [(k, codes("ld%d" % k, h, h + CR), codes("nq", c, c + CR), es[k][0:n]),
+                      (k, T["ld%ds" % k][:, y:y + NT], T.nqs[:, z:z + NT], es[k][n:])]
+        send(parts, "ar%d", ["nqa", "nqb"] + ["sd%d%s" % (k, x) for k in to for x in ("", "s")])
     for k in (1, 2, 3):
         arrive("al%d" % k, ["ll%d" % k])
         arrive("ar%d" % k, ["ld%d" % k])
 
     h1, h2, h3, h4, h5, h6, h7, h8, h9 = (T.hh[:, 24 * i:24 * i + 24] for i in range(9))
-    turn(T.tv[:, 0:NT], T.win[:, :], ["win"], ["tw"])
+    turn(T.tv[:, 0:NT], T.win[:, :], ["win0", "win1"], ["tw"])
     turn(T.tv[:, NT:2 * NT], T.pref[:, :], ["pref"], ["tp"])
     tw, tp = T.tv[:, 0:NT:8], T.tv[:, NT + 3:2 * NT:8]
     ts(h1, tw, 2.5, 2.0 * CP + 2, A.is_gt, A.mult, ["tw"], ["h1"])
@@ -404,43 +405,35 @@ def rank_program(g, core, T, topo):
     for k in (0, 1, 2, 3):
         e = rank ^ k
         for h in (0, 1):
-            o, p = slice(12 * POS[k] + h, 12 * POS[k] + 12, 2), (pf(10), ODD)[h]
+            o, p = slice(12 * k + h, 12 * k + 12, 2), (pf(10), ODD)[h]
             ts(T.offt[:, o], T.hh[:, 96 + e:120:4], float(CP), None, A.add, None, ["h5"], ["offt%d%d" % (k, h)])
             act(T.wgt[:, o], T.hh[:, 120 + e:144:4], F.Copy, ["h6", "owb", "pf10"], ["wgt%d%d" % (k, h)], scale=p)
     fill(T.cs[:, :], 0.0, ["csz"])
 
     def home(k, first, last):
-        tab, zc, q = T.tab[:, 128 * TAB[k]:128 * TAB[k] + 128], "zc%d" % k, 12 * POS[k]
+        tab, zc, q = T.tab[:, 128 * TAB[k]:128 * TAB[k] + 128], "zc%d" % k, 12 * k
         offt, of, ko = T.offt[:, q:q + 12], T.hof[:, q:q + 12], ["offt%d0" % k, "offt%d1" % k]
         s, s1 = slice(192 * k, 192 * k + 192), slice(768 + 192 * k, 960 + 192 * k)
         lst, g1 = T.ll[:, 8 * k:8 * k + 3], T.gg[:, 768 + 192 * k:960 + 192 * k:16]
-        if k in (1, 2):
-            cp(tab.indirect(lst), T.vals[:, k - 1:k - 1 + CR], ["vals", "ll%d" % k], ["tab%d" % k])
-        elif k:
-            cp(tab.indirect(lst), T.ot[:, 448:448 + CR], ["oneb", "ll3"], ["tab3"])
-            act(T.gid[:, :], T.idr[:, :].indirect(offt), F.Copy, ["idr"] + ko, ["gid"])
-        if k == 3:
-            tt(T.gg[:, s], tab.indirect(offt), T.gid[:, :], A.mult, ["tab3", "gid"] + ko, ["gr03"])
-        else:
-            act(T.gg[:, s], tab.indirect(offt), F.Copy, ["tab%d" % k] + ko, ["gr0%d" % k])
+        if k:
+            d = 2 if RUN[k][1] else 0
+            cp(tab.indirect(lst), T.vals[:, d:d + CR], ["vals", "ll%d" % k], ["tab%d" % k])
+        act(T.gg[:, s], tab.indirect(offt), F.Copy, ["tab%d" % k] + ko, ["gr0%d" % k])
         turn(T.gg[:, s1], T.gg[:, s], ["gr0%d" % k], ["gr1%d" % k])
-        if k in (1, 2):
+        if k:
             cp(of, g1, ["gr1%d" % k], ["hof%d" % k])
-            pick(zc, 0, NT, "ld%d" % k, 160 * k - 160, 160 * k - 111, of, ["hof%d" % k, "ld%d" % k, "ldz"], zc)
+            pick(zc, 0, NT, "ld%d" % k, RUN[k][1] - d, RUN[k][1] - d + 50, of, ["hof%d" % k, "ld%d" % k, "ldz"], zc)
         else:
-            ts(of, g1, 0.0, float(CP), A.min, A.add, ["gr1%d" % k], ["hof%d" % k])
-            if k:
-                pick(zc, 0, NT, "ld3", 0, CP + 2, of, ["hof3", "ld3"], zc)
-            else:
-                pick(zc, 0, NT, "qd", 0, 128, of, ["hof0", "qd0"], zc)
+            ts(of, g1, 0.0, float(CP), A.min, A.add, ["gr10"], ["hof0"])
+            pick(zc, 0, NT, "qd", 0, 128, of, ["hof0", "qd0"], zc)
         for b in range(4):
             mm("*z%d" % b, "eq", 128 * b, zc, 0, NT, first, last, ["eq%d" % b, zc, zc + "s"])
 
     for i, k in enumerate([int(c) for c in OPT["seq"]]):
         home(k, i == 0, i == 3)
-    ts(T.ff[:, 0:24], T.hof[:, 0:24], CP - 0.5, None, A.is_lt, None, ["hof0", "hof3"], ["fl0"])
-    ts(T.ff[:, 24:36], T.hof[:, 24:36], CR - 0.5, None, A.is_lt, None, ["hof1"], ["fl1"])
-    ts(T.ff[:, 36:48], T.hof[:, 36:48], 0.5, None, A.is_gt, None, ["hof2"], ["fl2"])
+    ts(T.ff[:, 0:12], T.hof[:, 0:12], CP - 0.5, None, A.is_lt, None, ["hof0"], ["fl0"])
+    ts(T.ff[:, 12:24], T.hof[:, 12:24], CR - 0.5, None, A.is_lt, None, ["hof1"], ["fl1"])
+    ts(T.ff[:, 24:48], T.hof[:, 24:48], 1.0, None, A.is_gt, None, ["hof2", "hof3"], ["fl2"])
     tt(T.ff[:, 48:96], T.ff[:, 0:48], T.wgt[:, :], A.mult,
        ["fl0", "fl1", "fl2"] + ["wgt%d%d" % (k, h) for k in range(4) for h in (0, 1)], ["fw"])
     tt(T.ff[:, 96:120], T.ff[:, 48:72], T.ff[:, 72:96], A.add, ["fw"], ["fs"])

from concourse.bass import DstId, RemoteDMATransfer
from concourse.mybir import dt, AluOpType as A, ActivationFunctionType as F

NT, CP, CR = 192, 112, 48
EPS = 2.0 ** -120
BELOW = 1.0 - 2.0 ** -24
WHOLE = 1.5 * 2.0 ** 23
OPT = {"ns": 9, "out": "c13 s123 c2", "back": "l13 w13 l2 w2", "mv": "3322", "seq": "0312"}
ORDER = "0 158 27 13 7 12 157 18 17 14 8 15 154 137 24 22 1 2 3 4 5 6 26 9 16 20 19 35 46 48 50 21 47 49 51 52 29 53 370 23 146 152 25 61 28 30 159 160 54 55 36 56 32 31 10 62 63 142 37 64 57 58 65 141 98 59 66 67 68 33 69 353 84 85 80 83 82 81 87 79 90 88 89 91 92 86 151 60 38 34 71 77 73 78 76 70 45 72 75 74 155 93 42 43 44 95 94 343 96 342 97 344 107 101 109 99 348 113 346 111 349 345 148 110 100 132 104 350 347 124 125 106 102 108 153 112 367 126 127 351 105 103 352 114 131 139 166 156 363 11 167 147 369 171 178 161 168 355 172 173 149 123 176 177 362 129 169 358 128 174 122 133 134 164 175 143 135 361 170 366 39 115 116 118 162 163 199 165 136 138 354 140 179 150 144 364 360 200 204 214 117 209 180 368 216 207 202 212 205 40 359 215 145 120 288 302 210 201 119 206 211 217 203 208 213 300 298 293 304 296 291 121 303 218 299 305 219 301 41 289 290 292 294 295 297 220 236 234 182 221 232 244 258 222 223 356 235 184 254 306 307 308 245 247 237 246 309 256 224 225 249 310 259 255 227 228 226 318 320 322 248 257 311 312 250 252 260 251 323 324 321 181 229 319 233 183 325 313 253 261 316 315 314 239 240 230 262 263 185 317 327 328 326 241 186 231 264 365 357 329 278 265 274 276 238 332 187 267 266 190 280 197 243 268 192 242 331 269 330 272 271 270 198 273 130 279 275 277 281 188 283 284 194 282 285 191 340 336 371 287 372 286 195 193 373 410 189 390 391 196 380 374 392 393 381 382 383 375 376 377 333 334 335 411 378 379 341 384 385 337 395 338 339 400 394 389 387 397 399 386 396 388 398 401 402 403 405 412 404 413 414 415 409 408 407 421 419 420 416 417 425 406 418 422 427 426 430 428 429 423 424 431"
TAB = {0: 0, 2: 1, 3: 2, 1: 3}
RUN = {1: (0, 0, 0, 0), 3: (192, 162, 48, 18), 2: (384, 162, 240, 18)}

SCRATCH = {
    "xt": ("sbuf", [128, 1024], "bfloat16"), "gt": ("sbuf", [128, 776], "bfloat16"),
    "rtt": ("sbuf", [128, 16], "bfloat16"), "prt": ("sbuf", [128, 16], "bfloat16"), "nt": ("sbuf", [128, 576], "bfloat16"),
    "wt": ("sbuf", [128, 2048], "bfloat16"), "ut": ("sbuf", [128, 2048], "bfloat16"), "ppt": ("sbuf", [128, 512], "bfloat16"),
    "vt": ("sbuf", [128, 512], "bfloat16"), "et": ("sbuf", [128, 516], "bfloat16"), "wnt": ("sbuf", [128, 512], "bfloat16"),
    "pt": ("sbuf", [128, 528], "bfloat16"), "zt": ("sbuf", [128, 768], "bfloat16"),
    "fi": ("sbuf", [128, 256], "float32"), "own": ("sbuf", [128, 256], "float32"), "pf": ("sbuf", [128, 24], "float32"),
    "sb": ("sbuf", [128, 16], "float32"), "rct": ("sbuf", [128, 1088], "bfloat16"), "ex": ("sbuf", [128, 384], "bfloat16"),
    "bt": ("sbuf", [128, 1024], "bfloat16"), "rx": ("sbuf", [128, 896], "bfloat16"),
    "tri0": ("sbuf", [128, 112], "float32"), "tri": ("sbuf", [128, 112], "float32"),
    "idr": ("sbuf", [128, 128], "bfloat16"),
    "vals": ("sbuf", [128, 50], "bfloat16"), "k4": ("sbuf", [128, 384], "bfloat16"),
    "win": ("sbuf", [128, 192], "bfloat16"), "m": ("sbuf", [128, 200], "bfloat16"), "pref": ("sbuf", [128, 192], "bfloat16"),
    "le": ("sbuf", [128, 192 * 26], "bfloat16"),
    "cn": ("sbuf", [128, 32], "float32"), "cnt": ("sbuf", [128, 32], "float32"), "off": ("sbuf", [128, 32], "uint16"),
    "tv": ("sbuf", [128, 384], "bfloat16"), "hh": ("sbuf", [128, 240], "float32"),
    "offt": ("sbuf", [128, 48], "uint16"), "wgt": ("sbuf", [128, 48], "float32"),
    "tab": ("sbuf", [128, 512], "bfloat16"), "gg": ("sbuf", [128, 1536], "bfloat16"), "hof": ("sbuf", [128, 48], "uint16"),
    "ff": ("sbuf", [128, 144], "float32"), "cs": ("sbuf", [128, 32], "float32"), "cst": ("sbuf", [128, 32], "float32"),
    "ysb": ("sbuf", [128, 192], "float32"), "ll": ("sbuf", [128, 32], "uint16"), "lo": ("sbuf", [128, 32], "uint16"),
    "mt": ("sbuf", [128, 2048], "bfloat16"), "dxt": ("sbuf", [128, 2048], "bfloat16"), "ot": ("sbuf", [128, 2052], "bfloat16"),
    "sm": ("sbuf", [128, 1792], "bfloat16"), "mk": ("sbuf", [128, 1792], "bfloat16"), "ra": ("sbuf", [128, 896], "float32"),
    "ca": ("sbuf", [128, 16], "float32"),
    "pz": ("psum", [128, 2048], "float32"), "px": ("psum", [128, 2048], "float32"),
}
_CODES = [("xq", 256), ("gq", 194), ("rq", 272), ("bq", 256), ("pp", 128), ("wq", 512), ("uq", 512), ("wn", 128),
          ("vq", 128), ("eq", 512), ("cq", 132), ("zq", 192), ("qm", 512), ("qd", 512), ("qo", 512), ("nq", 432)]
for _k in range(4):
    _CODES += [("lc%d" % _k, 224), ("zc%d" % _k, 192)]
    if _k:
        _CODES += [("sc%d" % _k, 224), ("ld%d" % _k, 224)]
for _n, _w in _CODES:
    SCRATCH[_n] = ("sbuf", [128, _w], "float8_e4m3fn_x4")
    SCRATCH[_n + "s"] = ("sbuf", [128, _w], "uint8")

SEMAPHORES = ["cV", "cS", "cP", "cG", "dx", "dy", "dgr", "drt", "dpr", "dw", "dub", "dv", "doy", "dos", "left", "az"]
for _k in (1, 2, 3):
    SEMAPHORES += ["ax%d" % _k, "al%d" % _k, "ar%d" % _k]


def rank_program(g, core, T, topo):
    rank = T.rank_of(core)
    if rank is None:
        return
    queue = {"V": g.vector, "S": g.scalar, "P": g.tensor, "G": g, "Y": g.sync}
    tasks, wrote, read, total = [], {}, {}, {}
    NS = OPT["ns"]

    def task(q, call, reads, writes, sem=None, inc=1, after=()):
        before = {i: True for i in after}
        for k in reads:
            if k in wrote:
                before[wrote[k]] = True
            if k[0] == "*":
                for i in read.get(k, []):
                    if tasks[i]["q"] != q:
                        before[i] = True
        for k in writes:
            if k in wrote:
                i = wrote[k]
                before[i] = before.get(i, False) or not (q == "P" and tasks[i]["q"] == "P")
            for i in read.get(k, []):
                before[i] = before.get(i, False) or tasks[i]["q"] != q
        n = len(tasks)
        tasks.append({"q": q, "call": call, "before": before, "sem": sem, "inc": inc,
                      "use": [k for k in reads + writes if k[0] == "*"]})
        for k in reads:
            read.setdefault(k, []).append(n)
        for k in writes:
            wrote[k], read[k] = n, []
        return n

    place = {}

    def at(a):
        if not isinstance(a, tuple):
            return a
        i = place[a[0]]
        return (T.pz, T.px)[i // 4][:, 512 * (i % 4) + a[1]:512 * (i % 4) + a[2]]

    def run(q, call, reads, writes):
        return task(q, call, reads, writes, "c" + q)

    def dma(q, sem, out, in_, reads, writes):
        return task(q, lambda e: e.dma_start(out, in_), reads, writes, sem, 16)

    def ts(out, in0, s1, s2, o0, o1, reads, writes):
        if o1 is None:
            run("V", lambda e: e.tensor_scalar(out, at(in0), s1, None, o0), reads, writes)
        else:
            run("V", lambda e: e.tensor_scalar(out, at(in0), s1, s2, o0, o1), reads, writes)

    def tt(out, a, b, op, reads, writes):
        run("V", lambda e: e.tensor_tensor(out, a, at(b), op), reads, writes)

    def scan(out, a, b, reads, writes, start=0.0):
        run("V", lambda e: e.tensor_tensor_scan(out, a, b, start, A.add, A.add), reads, writes)

    def cp(out, a, reads, writes):
        run("V", lambda e: e.tensor_copy(out, at(a)), reads, writes)

    def turn(out, a, reads, writes):
        run("V", lambda e: e.transpose(out, a), reads, writes)

    def fill(ap, v, writes):
        run("V", lambda e: e.memset(ap, v), [], writes)

    def act(out, a, f, reads, writes, **kw):
        run("S", lambda e: e.activation(out, at(a), f, **kw), reads, writes)

    def clear(ap, key):
        act(ap, T.nt[:, 0:ap.shape[1]], F.Copy, ["nt"], [key])

    def quant(q, a, b, tile, c, d, reads, writes):
        o, s, i = T[q][:, a:b], T[q + "s"][:, a:b], T[tile][:, c:d]
        run("V", lambda e: e.quantize_mx(o, s, i), reads, writes)

    def mm(use, l, la, r, ra, n, start, stop, reads):
        w, ws, x, xs = T[l][:, la:la + 128], T[l + "s"][:, la:la + 128], T[r][:, ra:ra + n], T[r + "s"][:, ra:ra + n]
        run("P", lambda e: e.matmul_mx(at((use, 0, n)), w, ws, x, xs, start, stop), reads, [use])

    def pick(dst, c, n, src, a, b, offs, reads, key):
        cp(T[dst][:, c:c + n].bitcast(dt.uint32), T[src][:, a:b].bitcast(dt.uint32).indirect(offs), reads, [key])
        act(T[dst + "s"][:, c:c + n], T[src + "s"][:, a:b].indirect(offs), F.Copy, reads, [key + "s"])

    def iota(out, pattern, base, ch, key):
        run("G", lambda e: e.iota(out, pattern, base, ch, allow_small_or_imprecise_dtypes=True), [], [key])

    peer = [T.cores[rank ^ k] for k in range(4)]
    away = [k for k in (1, 2, 3) if topo.chip(peer[k]) != topo.chip(core)]
    out_eng = topo.engines(core, peer[away[0]])
    near_eng = [e for e in topo.engines(core, peer[1]) if e not in out_eng] or out_eng
    eng = {k: (out_eng if k in away else near_eng) for k in (1, 2, 3)}
    half = {k: (out_eng[4 * away.index(k):4 * away.index(k) + 4] if k in away else near_eng) for k in (1, 2, 3)}
    due = {}

    def send(parts, sem, reads):
        def call(e):
            tr = []
            for k, dst, src, es in parts:
                rid, pid, _s = topo.addr(peer[k])
                tr.append((dst, src, T.sem[sem % k if "%" in sem else sem], rid, pid, sum(1 << x for x in es)))
            if len(tr) == 1:
                dst, src, s, rid, pid, mask = tr[0]
                g.remote_dma(out_ap=dst, in_ap=src, remote_sem=s, local_sem=T.sem["left"], pid=pid, routing_id=rid,
                             dma_engine_mask=mask)
            else:
                g.remote_dma_fused([RemoteDMATransfer(dst_ids=[DstId(rid=rid, pnc=pid)], dma_engine_mask=mask, remote_sem=s,
                                                      srcs=[src], dsts=[dst]) for dst, src, s, rid, pid, mask in tr],
                                   local_sem=T.sem["left"])
        n = task("G", call, reads, [])
        for k, _d, _s, es in parts:
            name = sem % k if "%" in sem else sem
            due.setdefault(name, []).append(n)
            for s in (name, "left"):
                total[s] = total.get(s, 0) + len(es)

    def share(to):
        return half if len([k for k in to if k in away]) > 1 else eng

    def arrive(sem, keys):
        task(None, None, [], keys, sem, total[sem], due[sem])

    def codes(name, a, b):
        return T[name][:, a:b].bitcast(dt.uint8)

    dma("S", "drt", T.rtt[:, 0:16], T.rt[:, 0:16], [], ["rtt"])
    dma("Y", "dx", T.xt[:, 0:512], T.x[:, 0:512], [], ["xt0"])
    dma("Y", "dy", T.xt[:, 512:768], T.x[:, 512:768], [], ["xt1"])
    dma("Y", "dgr", T.gt[:, 0:768], T.gr[:, :], [], ["gt"])
    dma("Y", "dw", T.wt[:, :], T.w[:, :], [], ["wt"])
    dma("Y", "dpr", T.prt[:, 0:8], T.pr[:, 0:8], [], ["prt"])
    dma("Y", "dub", T.ut[:, :], T.ub[:, :], [], ["ut"])

    fill(T.nt[:, :], 0.0, ["nt"])
    quant("nq", 48, 192, "nt", 0, 576, ["nt"], ["nqa"])
    quant("nq", 240, 384, "nt", 0, 576, ["nt"], ["nqb"])
    send([(k, codes("ld%d" % k, z, z + 2), codes("nq", c, c + 2), half[k])
          for k, z, c in ((1, 48, 48), (3, 160, 190), (2, 160, 382))], "az", ["nqa", "nqb"])
    arrive("az", ["ldz"])

    def pf(i):
        return T.pf[:, i:i + 1]

    LO, HI, M7, BASE, P15, ODD, HIGH, ENT = (T.own[:, 32 * i:32 * i + 1] for i in range(8))
    fill(T.fi[:, 0:64], -1.0, ["fi0", "fi1"])
    iota(T.ex[:, 0:128], [[0, 4], [1, 4], [0, 8]], 0, 0, "ex")
    iota(T.fi[:, 1:17], [[0, 4], [1, 4]], 0, 1, "fi0")
    iota(T.fi[:, 33:49], [[1, 4], [1, 4]], 1, 1, "fi1")
    turn(T.own[:, 0:64], T.fi[:, 0:64], ["fi0", "fi1"], ["owa"])
    clear(T.rct[:, 0:504], "rcy")
    fill(T.rct[:, 504:1088], 0.0, ["rcz"])
    ts(T.ex[:, 128:256], T.ex[:, 0:128], LO, None, A.is_equal, None, ["ex", "owa"], ["ex1"])
    ts(T.ex[:, 256:384], T.ex[:, 0:128], HI, None, A.is_equal, None, ["ex", "owa"], ["ex2"])
    tt(T.rct[:, 0:508:4], T.ex[:, 128:255], T.ex[:, 256:383], A.subtract, ["ex1", "ex2", "rcy", "rcz"], ["rc0"])
    clear(T.xt[:, 768:1024], "xz")
    clear(T.bt[:, 0:512], "bz0")
    clear(T.bt[:, 512:1024], "bz1")
    clear(T.m[:, 0:2], "mz")
    for i, (pattern, base, ch) in enumerate([([[0, 4], [-2, 8]], 0, 0), ([[0, 2], [7, 8], [3, 2]], NT // 2, 0),
                                             ([[0, 2], [1, 16]], 0, 0), ([[1, 2], [0, 16]], 0, 0),
                                             ([[16, 2], [0, 16]], 0, 1), ([[16, 2], [112, 16]], 0, 1)], 2):
        iota(T.fi[:, 32 * i:32 * i + 32], pattern, base, ch, "fi%d" % i)
    turn(T.own[:, 64:128], T.fi[:, 64:128], ["fi2", "fi3"], ["owc"])
    turn(T.own[:, 128:256], T.fi[:, 128:256], ["fi%d" % i for i in range(4, 8)], ["owb"])
    iota(T.sb[:, :], [[14, 16]], 1, 0, "sb")
    fill(T.ot[:, 0:516], 1.0, ["one", "oneb", "ot1_0"])
    iota(T.tri0[:, :], [[16, 7], [112, 16]], 0, 0, "tri0")
    clear(T.gt[:, 768:776], "gz")
    ts(pf(17), HIGH, float(CP), 2048.0, A.is_ge, A.mult, ["owb"], ["pf17"])
    ts(pf(18), pf(17), ENT, None, A.add, None, ["pf17", "owb"], ["pf18"])
    ts(T.tri[:, :], T.tri0[:, :], pf(18), BELOW - 1.0, A.is_lt, A.mult, ["tri0", "pf18"], ["tri1"])
    act(T.tri[:, :], T.tri[:, :], F.Copy, ["tri1"], ["tri"], bias=1.0)
    run("G", lambda e: e.affine_select(T.et[:, :], T.ot[:, 0:516], [[-1, 516]], A.is_equal, 0.0, 3, 4),
        ["one", "oneb", "ot1_0"], ["et"])
    iota(T.idr[:, :], [[1, 128]], -CP, 0, "idr")
    iota(T.k4[:, :], [[16, 3], [0, 8], [1, 16]], 0, 0, "k4")
    iota(T.vals[:, :], [[1, CR + 2]], 0, 0, "vals")

    for d in (1, 2, 3):
        n, c = 16 - 4 * d, 16 * d - 12
        act(T.rct[:, 504 + c:504 + c + n], T.rtt[:, 4 * d:16], F.Copy, ["rtt", "rcz"], ["rb%d" % d], scale=-1.0)
        cp(T.rct[:, 576 + c:576 + c + n], T.rtt[:, 0:n], ["rtt", "rcz"], ["rc%d" % d])
    quant("rq", 0, 272, "rct", 0, 1088, ["rc0"] + [n % d for n in ("rb%d", "rc%d") for d in (1, 2, 3)], ["rq"])
    for h, n in ((0, 128), (1, NT - 128)):
        c, d, w = 128 * h, "*d%d" % h, "*w%d" % h
        quant("xq", c, c + 128, "xt", 4 * c, 4 * c + 512, ["xt%d" % h, "xz"], ["xq%d" % h])
        mm(d, "rq", 144, "xq", c, 128, True, False, ["rq", "xq%d" % h])
        mm(d, "rq", 126, "xq", c, 128, False, True, ["rq", "xq%d" % h])
        ts(T.bt[:, 4 * c:4 * (c + n):4], (d, 0, n), 0.0, None, A.is_ge, None, [d, "bz%d" % h], ["bt%d" % h])
        quant("bq", c, c + 128, "bt", 4 * c, 4 * c + 512, ["bt%d" % h], ["bq%d" % h])
        mm(w, "rq", 0, "bq", c, 128, True, True, ["rq", "bq%d" % h])
        ts(T.m[:, 2 + c:2 + c + n], (w, 0, n), 2.5, None, A.is_gt, None, [w], ["m%d" % h])
        act(T.win[:, c:c + n], (w, 0, n), F.Copy, [w], ["win%d" % h])
    scan(T.pref[:, :], T.m[:, 2:2 + NT], T.m[:, 1:1 + NT], ["m0", "m1", "mz", "owc"], ["pref"], M7)

    def piece(i, t):
        return T.le[:, NT * i + 7 * t:NT * i + NT]

    for t in range(NS):
        a = 7 * t // 2
        act(T.le[:, NT * t + a:NT * t + NT // 2], T.pref[:, 2 * a + 1:NT:2], F.Sign, ["pref", "sb"], ["cn%d" % t],
            bias=T.sb[:, t:t + 1], scale=-1.0, accum_out=T.cn[:, t:t + 1])
    for t in range(NS, 16):
        ts(piece(t, t), T.pref[:, 7 * t:NT], 14.0 * t + 1, None, A.is_lt, None, ["pref"], ["le%d" % t])
    for t in range(NS, 16):
        scan(piece(t + 16 - NS, t), piece(t, t), T.nt[:, 0:NT - 7 * t], ["le%d" % t, "nt"], ["ls%d" % t],
             float(7 * t - NT // 2 - 7 * t // 2))
    mine, last = ["cn%d" % t for t in range(NS)], T.le[:, NT * 17 - 1:NT * (32 - NS):NT]
    act(T.cn[:, 16:16 + NS], T.cn[:, 0:NS], F.Copy, mine, ["cnd"])
    for c in (0, 16):
        cp(T.cn[:, c + NS:c + 16], last, ["ls%d" % t for t in range(NS, 16)], ["cnl%d" % c])
    turn(T.cnt[:, :], T.cn[:, :], mine + ["cnd", "cnl0", "cnl16"], ["cnt"])
    ts(T.off[:, :], T.cnt[:, :], BASE, None, A.add, None, ["cnt", "owc"], ["off"])
    quant("gq", 0, 194, "gt", 0, 776, ["gt", "gz"], ["gq"])

    for k in (1, 2, 3, 0):
        d, o = ("sc%d" if k else "lc%d") % k, T.off[:, 8 * (rank ^ k):8 * (rank ^ k) + 7]
        pick(d, CP, CP, "xq", 0, 194, o, ["xq0", "xq1", "off"], d + "x")
        pick(d, 0, CP, "gq", 0, 194, o, ["gq", "off"], d + "g")
    for w in OPT["out"].split():
        to = [int(c) for c in w[1:]]
        if w[0] == "s":
            send([(k, T["lc%ds" % k][:, 0:2 * CP], T["sc%ds" % k][:, 0:2 * CP], share(to)[k]) for k in to], "ax%d",
                 [n % k for k in to for n in ("sc%dxs", "sc%dgs")])
        else:
            send([(k, codes("lc%d" % k, 0, 2 * CP), codes("sc%d" % k, 0, 2 * CP), share(to)[k]) for k in to], "ax%d",
                 [n % k for k in to for n in ("sc%dx", "sc%dg")])
    for k in (1, 2, 3):
        arrive("ax%d" % k, ["lc%d" % k])
    dma("Y", "dv", T.vt[:, :], T.v[:, :], ["lc1"], ["vt"])
    came = {k: ["lc%d" % k] for k in (1, 2, 3)}
    came[0] = ["lc0x", "lc0g", "lc0xs", "lc0gs"]

    for b in range(4):
        quant("eq", 128 * b, 128 * b + 128, "et", 3 - b, 515 - b, ["et"], ["eq%d" % b])
    quant("wq", 0, 256, "wt", 0, 1024, ["wt"], ["wq0", "wq1"])
    quant("wq", 256, 512, "wt", 1024, 2048, ["wt"], ["wq2", "wq3"])
    quant("uq", 0, 256, "ut", 0, 1024, ["ut"], ["uq0", "uq1"])
    quant("uq", 256, 512, "ut", 1024, 2048, ["ut"], ["uq2", "uq3"])
    quant("vq", 0, 128, "vt", 0, 512, ["vt"], ["vq"])
    for t in range(4):
        act(T.ppt[:, t:512:4], T.nt[:, 0:128], F.Identity, ["nt", "prt"], ["ppt%d" % t], bias=T.prt[:, t:t + 1])
    quant("pp", 0, 128, "ppt", 0, 512, ["ppt%d" % t for t in range(4)], ["pp"])
    for t, v in ((0, -256.0), (1, 160.0), (2, -1.0), (3, 0.0)):
        act(T.wnt[:, t:512:4], T.nt[:, 0:128], F.Copy, ["nt"], ["wnt%d" % t], bias=v)
    quant("wn", 0, 128, "wnt", 0, 512, ["wnt%d" % t for t in range(4)], ["wn"])
    clear(T.pt[:, 0:272], "pt0")
    clear(T.pt[:, 272:528], "pt1")
    ts(T.pt[:, 0:11:5], T.nt[:, 0:3], HIGH, None, A.add, None, ["nt", "owb", "pt0"], ["pth"])
    ts(T.pt[:, 16:27:5], T.nt[:, 0:3], P15, None, A.add, None, ["nt", "owb", "pt0"], ["ptl"])
    quant("cq", 0, 132, "pt", 0, 528, ["pt0", "pt1", "pth", "ptl"], ["cq"])
    for k in range(4):
        clear(T.mt[:, 512 * k + 448:512 * k + 512], "mz%d" % k)
        clear(T.dxt[:, 512 * k + 448:512 * k + 512], "dz%d" % k)
        if k:
            clear(T.ot[:, 512 * k + 7:512 * k + 512:4], "ot%d_3" % k)
    fill(T.ot[:, 1027:2051:512], 0.0, ["ot23"])
    fill(pf(12), EPS, ["eps"])

    def stage1(k):
        lc, c = "lc%d" % k, came[k]
        for b in range(4):
            key = "*f%d%d" % (k, b)
            mm(key, "wq", 128 * b, lc, 96, 128, True, True, ["wq%d" % b] + c)
            o = 448 * k + CP * b
            if b >= int(OPT["mv"][k]):
                ts(T.mk[:, o:o + CP], (key, 16, 128), 0.0, None, A.is_gt, None, [key], ["mk%d_%d" % (k, b)])
            else:
                act(T.sm[:, o:o + CP], (key, 16, 128), F.Sign, [key], ["sm%d_%d" % (k, b)])
                act(T.mk[:, o:o + CP], T.sm[:, o:o + CP], F.Relu, ["sm%d_%d" % (k, b)], ["mk%d_%d" % (k, b)])
            key = "*g%d%d" % (k, b)
            mm(key, "eq", 128 * b, lc, 0, 128, True, True, ["eq%d" % b] + c)
            tt(T.mt[:, 512 * k + b:512 * k + 448:4], T.mk[:, o:o + CP], (key, 0, CP), A.mult,
               ["mk%d_%d" % (k, b), key], ["mt%d_%d" % (k, b)])
        quant("qm", 128 * k, 128 * k + 128, "mt", 512 * k, 512 * k + 512,
              ["mz%d" % k] + ["mt%d_%d" % (k, b) for b in range(4)], ["qm%d" % k])

    def stage2(k):
        m, rk = "qm%d" % k, T.rx[:, 448 + CP * k + CP - 1:448 + CP * k + CP]
        kc, kr = "*c%d" % k, "*r%d" % k
        mm(kc, "qm", 128 * k, "pp", 0, 128, True, True, [m, "pp"])
        mm(kr, "pp", 0, "qm", 128 * k, 128, True, True, [m, "pp"])
        act(T.ca[:, 4 * k:4 * k + 1], (kc, 0, 1), F.Abs, [kc, "eps"], ["ca%d" % k], bias=pf(12))
        s, sd = (slice(c + CP * k, c + CP * k + CP) for c in (0, 448))
        act(T.ra[:, s], (kr, 0, CP), F.Abs, [kr, "eps"], ["ra%d" % k], bias=pf(12))
        act(T.ra[:, sd], T.tri[:, :], F.Copy, ["tri", "ca%d" % k], ["rd%d" % k], scale=T.ca[:, 4 * k:4 * k + 1])
        if k:
            tt(T.rx[:, s], T.ra[:, s], T.ra[:, sd], A.is_gt, ["rd%d" % k, "ra%d" % k], ["rx%d" % k])
            scan(T.rx[:, sd], T.rx[:, s], T.nt[:, 0:CP], ["rx%d" % k, "nt"], ["rk%d" % k])
            for t in range(3):
                ts(T.ot[:, 512 * k + t:512 * k + 512:4], T.k4[:, 128 * t:128 * t + 128], rk, None, A.is_equal, None,
                   ["k4", "rk%d" % k], ["ot%d_%d" % (k, t)])
        else:
            tt(T.ot[:, 0:448:4], T.ra[:, s], T.ra[:, sd], A.is_gt, ["rd0", "ra0"], ["ot0_0", "one"])
        quant("qo", 128 * k, 128 * k + 128, "ot", 512 * k, 512 * k + 512,
              ["ot23"] + ["ot%d_%d" % (k, t) for t in range(4 if k else 1)], ["qo%d" % k])
        for b in range(4):
            key = "*u%d%d" % (k, b)
            mm(key, "uq", 128 * b, "qm", 128 * k, 128, True, True, ["uq%d" % b, m])
            act(T.dxt[:, 512 * k + b:512 * k + 448:4], (key, 0, CP), F.Copy, [key], ["dt%d_%d" % (k, b)], scale=0.0625)

    def stage3(k):
        key = "*l%d" % k
        quant("qd", 128 * k, 128 * k + 128, "dxt", 512 * k, 512 * k + 512,
              ["dz%d" % k] + ["dt%d_%d" % (k, b) for b in range(4)], ["qd%d" % k])
        if not k:
            mm(key, "wn", 0, "qo", 0, 128, True, True, ["qo0", "wn"])
            tt(T.tab[:, 0:CP], T.idr[:, 0:CP], (key, 0, CP), A.max, ["idr", key], ["tab0"])
            return
        for c in (0, 1):
            mm(key, "qo", 128 * k, "cq", 4 * c, 128, c == 0, c == 1, ["qo%d" % k, "cq"])
        cp(T.lo[:, 8 * k:8 * k + 3], (key, 0, 3), [key], ["lo%d" % k])
        pick("nq", RUN[k][0], CR, "qd", 128 * k, 128 * k + 128, T.lo[:, 8 * k:8 * k + 3], ["qd%d" % k, "lo%d" % k], "sd%d" % k)

    fill(T.tab[:, 0:384], 0.0, ["tab0", "tab2", "tab3"])
    fill(T.tab[:, 384:512], float(CR), ["tab1"])
    for k in range(4):
        stage1(k)
        stage2(k)
        stage3(k)
    for w in OPT["back"].split():
        to = [int(c) for c in w[1:]]
        es = share(to)
        if w[0] == "l":
            send([(j, T.ll[:, 8 * j:8 * j + 3], T.lo[:, 8 * j:8 * j + 3], es[j]) for j in to], "al%d", ["lo%d" % j for j in to])
            continue
        parts = []
        for k in to:
            c, h, z, y = RUN[k]
            n = len(es[k]) // 2
            parts += [(k, codes("ld%d" % k, h, h + CR), codes("nq", c, c + CR), es[k][0:n]),
                      (k, T["ld%ds" % k][:, y:y + NT], T.nqs[:, z:z + NT], es[k][n:])]
        send(parts, "ar%d", ["nqa", "nqb"] + ["sd%d%s" % (k, x) for k in to for x in ("", "s")])
    for k in (1, 2, 3):
        arrive("al%d" % k, ["ll%d" % k])
        arrive("ar%d" % k, ["ld%d" % k])

    h1, h2, h3, h4, h5, h6, h7, h8, h9 = (T.hh[:, 24 * i:24 * i + 24] for i in range(9))
    turn(T.tv[:, 0:NT], T.win[:, :], ["win0", "win1"], ["tw"])
    turn(T.tv[:, NT:2 * NT], T.pref[:, :], ["pref"], ["tp"])
    tw, tp = T.tv[:, 0:NT:8], T.tv[:, NT + 3:2 * NT:8]
    ts(h1, tw, 2.5, 2.0 * CP + 2, A.is_gt, A.mult, ["tw"], ["h1"])
    ts(h6, tw, 3.5, 1.0, A.is_lt, A.add, ["tw"], ["h6"])
    act(h2, tp, F.Copy, ["tp"], ["h2"], bias=8.0)
    tt(h4, h2, h1, A.is_lt, ["h1", "h2"], ["h4"])
    ts(h7, tp, 0.999 / 14, WHOLE, A.mult, A.add, ["tp"], ["h7"])
    ts(h8, h7, WHOLE, -111.0, A.subtract, A.mult, ["h7"], ["h8"])
    act(h9, tp, F.Copy, ["tp"], ["h9"], scale=8.0, bias=40.0 - CP)
    tt(h3, h8, h9, A.add, ["h8", "h9"], ["h3"])
    tt(h5, h4, h3, A.mult, ["h4", "h3"], ["h5"])
    ts(pf(10), ODD, -1.0, 1.0, A.mult, A.add, ["owb"], ["pf10"])
    for k in (0, 1, 2, 3):
        e = rank ^ k
        for h in (0, 1):
            o, p = slice(12 * k + h, 12 * k + 12, 2), (pf(10), ODD)[h]
            ts(T.offt[:, o], T.hh[:, 96 + e:120:4], float(CP), None, A.add, None, ["h5"], ["offt%d%d" % (k, h)])
            act(T.wgt[:, o], T.hh[:, 120 + e:144:4], F.Copy, ["h6", "owb", "pf10"], ["wgt%d%d" % (k, h)], scale=p)
    fill(T.cs[:, :], 0.0, ["csz"])

    def home(k, first, last):
        tab, zc, q = T.tab[:, 128 * TAB[k]:128 * TAB[k] + 128], "zc%d" % k, 12 * k
        offt, of, ko = T.offt[:, q:q + 12], T.hof[:, q:q + 12], ["offt%d0" % k, "offt%d1" % k]
        s, s1 = slice(192 * k, 192 * k + 192), slice(768 + 192 * k, 960 + 192 * k)
        lst, g1 = T.ll[:, 8 * k:8 * k + 3], T.gg[:, 768 + 192 * k:960 + 192 * k:16]
        if k:
            d = 2 if RUN[k][1] else 0
            cp(tab.indirect(lst), T.vals[:, d:d + CR], ["vals", "ll%d" % k], ["tab%d" % k])
        act(T.gg[:, s], tab.indirect(offt), F.Copy, ["tab%d" % k] + ko, ["gr0%d" % k])
        turn(T.gg[:, s1], T.gg[:, s], ["gr0%d" % k], ["gr1%d" % k])
        if k:
            cp(of, g1, ["gr1%d" % k], ["hof%d" % k])
            pick(zc, 0, NT, "ld%d" % k, RUN[k][1] - d, RUN[k][1] - d + 50, of, ["hof%d" % k, "ld%d" % k, "ldz"], zc)
        else:
            ts(of, g1, 0.0, float(CP), A.min, A.add, ["gr10"], ["hof0"])
            pick(zc, 0, NT, "qd", 0, 128, of, ["hof0", "qd0"], zc)
        for b in range(4):
            mm("*z%d" % b, "eq", 128 * b, zc, 0, NT, first, last, ["eq%d" % b, zc, zc + "s"])

    for i, k in enumerate([int(c) for c in OPT["seq"]]):
        home(k, i == 0, i == 3)
    ts(T.ff[:, 0:12], T.hof[:, 0:12], CP - 0.5, None, A.is_lt, None, ["hof0"], ["fl0"])
    ts(T.ff[:, 12:24], T.hof[:, 12:24], CR - 0.5, None, A.is_lt, None, ["hof1"], ["fl1"])
    ts(T.ff[:, 24:48], T.hof[:, 24:48], 1.0, None, A.is_gt, None, ["hof2", "hof3"], ["fl2"])
    tt(T.ff[:, 48:96], T.ff[:, 0:48], T.wgt[:, :], A.mult,
       ["fl0", "fl1", "fl2"] + ["wgt%d%d" % (k, h) for k in range(4) for h in (0, 1)], ["fw"])
    tt(T.ff[:, 96:120], T.ff[:, 48:72], T.ff[:, 72:96], A.add, ["fw"], ["fs"])
    tt(T.ff[:, 120:132], T.ff[:, 96:108], T.ff[:, 108:120], A.add, ["fs"], ["ft"])
    tt(T.cs[:, 0:6], T.ff[:, 120:132:2], T.ff[:, 121:132:2], A.add, ["ft", "csz"], ["cs"])
    turn(T.cst[0:32, :], T.cs[0:32, :], ["cs", "csz"], ["cst"])

    for b in range(4):
        key = "*z%d" % b
        if b % 2:
            cp(T.zt[:, b:768:4], (key, 0, NT), [key], ["zt%d" % b])
        else:
            act(T.zt[:, b:768:4], (key, 0, NT), F.Copy, [key], ["zt%d" % b])
    quant("zq", 0, 192, "zt", 0, 768, ["zt0", "zt1", "zt2", "zt3"], ["zq"])
    mm("*y", "vq", 0, "zq", 0, NT, True, True, ["vq", "zq"])
    cp(T.ysb[:, :], ("*y", 0, NT), ["*y"], ["ysb"])
    dma("Y", "doy", T.ct[0:1, 0:NT], T.cst[0:6, 0:32], ["cst"], [])
    dma("Y", "doy", T.oc[:, 0:768], T.zq[:, 0:NT].bitcast(dt.uint8), ["zq"], [])
    for i in range(4):
        q, s = ("S", "dos") if i < 3 else ("Y", "doy")
        dma(q, s, T.osc[4 * i:4 * i + 4, 0:NT], T.zqs[32 * i:32 * i + 4, 0:NT], ["zq"], [])
    dma("Y", "doy", T.y[:, :], T.ysb[:, :], ["ysb"], [])

    order = [int(w) for w in ORDER.split()] or range(len(tasks))
    waited, token, users, idle = {}, {}, {}, [(i, []) for i in range(8)]
    for i, t in enumerate(tasks):
        for k in t["use"]:
            users.setdefault(k, []).append(i)
    todo = {k: len(v) for k, v in users.items()}

    def need(q, tok):
        if waited.get((q, tok[0]), 0) < tok[1]:
            queue[q].wait_ge(T.sem[tok[0]], tok[1])
            waited[(q, tok[0])] = tok[1]

    for i in order:
        t = tasks[i]
        if t["q"] is None:
            token[i] = (t["sem"], t["inc"])
            continue
        for k in t["use"]:
            if k not in place:
                place[k], old = idle.pop(0)
                t["before"].update({j: True for j in old})
            todo[k] -= 1
            if not todo[k]:
                idle.append((place[k], [j for j in users[k] if tasks[j]["q"] != "P"]))
        best = {}
        for j, full in t["before"].items():
            if full:
                s, v = token[j]
                best[s] = max(best.get(s, 0), v)
        for s, v in best.items():
            need(t["q"], (s, v))
        made = t["call"](queue[t["q"]])
        if t["sem"]:
            made.then_inc(T.sem[t["sem"]], t["inc"])
            total[t["sem"]] = total.get(t["sem"], 0) + t["inc"]
            token[i] = (t["sem"], total[t["sem"]])
    for s, v in total.items():
        need("G", (s, v))
